import numpy as np
import ml_dtypes


def mxq(x, axis, fmt="e4m3"):
    dtype, down = {"e4m3": (ml_dtypes.float8_e4m3fn, 7), "e5m2": (ml_dtypes.float8_e5m2, 14)}[fmt]
    v = np.moveaxis(np.asarray(x, np.float32).astype(ml_dtypes.bfloat16).astype(np.float64), axis, -1)
    blocks = v.reshape(v.shape[:-1] + (-1, 32))
    amax = np.abs(blocks).max(-1, keepdims=True)
    byte = np.maximum(np.where(amax > 0, np.frexp(amax)[1] - 1 + 127, 0) - down, 1)
    scale = np.exp2(byte - 127.0)
    codes = (blocks / scale).astype(np.float32).astype(dtype).astype(np.float64)
    return np.moveaxis((codes * scale).reshape(v.shape), -1, axis)


WIDE = False


def mx_kscale(k):
    if not WIDE:
        return np.ones(k)
    levels = np.array([10, -10, 5, -5, 0])
    if k % 512:
        return np.exp2(np.random.permutation(np.resize(levels, k // 32))).repeat(32)
    a = np.empty((k // 512, 16))
    for p in range(k // 512):
        a[p, :8] = np.random.permutation(np.resize(levels, 8))
        for g in range(8):
            far = levels[np.abs(levels - a[p, g]) >= 10]
            a[p, g + 8] = far[np.random.randint(len(far))]
    return np.exp2(a.ravel()).repeat(32)


def f64(x):
    return np.asarray(x).astype(np.float64)


def striped(idx):
    return np.tile(idx.reshape(-1, 16).T, (8, 1)).astype(np.uint16)


def unstriped(offs):
    return offs[:16].T.reshape(-1).astype(np.int64)


E2M1 = np.array([0.0, 0.5, 1.0, 1.5, 2.0, 3.0, 4.0, 6.0, -0.0, -0.5, -1.0, -1.5, -2.0, -3.0, -4.0, -6.0])


def pack_weight(w, fmt):
    k, n = w.shape
    w = f64(np.asarray(w, np.float32).astype(ml_dtypes.bfloat16)).reshape(k // 32, 32, n)
    amax = np.abs(w).max(1)
    if fmt == "e4m3":
        byte = np.frexp(amax)[1] - 1 + 127 - 7
    else:
        mant, ex = np.frexp(amax / 6.0)
        byte = np.where(mant > 0.5, ex, ex - 1) + 127
    byte = np.clip(np.where(amax > 0, byte, 1), 1, 254)
    scaled = (w * np.exp2(127.0 - byte)[:, None, :]).reshape(k, n).astype(np.float32)
    by_word = np.ascontiguousarray(scaled.reshape(k // 512, 128, 4, n).transpose(0, 1, 3, 2))
    if fmt == "e4m3":
        words = by_word.astype(ml_dtypes.float8_e4m3fn).view(np.uint8)
    else:
        c = by_word.astype(ml_dtypes.float4_e2m1fn).view(np.uint8) & 0xF
        words = (c[..., 0::2] | (c[..., 1::2] << 4)).reshape(k // 512, 128, 2 * n)
    return np.ascontiguousarray(words), np.ascontiguousarray(byte.astype(np.uint8).reshape(k // 512, 16, n))


def unpack_weight(words, scales, fmt):
    g, _, n = scales.shape
    words = np.ascontiguousarray(words).reshape(g, 128, n, -1)
    if fmt == "e4m3":
        vals = words.view(ml_dtypes.float8_e4m3fn).astype(np.float64)
    else:
        nib = np.empty((g, 128, n, 4), np.uint8)
        nib[..., 0::2] = words & 0xF
        nib[..., 1::2] = words >> 4
        vals = E2M1[nib]
    vals = vals * np.repeat(np.exp2(scales.astype(np.float64) - 127.0), 8, axis=1)[..., None]
    return vals.transpose(0, 1, 3, 2).reshape(g * 512, n)


def relu2(v):
    return np.maximum(v, 0.0) ** 2


K, T, E, C, N = 2560, 768, 12, 128, 128


def by_expert(wq, xq):
    return np.concatenate([wq[e].T @ xq[:, e * C:(e + 1) * C] for e in range(E)], axis=1)


def setup_inputs():
    n = np.random.standard_normal
    s = mx_kscale(K)[:, None]
    first = np.random.permutation(np.repeat(np.arange(E), T // E))
    second = (first + 1 + np.random.permutation(np.repeat(np.arange(E - 1), -(-T // (E - 1)))[:T])) % E
    while np.bincount(second, minlength=E).max() != T // E:
        load = np.bincount(second, minlength=E); hi, lo = int(load.argmax()), int(load.argmin())
        t = np.flatnonzero((second == hi) & (first != lo))[0]; second[t] = lo
    slot_token = np.empty(E * C, np.int64); pos = np.empty((2, T), np.int64); fill = np.zeros(E, np.int64)
    place = np.stack([np.random.permutation(C) for _ in range(E)])
    for r, deal in enumerate((first, second)):
        for t in np.random.permutation(T):
            e = deal[t]; j = e * C + place[e, fill[e]]; fill[e] += 1; slot_token[j] = t; pos[r, t] = j
    g = np.random.uniform(0.2, 0.8, T)
    w = [pack_weight(m, "e2m1") for m in n((E + 1, K, N)) / np.sqrt(K) / s[None]]
    return {
        "xT": (n((K, T)) * s).astype(np.float32),
        "w_words": np.stack([m[0] for m in w]),
        "w_scales": np.stack([m[1] for m in w]),
        "b": (0.3 * n((N, E + 1))).astype(np.float32),
        "gate": np.stack([np.tile(g, (N, 1)), np.tile(1.0 - g, (N, 1))]).astype(np.float32),
        "offs": striped(slot_token),
        "pos1": striped(pos[0]),
        "pos2": striped(pos[1]),
    }


def reference(xT, w_words, w_scales, b, gate, offs, pos1, pos2):
    idx = unstriped(offs)
    w = np.stack([unpack_weight(w_words[e], w_scales[e], "e2m1") for e in range(E + 1)])
    wq = w
    xs = mxq(f64(xT), 0, "e4m3")
    ys = relu2((wq[E].T @ xs) + f64(b)[:, E:])
    xq = mxq(f64(xT)[:, idx], 0, "e4m3")
    y = by_expert(w, xq)
    y = relu2(y + np.repeat(f64(b)[:, :E], C, axis=1))
    return ys + f64(gate[0]) * y[:, unstriped(pos1)] + f64(gate[1]) * y[:, unstriped(pos2)]

@@ -1,0 +1,246 @@
+from contextlib import ExitStack
+
+import concourse.mybir as mybir
+
+K, T, E, C, N = 2560, 768, 12, 128, 128
+S = E * C
+P = 128
+PASSES = K // 512
+VINTER = {(4, 1280)}
+FLOPS = 2 * K * N * (S + T)
+
+F32 = mybir.dt.float32
+BF16 = mybir.dt.bfloat16
+U32 = mybir.dt.uint32
+I32 = mybir.dt.int32
+U16 = mybir.dt.uint16
+U8 = mybir.dt.uint8
+FP8 = mybir.dt.float8_e4m3fn_x4
+FP4 = mybir.dt.float4_e2m1fn_x4
+ADD, MULT, MAX = mybir.AluOpType.add, mybir.AluOpType.mult, mybir.AluOpType.max
+COPY = mybir.ActivationFunctionType.Copy
+RELU = mybir.ActivationFunctionType.Relu
+SQUARE = mybir.ActivationFunctionType.Square
+
+
+def tile_moe_shr_lin_relu2_kernel(tc, xT, w_words, w_scales, b, gate, offs, pos1, pos2, out):
+    nc = tc.nc
+    with ExitStack() as ctx:
+        keep = ctx.enter_context(tc.tile_pool(name="keep", bufs=1))
+        xpool = ctx.enter_context(tc.tile_pool(name="xpool", bufs=8))
+        winp = ctx.enter_context(tc.tile_pool(name="winp", bufs=4))
+        gp = ctx.enter_context(tc.tile_pool(name="gp", bufs=4))
+        gsp = ctx.enter_context(tc.tile_pool(name="gsp", bufs=2))
+        gip = ctx.enter_context(tc.tile_pool(name="gip", bufs=4))
+        shp = ctx.enter_context(tc.tile_pool(name="shp", bufs=2))
+        psum = ctx.enter_context(tc.psum_pool(name="psum", bufs=1))
+
+        offs_t = keep.tile([P, S // 16], U16, name="offs_t")
+        pos1_t = keep.tile([P, T // 16], U16, name="pos1_t")
+        pos2_t = keep.tile([P, T // 16], U16, name="pos2_t")
+        bias = keep.tile([P, E + 1], F32, name="bias")
+        gate_t = keep.tile([P, 2, T], F32, name="gate_t")
+        wt = keep.tile([P, (E + 1) * PASSES, 2 * N], U8, name="wt", align_bytes=64)
+        wsc = keep.tile([P, (E + 1) * PASSES, N], U8, name="wsc", align_bytes=64)
+        planes = keep.tile([P, 2, T], BF16, name="planes")
+        codes = [keep.tile([P, S], U32, name="codes%d" % a, align_bytes=64) for a in range(PASSES)]
+        cscale = [keep.tile([P, S], U8, name="cscale%d" % a, align_bytes=64) for a in range(PASSES)]
+        scodes = [keep.tile([P, T], U32, name="scodes%d" % a, align_bytes=64) for a in range(PASSES)]
+        sscale = [keep.tile([P, T], U8, name="sscale%d" % a, align_bytes=64) for a in range(PASSES)]
+        y = keep.tile([P, S], F32, name="y")
+        ys = keep.tile([P, T], F32, name="ys")
+        g1 = keep.tile([P, T], F32, name="g1")
+        g2 = keep.tile([P, T], F32, name="g2")
+        ot = keep.tile([P, T], F32, name="ot")
+
+        ps_sa = psum.tile([P, 512], F32, name="ps_sa")
+        ps_sb = psum.tile([P, 512], F32, name="ps_sb")
+        ps_q = [psum.tile([P, 512], F32, name="ps_q%d" % i) for i in range(2)]
+        ps_l = [psum.tile([P, 128], F32, name="ps_l%d" % i) for i in range(4)]
+
+        nc.gpsimd.memset(wsc[:].rearrange("p a n -> p (a n)").bitcast(I32), 0)
+
+        xv = xT.rearrange("(a p j) t -> a p j t", a=PASSES, j=4)
+        xr = {}
+        H = T // 2
+
+        def load_x(a, u):
+            t = xpool.tile([P, 2, T], F32, name="xr")
+            if a == 0 and u == 0:
+                nc.sync.dma_start(out=t[:, :, :H], in_=xv[a][:, 2 * u:2 * u + 2, :H])
+                nc.sync.dma_start(out=t[:, :, H:], in_=xv[a][:, 2 * u:2 * u + 2, H:])
+            else:
+                nc.sync.dma_start(out=t[:], in_=xv[a][:, 2 * u:2 * u + 2, :])
+            xr[a, u] = t
+
+        def late_loads():
+            load_x(4, 0)
+            load_x(4, 1)
+            nc.sync.dma_start(out=bias[:], in_=b)
+            wsv = w_scales.bitcast(I32).rearrange("e a q n -> q (e a) n")
+            for q in range(4):
+                nc.sync.dma_start(out=wsc[32 * q:32 * q + 4].rearrange("p a n -> p (a n)").bitcast(I32).rearrange("p (a n) -> p a n", n=N // 4),
+                                  in_=wsv[4 * q:4 * q + 4])
+            wv = w_words.bitcast(I32).rearrange("e a p n -> p (e a) n")
+            wd = wt[:].rearrange("p a n -> p (a n)").bitcast(I32).rearrange("p (a n) -> p a n", n=N // 2)
+            for lo, hi in ((40, 65), (0, 20), (20, 40)):
+                nc.sync.dma_start(out=wd[:, lo:hi, :], in_=wv[:, lo:hi, :])
+            nc.sync.dma_start(out=gate_t[:], in_=gate.rearrange("g p t -> p g t"))
+            nc.sync.dma_start(pos1_t[:], pos1)
+            nc.sync.dma_start(pos2_t[:], pos2)
+
+        win, gt, goff, gi, sh = {}, {}, {}, {}, {}
+
+        def cast(a, u):
+            if a not in win:
+                win[a] = winp.tile([P, 2, 2 * T], BF16, name="win", align_bytes=64)
+            d = win[a][:, u, :].rearrange("p (t j) -> p t j", j=2)
+            s = xr[a, u][:].rearrange("p j t -> p t j")
+            if a == 0 and u == 0:
+                nc.vector.tensor_copy(out=d[:, :H, :], in_=s[:, :H, :])
+                nc.vector.tensor_copy(out=d[:, H:H + 256, :], in_=s[:, H:H + 256, :])
+                nc.scalar.copy(out=d[:, H + 256:, :], in_=s[:, H + 256:, :])
+            else:
+                nc.scalar.copy(out=d, in_=s)
+
+        def s_cast():
+            nc.scalar.copy(out=planes[:], in_=xr[4, 1][:])
+
+        def s_gather(lo):
+            g = gsp.tile([P, 2, 256], U32, name="gs")
+            gt[4, lo] = g
+            v = g[:, 1, :].bitcast(BF16).rearrange("p (s j) -> p s j", j=2)
+            for s0 in range(0, 256, C):
+                for j in range(2):
+                    nc.scalar.activation(v[:, s0:s0 + C, j], planes[:, j, :].indirect(offs_t[:, (lo + s0) // 16:(lo + s0 + C) // 16]), COPY)
+
+        def gather(a, lo, n):
+            us = (0,) if (a, lo) in gt else (0, 1)
+            if (a, lo) not in gt:
+                gt[a, lo] = gp.tile([P, 2, 512], U32, name="g")
+            for u in us:
+                nc.vector.tensor_copy(gt[a, lo][:, u, :n], win[a][:, u, :].bitcast(U32).indirect(offs_t[:, lo // 16:(lo + n) // 16]))
+
+        def inter(a, lo, n):
+            t = gip.tile([P, 2 * 1024], BF16, name="gi", align_bytes=64)
+            gi[a, lo] = t
+            if (a, lo) in VINTER:
+                nc.vector.tensor_copy(out=t[:].bitcast(I32)[:, :2 * n].rearrange("p (s u) -> p s u", u=2),
+                                      in_=gt[a, lo][:, :, :n].bitcast(I32).rearrange("p u s -> p s u"))
+            else:
+                nc.scalar.copy(out=t[:].bitcast(U32)[:, :2 * n].rearrange("p (s u) -> p s u", u=2),
+                               in_=gt[a, lo][:, :, :n].rearrange("p u s -> p s u"))
+
+        def quant(a, lo, n):
+            nc.vector.quantize_mx(out=codes[a][:, lo:lo + n].bitcast(FP8), scales=cscale[a][:, lo:lo + n], in_=gi[a, lo][:, :4 * n])
+
+        def sh_inter(a):
+            t = shp.tile([P, 4 * T], BF16, name="sh", align_bytes=64)
+            nc.scalar.copy(out=t[:].bitcast(U32).rearrange("p (s u) -> p s u", u=2),
+                           in_=win[a][:].rearrange("p u t -> p (u t)").bitcast(U32).rearrange("p (u s) -> p s u", u=2))
+            sh[a] = t
+
+        def sh_quant(a):
+            for lo, n in ((0, 512), (512, 256)):
+                nc.vector.quantize_mx(out=scodes[a][:, lo:lo + n].bitcast(FP8), scales=sscale[a][:, lo:lo + n],
+                                      in_=sh[a][:, 4 * lo:4 * (lo + n)])
+
+        def mm(dst, e, a, cd, cs, cols):
+            nc.tensor.matmul_mx(out=dst, lhsT=wt[:, e * PASSES + a, :].bitcast(FP4), lhsT_scale=wsc[:, e * PASSES + a, :],
+                                rhs=cd[a][:, cols].bitcast(FP8), rhs_scale=cs[a][:, cols], start=a == 0, stop=a == PASSES - 1)
+
+        def shared_mm(a):
+            mm(ps_sa[:], E, a, scodes, sscale, slice(0, 512))
+            mm(ps_sb[:], E, a, scodes, sscale, slice(256, 768))
+
+        def quad_mm(i):
+            for e in range(4 * i, 4 * i + 4):
+                for a in range(PASSES):
+                    mm(ps_q[i][:, (e % 4) * C:(e % 4 + 1) * C], e, a, codes, cscale, slice(e * C, (e + 1) * C))
+
+        def quad_out(i):
+            for e in range(4 * i, 4 * i + 4):
+                nc.scalar.activation(out=y[:, e * C:(e + 1) * C], in_=ps_q[i][:, (e % 4) * C:(e % 4 + 1) * C], func=RELU, bias=bias[:, e:e + 1])
+            nc.scalar.activation(out=y[:, 512 * i:512 * i + 512], in_=y[:, 512 * i:512 * i + 512], func=SQUARE)
+
+        def last_mm(es, passes):
+            for a in passes:
+                for e in es:
+                    mm(ps_l[e - 8][:], e, a, codes, cscale, slice(e * C, (e + 1) * C))
+
+        def last_out(e0, vector):
+            sq = slice(e0 * C, (e0 + 2) * C)
+            for e in (e0, e0 + 1):
+                cols = slice(e * C, (e + 1) * C)
+                if vector:
+                    nc.vector.tensor_scalar(out=y[:, cols], in0=ps_l[e - 8][:], scalar1=bias[:, e:e + 1], scalar2=0.0, op0=ADD, op1=MAX)
+                else:
+                    nc.scalar.activation(out=y[:, cols], in_=ps_l[e - 8][:], func=RELU, bias=bias[:, e:e + 1])
+            if vector:
+                nc.vector.tensor_tensor(y[:, sq], y[:, sq], y[:, sq], MULT)
+            else:
+                nc.scalar.activation(out=y[:, sq], in_=y[:, sq], func=SQUARE)
+
+        pend = []
+
+        def flush(depth):
+            while len(pend) > depth:
+                pend.pop(0)()
+
+        def shared(a):
+            sh_inter(a)
+            pend.append(lambda: sh_quant(a))
+
+        nc.sync.dma_start(offs_t[:], offs)
+        for a in range(4):
+            load_x(a, 0)
+            load_x(a, 1)
+        cast(0, 0)
+        cast(0, 1)
+        late_loads()
+
+        L = PASSES - 1
+        steps = [(a, lo, 512) for a in range(3) for lo in (0, 512, 1024)]
+        for lo, n in ((0, 512), (512, 512), (1024, 256), (1280, 256)):
+            steps += [(3, lo, n), (4, lo, n)]
+        hooks = {
+            (0, 0): lambda: (cast(1, 0), cast(1, 1)),
+            (0, 512): lambda: cast(2, 0),
+            (0, 1024): lambda: shared(0),
+            (1, 0): lambda: (last_mm(range(8, 12), [0]), shared(1), s_cast()),
+            (1, 512): lambda: (shared_mm(0), shared_mm(1), s_gather(1024)),
+            (1, 1024): lambda: (cast(2, 1), cast(3, 0)),
+            (2, 0): lambda: (last_mm(range(8, 12), [1]), cast(4, 1)),
+            (2, 512): lambda: cast(4, 0),
+            (2, 1024): lambda: (cast(3, 1), shared(2)),
+            (3, 0): lambda: (last_mm(range(8, 12), [2]), shared_mm(2)),
+            (3, 512): lambda: (quad_mm(0), shared(3), s_gather(1280)),
+            (4, 512): lambda: (shared_mm(3), shared(4), quad_out(0)),
+            (3, 1024): lambda: (quad_mm(1), shared_mm(4)),
+            (4, 1024): lambda: (quad_out(1), last_mm((8, 9), [3])),
+            (3, 1280): lambda: last_mm((8, 9), [4]),
+            (4, 1280): lambda: (last_out(8, False), last_mm((10, 11), [3])),
+        }
+        for a, lo, n in steps:
+            gather(a, lo, n)
+            inter(a, lo, n)
+            pend.append(lambda a=a, lo=lo, n=n: quant(a, lo, n))
+            flush(1)
+            if (a, lo) in hooks:
+                hooks[a, lo]()
+        flush(0)
+        last_mm((10, 11), [4])
+        last_out(10, True)
+
+        nc.vector.tensor_scalar(out=ys[:, 512:], in0=ps_sb[:, 256:], scalar1=bias[:, E:E + 1], scalar2=0.0, op0=ADD, op1=MAX)
+        nc.vector.tensor_tensor(ys[:, 512:], ys[:, 512:], ys[:, 512:], MULT)
+        nc.scalar.activation(out=ys[:, :512], in_=ps_sa[:], func=RELU, bias=bias[:, E:E + 1])
+        nc.scalar.activation(out=ys[:, :512], in_=ys[:, :512], func=SQUARE)
+
+        nc.vector.tensor_tensor(g1[:], y[:].indirect(pos1_t[:]), gate_t[:, 0, :], MULT)
+        nc.vector.tensor_tensor(g1[:], g1[:], ys[:], ADD)
+        for lo, n in ((0, 512), (512, 256)):
+            c = slice(lo, lo + n)
+            nc.vector.tensor_tensor(g2[:, c], y[:].indirect(pos2_t[:, lo // 16:(lo + n) // 16]), gate_t[:, 1, c], MULT)
+            nc.vector.tensor_tensor(ot[:, c], g1[:, c], g2[:, c], ADD)
+            nc.sync.dma_start(out=out[:, c], in_=ot[:, c])

@@ -6,7 +6,9 @@ K, T, E, C, N = 2560, 768, 12, 128, 128
 S = E * C
 P = 128
 PASSES = K // 512
-VINTER = {(4, 1280)}
+RING = 3
+HELD = 2
+GROUPS = ((0, 512), (512, 512), (1024, 256), (1280, 256))
 FLOPS = 2 * K * N * (S + T)
 
 F32 = mybir.dt.float32
@@ -17,8 +19,7 @@ U16 = mybir.dt.uint16
 U8 = mybir.dt.uint8
 FP8 = mybir.dt.float8_e4m3fn_x4
 FP4 = mybir.dt.float4_e2m1fn_x4
-ADD, MULT, MAX = mybir.AluOpType.add, mybir.AluOpType.mult, mybir.AluOpType.max
-COPY = mybir.ActivationFunctionType.Copy
+ADD, MULT = mybir.AluOpType.add, mybir.AluOpType.mult
 RELU = mybir.ActivationFunctionType.Relu
 SQUARE = mybir.ActivationFunctionType.Square
 
@@ -28,11 +29,9 @@ def tile_moe_shr_lin_relu2_kernel(tc, xT, w_words, w_scales, b, gate, offs, pos1
     with ExitStack() as ctx:
         keep = ctx.enter_context(tc.tile_pool(name="keep", bufs=1))
         xpool = ctx.enter_context(tc.tile_pool(name="xpool", bufs=8))
-        winp = ctx.enter_context(tc.tile_pool(name="winp", bufs=4))
-        gp = ctx.enter_context(tc.tile_pool(name="gp", bufs=4))
-        gsp = ctx.enter_context(tc.tile_pool(name="gsp", bufs=2))
+        gp = ctx.enter_context(tc.tile_pool(name="gp", bufs=1))
         gip = ctx.enter_context(tc.tile_pool(name="gip", bufs=4))
-        shp = ctx.enter_context(tc.tile_pool(name="shp", bufs=2))
+        shp = ctx.enter_context(tc.tile_pool(name="shp", bufs=3))
         psum = ctx.enter_context(tc.psum_pool(name="psum", bufs=1))
 
         offs_t = keep.tile([P, S // 16], U16, name="offs_t")
@@ -42,10 +41,9 @@ def tile_moe_shr_lin_relu2_kernel(tc, xT, w_words, w_scales, b, gate, offs, pos1
         gate_t = keep.tile([P, 2, T], F32, name="gate_t")
         wt = keep.tile([P, (E + 1) * PASSES, 2 * N], U8, name="wt", align_bytes=64)
         wsc = keep.tile([P, (E + 1) * PASSES, N], U8, name="wsc", align_bytes=64)
-        planes = keep.tile([P, 2, T], BF16, name="planes")
+        win = [keep.tile([P, 2, 2 * T], BF16, name="win%d" % a, align_bytes=64) for a in range(PASSES)]
         codes = [keep.tile([P, S], U32, name="codes%d" % a, align_bytes=64) for a in range(PASSES)]
         cscale = [keep.tile([P, S], U8, name="cscale%d" % a, align_bytes=64) for a in range(PASSES)]
-        scodes = [keep.tile([P, T], U32, name="scodes%d" % a, align_bytes=64) for a in range(PASSES)]
         sscale = [keep.tile([P, T], U8, name="sscale%d" % a, align_bytes=64) for a in range(PASSES)]
         y = keep.tile([P, S], F32, name="y")
         ys = keep.tile([P, T], F32, name="ys")
@@ -55,8 +53,7 @@ def tile_moe_shr_lin_relu2_kernel(tc, xT, w_words, w_scales, b, gate, offs, pos1
 
         ps_sa = psum.tile([P, 512], F32, name="ps_sa")
         ps_sb = psum.tile([P, 512], F32, name="ps_sb")
-        ps_q = [psum.tile([P, 512], F32, name="ps_q%d" % i) for i in range(2)]
-        ps_l = [psum.tile([P, 128], F32, name="ps_l%d" % i) for i in range(4)]
+        ps = {lo: psum.tile([P, 512], F32, name="ps%d" % lo) for lo, n in GROUPS}
 
         nc.gpsimd.memset(wsc[:].rearrange("p a n -> p (a n)").bitcast(I32), 0)
 
@@ -83,17 +80,15 @@ def tile_moe_shr_lin_relu2_kernel(tc, xT, w_words, w_scales, b, gate, offs, pos1
                                   in_=wsv[4 * q:4 * q + 4])
             wv = w_words.bitcast(I32).rearrange("e a p n -> p (e a) n")
             wd = wt[:].rearrange("p a n -> p (a n)").bitcast(I32).rearrange("p (a n) -> p a n", n=N // 2)
-            for lo, hi in ((40, 65), (0, 20), (20, 40)):
+            for lo, hi in ((0, 20), (20, 40), (40, 65)):
                 nc.sync.dma_start(out=wd[:, lo:hi, :], in_=wv[:, lo:hi, :])
             nc.sync.dma_start(out=gate_t[:], in_=gate.rearrange("g p t -> p g t"))
             nc.sync.dma_start(pos1_t[:], pos1)
             nc.sync.dma_start(pos2_t[:], pos2)
 
-        win, gt, goff, gi, sh = {}, {}, {}, {}, {}
+        gi, sh, scodes = {}, {}, {}
 
         def cast(a, u):
-            if a not in win:
-                win[a] = winp.tile([P, 2, 2 * T], BF16, name="win", align_bytes=64)
             d = win[a][:, u, :].rearrange("p (t j) -> p t j", j=2)
             s = xr[a, u][:].rearrange("p j t -> p t j")
             if a == 0 and u == 0:
@@ -103,33 +98,17 @@ def tile_moe_shr_lin_relu2_kernel(tc, xT, w_words, w_scales, b, gate, offs, pos1
             else:
                 nc.scalar.copy(out=d, in_=s)
 
-        def s_cast():
-            nc.scalar.copy(out=planes[:], in_=xr[4, 1][:])
+        def gather(i, a, lo, n):
+            g = gp.tile([P, 2, 512], U32, name="g", tag="ring%d" % slot[i], align_bytes=64)
+            for u in range(2):
+                nc.vector.tensor_copy(g[:, u, :n], win[a][:, u, :].bitcast(U32).indirect(offs_t[:, lo // 16:(lo + n) // 16]))
+            return g
 
-        def s_gather(lo):
-            g = gsp.tile([P, 2, 256], U32, name="gs")
-            gt[4, lo] = g
-            v = g[:, 1, :].bitcast(BF16).rearrange("p (s j) -> p s j", j=2)
-            for s0 in range(0, 256, C):
-                for j in range(2):
-                    nc.scalar.activation(v[:, s0:s0 + C, j], planes[:, j, :].indirect(offs_t[:, (lo + s0) // 16:(lo + s0 + C) // 16]), COPY)
-
-        def gather(a, lo, n):
-            us = (0,) if (a, lo) in gt else (0, 1)
-            if (a, lo) not in gt:
-                gt[a, lo] = gp.tile([P, 2, 512], U32, name="g")
-            for u in us:
-                nc.vector.tensor_copy(gt[a, lo][:, u, :n], win[a][:, u, :].bitcast(U32).indirect(offs_t[:, lo // 16:(lo + n) // 16]))
-
-        def inter(a, lo, n):
+        def inter(g, a, lo, n):
             t = gip.tile([P, 2 * 1024], BF16, name="gi", align_bytes=64)
             gi[a, lo] = t
-            if (a, lo) in VINTER:
-                nc.vector.tensor_copy(out=t[:].bitcast(I32)[:, :2 * n].rearrange("p (s u) -> p s u", u=2),
-                                      in_=gt[a, lo][:, :, :n].bitcast(I32).rearrange("p u s -> p s u"))
-            else:
-                nc.scalar.copy(out=t[:].bitcast(U32)[:, :2 * n].rearrange("p (s u) -> p s u", u=2),
-                               in_=gt[a, lo][:, :, :n].rearrange("p u s -> p s u"))
+            nc.scalar.copy(out=t[:].bitcast(U32)[:, :2 * n].rearrange("p (s u) -> p s u", u=2),
+                           in_=g[:, :, :n].rearrange("p u s -> p s u"))
 
         def quant(a, lo, n):
             nc.vector.quantize_mx(out=codes[a][:, lo:lo + n].bitcast(FP8), scales=cscale[a][:, lo:lo + n], in_=gi[a, lo][:, :4 * n])
@@ -140,56 +119,42 @@ def tile_moe_shr_lin_relu2_kernel(tc, xT, w_words, w_scales, b, gate, offs, pos1
                            in_=win[a][:].rearrange("p u t -> p (u t)").bitcast(U32).rearrange("p (u s) -> p s u", u=2))
             sh[a] = t
 
-        def sh_quant(a):
+        def sh_quant(a, dst):
+            scodes[a] = dst
             for lo, n in ((0, 512), (512, 256)):
-                nc.vector.quantize_mx(out=scodes[a][:, lo:lo + n].bitcast(FP8), scales=sscale[a][:, lo:lo + n],
+                nc.vector.quantize_mx(out=dst[:, lo:lo + n].bitcast(FP8), scales=sscale[a][:, lo:lo + n],
                                       in_=sh[a][:, 4 * lo:4 * (lo + n)])
 
-        def mm(dst, e, a, cd, cs, cols):
+        def mm(dst, e, a, cd, cs, cols, start, stop):
             nc.tensor.matmul_mx(out=dst, lhsT=wt[:, e * PASSES + a, :].bitcast(FP4), lhsT_scale=wsc[:, e * PASSES + a, :],
-                                rhs=cd[a][:, cols].bitcast(FP8), rhs_scale=cs[a][:, cols], start=a == 0, stop=a == PASSES - 1)
+                                rhs=cd[a][:, cols].bitcast(FP8), rhs_scale=cs[a][:, cols], start=start, stop=stop)
 
         def shared_mm(a):
-            mm(ps_sa[:], E, a, scodes, sscale, slice(0, 512))
-            mm(ps_sb[:], E, a, scodes, sscale, slice(256, 768))
+            mm(ps_sa[:], E, a, scodes, sscale, slice(0, 512), a == 0, a == PASSES - 1)
+            mm(ps_sb[:], E, a, scodes, sscale, slice(256, 768), a == 0, a == PASSES - 1)
 
-        def quad_mm(i):
-            for e in range(4 * i, 4 * i + 4):
-                for a in range(PASSES):
-                    mm(ps_q[i][:, (e % 4) * C:(e % 4 + 1) * C], e, a, codes, cscale, slice(e * C, (e + 1) * C))
+        def routed_mm(a, lo, n):
+            for glo, gn in GROUPS:
+                if lo <= glo < lo + n:
+                    for c0 in range(0, gn, C):
+                        mm(ps[glo][:, c0:c0 + C], (glo + c0) // C, a, codes, cscale, slice(glo + c0, glo + c0 + C),
+                           a == 0 and c0 == 0, a == PASSES - 1 and c0 + C == gn)
 
-        def quad_out(i):
-            for e in range(4 * i, 4 * i + 4):
-                nc.scalar.activation(out=y[:, e * C:(e + 1) * C], in_=ps_q[i][:, (e % 4) * C:(e % 4 + 1) * C], func=RELU, bias=bias[:, e:e + 1])
-            nc.scalar.activation(out=y[:, 512 * i:512 * i + 512], in_=y[:, 512 * i:512 * i + 512], func=SQUARE)
+        def routed_out(lo, n):
+            for c0 in range(0, n, C):
+                e = (lo + c0) // C
+                nc.scalar.activation(out=y[:, lo + c0:lo + c0 + C], in_=ps[lo][:, c0:c0 + C], func=RELU, bias=bias[:, e:e + 1])
+            nc.scalar.activation(out=y[:, lo:lo + n], in_=y[:, lo:lo + n], func=SQUARE)
 
-        def last_mm(es, passes):
-            for a in passes:
-                for e in es:
-                    mm(ps_l[e - 8][:], e, a, codes, cscale, slice(e * C, (e + 1) * C))
-
-        def last_out(e0, vector):
-            sq = slice(e0 * C, (e0 + 2) * C)
-            for e in (e0, e0 + 1):
-                cols = slice(e * C, (e + 1) * C)
-                if vector:
-                    nc.vector.tensor_scalar(out=y[:, cols], in0=ps_l[e - 8][:], scalar1=bias[:, e:e + 1], scalar2=0.0, op0=ADD, op1=MAX)
-                else:
-                    nc.scalar.activation(out=y[:, cols], in_=ps_l[e - 8][:], func=RELU, bias=bias[:, e:e + 1])
-            if vector:
-                nc.vector.tensor_tensor(y[:, sq], y[:, sq], y[:, sq], MULT)
-            else:
-                nc.scalar.activation(out=y[:, sq], in_=y[:, sq], func=SQUARE)
-
-        pend = []
-
-        def flush(depth):
-            while len(pend) > depth:
-                pend.pop(0)()
-
-        def shared(a):
+        def early_shared(a):
             sh_inter(a)
-            pend.append(lambda: sh_quant(a))
+            t = keep.tile([P, T], U32, name="scodes%d" % a, align_bytes=64)
+            sh_quant(a, t)
+            shared_mm(a)
+
+        def finish(a, lo, n):
+            quant(a, lo, n)
+            routed_mm(a, lo, n)
 
         nc.sync.dma_start(offs_t[:], offs)
         for a in range(4):
@@ -199,48 +164,47 @@ def tile_moe_shr_lin_relu2_kernel(tc, xT, w_words, w_scales, b, gate, offs, pos1
         cast(0, 1)
         late_loads()
 
-        L = PASSES - 1
-        steps = [(a, lo, 512) for a in range(3) for lo in (0, 512, 1024)]
-        for lo, n in ((0, 512), (512, 512), (1024, 256), (1280, 256)):
-            steps += [(3, lo, n), (4, lo, n)]
-        hooks = {
-            (0, 0): lambda: (cast(1, 0), cast(1, 1)),
-            (0, 512): lambda: cast(2, 0),
-            (0, 1024): lambda: shared(0),
-            (1, 0): lambda: (last_mm(range(8, 12), [0]), shared(1), s_cast()),
-            (1, 512): lambda: (shared_mm(0), shared_mm(1), s_gather(1024)),
-            (1, 1024): lambda: (cast(2, 1), cast(3, 0)),
-            (2, 0): lambda: (last_mm(range(8, 12), [1]), cast(4, 1)),
-            (2, 512): lambda: cast(4, 0),
-            (2, 1024): lambda: (cast(3, 1), shared(2)),
-            (3, 0): lambda: (last_mm(range(8, 12), [2]), shared_mm(2)),
-            (3, 512): lambda: (quad_mm(0), shared(3), s_gather(1280)),
-            (4, 512): lambda: (shared_mm(3), shared(4), quad_out(0)),
-            (3, 1024): lambda: (quad_mm(1), shared_mm(4)),
-            (4, 1024): lambda: (quad_out(1), last_mm((8, 9), [3])),
-            (3, 1280): lambda: last_mm((8, 9), [4]),
-            (4, 1280): lambda: (last_out(8, False), last_mm((10, 11), [3])),
-        }
-        for a, lo, n in steps:
-            gather(a, lo, n)
-            inter(a, lo, n)
-            pend.append(lambda a=a, lo=lo, n=n: quant(a, lo, n))
-            flush(1)
-            if (a, lo) in hooks:
-                hooks[a, lo]()
-        flush(0)
-        last_mm((10, 11), [4])
-        last_out(10, True)
+        steps = [(a, lo, 512) for a in range(PASSES - 1) for lo in (0, 512, 1024)] + [(PASSES - 1, lo, n) for lo, n in GROUPS]
+        jobs = []
+        for a in range(PASSES - 1):
+            jobs += [lambda a=a: cast(a + 1, 0), lambda a=a: cast(a + 1, 1),
+                     lambda a=a: early_shared(a) if a < HELD else sh_inter(a)]
+        jobs += [lambda: sh_inter(PASSES - 1)]
+        last = len(steps) - 1
+        slot = [i % RING for i in range(last - 2)]
+        while len(slot) <= last:
+            slot.append(slot[-2])
+        for i, (a, lo, n) in enumerate(steps):
+            g = gather(i, a, lo, n)
+            if jobs:
+                jobs.pop(0)()
+            inter(g, a, lo, n)
+            if i > 0:
+                finish(*steps[i - 1])
+            if i == last - 2:
+                routed_out(*GROUPS[0])
+        held = gp.tile([P, T], U32, name="held", tag="ring%d" % slot[last - 1], align_bytes=64)
+        sh_quant(HELD, held)
+        finish(*steps[last])
+        for lo, n in GROUPS[1:]:
+            routed_out(lo, n)
+        shared_mm(HELD)
+        held = gp.tile([P, 2 * T], U32, name="held", tag="ring%d" % slot[last], align_bytes=64)
+        for a in range(HELD + 1, PASSES):
+            sh_quant(a, held[:, (a - HELD - 1) * T:(a - HELD) * T])
+            shared_mm(a)
 
-        nc.vector.tensor_scalar(out=ys[:, 512:], in0=ps_sb[:, 256:], scalar1=bias[:, E:E + 1], scalar2=0.0, op0=ADD, op1=MAX)
-        nc.vector.tensor_tensor(ys[:, 512:], ys[:, 512:], ys[:, 512:], MULT)
-        nc.scalar.activation(out=ys[:, :512], in_=ps_sa[:], func=RELU, bias=bias[:, E:E + 1])
-        nc.scalar.activation(out=ys[:, :512], in_=ys[:, :512], func=SQUARE)
+        halves = (slice(0, H), slice(H, T))
+        nc.scalar.activation(out=ys[:, :H], in_=ps_sa[:, :H], func=RELU, bias=bias[:, E:E + 1])
+        nc.scalar.activation(out=ys[:, H:], in_=ps_sb[:, 512 - H:], func=RELU, bias=bias[:, E:E + 1])
+        for c in halves:
+            nc.scalar.activation(out=ys[:, c], in_=ys[:, c], func=SQUARE)
 
         nc.vector.tensor_tensor(g1[:], y[:].indirect(pos1_t[:]), gate_t[:, 0, :], MULT)
-        nc.vector.tensor_tensor(g1[:], g1[:], ys[:], ADD)
-        for lo, n in ((0, 512), (512, 256)):
-            c = slice(lo, lo + n)
-            nc.vector.tensor_tensor(g2[:, c], y[:].indirect(pos2_t[:, lo // 16:(lo + n) // 16]), gate_t[:, 1, c], MULT)
-            nc.vector.tensor_tensor(ot[:, c], g1[:, c], g2[:, c], ADD)
+        nc.vector.tensor_tensor(g2[:, :H], y[:].indirect(pos2_t[:, :H // 16]), gate_t[:, 1, :H], MULT)
+        nc.vector.tensor_tensor(g2[:, H:], y[:].indirect(pos2_t[:, H // 16:]), gate_t[:, 1, H:], MULT)
+        for c in halves:
+            nc.vector.tensor_tensor(g1[:, c], g1[:, c], g2[:, c], ADD)
+        for c in halves:
+            nc.vector.tensor_tensor(ot[:, c], g1[:, c], ys[:, c], ADD)
             nc.sync.dma_start(out=out[:, c], in_=ot[:, c])

@@ -6,9 +6,11 @@ K, T, E, C, N = 2560, 768, 12, 128, 128
 S = E * C
 P = 128
 PASSES = K // 512
-RING = 3
-HELD = 2
-GROUPS = ((0, 512), (512, 512), (1024, 256), (1280, 256))
+LAST = PASSES - 1
+WINDOW = 2048
+BANK = 512
+EARLY = 0
+BLOCK = 2 * T
 FLOPS = 2 * K * N * (S + T)
 
 F32 = mybir.dt.float32
@@ -20,6 +22,7 @@ U8 = mybir.dt.uint8
 FP8 = mybir.dt.float8_e4m3fn_x4
 FP4 = mybir.dt.float4_e2m1fn_x4
 ADD, MULT = mybir.AluOpType.add, mybir.AluOpType.mult
+COPY = mybir.ActivationFunctionType.Copy
 RELU = mybir.ActivationFunctionType.Relu
 SQUARE = mybir.ActivationFunctionType.Square
 
@@ -28,10 +31,8 @@ def tile_moe_shr_lin_relu2_kernel(tc, xT, w_words, w_scales, b, gate, offs, pos1
     nc = tc.nc
     with ExitStack() as ctx:
         keep = ctx.enter_context(tc.tile_pool(name="keep", bufs=1))
-        xpool = ctx.enter_context(tc.tile_pool(name="xpool", bufs=8))
-        gp = ctx.enter_context(tc.tile_pool(name="gp", bufs=1))
-        gip = ctx.enter_context(tc.tile_pool(name="gip", bufs=4))
-        shp = ctx.enter_context(tc.tile_pool(name="shp", bufs=3))
+        cdp = ctx.enter_context(tc.tile_pool(name="cdp", bufs=PASSES))
+        shp = ctx.enter_context(tc.tile_pool(name="shp", bufs=PASSES - EARLY))
         psum = ctx.enter_context(tc.psum_pool(name="psum", bufs=1))
 
         offs_t = keep.tile([P, S // 16], U16, name="offs_t")
@@ -41,38 +42,44 @@ def tile_moe_shr_lin_relu2_kernel(tc, xT, w_words, w_scales, b, gate, offs, pos1
         gate_t = keep.tile([P, 2, T], F32, name="gate_t")
         wt = keep.tile([P, (E + 1) * PASSES, 2 * N], U8, name="wt", align_bytes=64)
         wsc = keep.tile([P, (E + 1) * PASSES, N], U8, name="wsc", align_bytes=64)
-        win = [keep.tile([P, 2, 2 * T], BF16, name="win%d" % a, align_bytes=64) for a in range(PASSES)]
-        codes = [keep.tile([P, S], U32, name="codes%d" % a, align_bytes=64) for a in range(PASSES)]
-        cscale = [keep.tile([P, S], U8, name="cscale%d" % a, align_bytes=64) for a in range(PASSES)]
+        arena = keep.tile([P, (PASSES + 2) * BLOCK - T + WINDOW], U32, name="arena", align_bytes=64)
+        picked = keep.tile([P, 6 * S], U32, name="picked", tag="picked", align_bytes=64)
+        planes = keep.tile([P, 2 * T], BF16, name="planes", align_bytes=64)
         sscale = [keep.tile([P, T], U8, name="sscale%d" % a, align_bytes=64) for a in range(PASSES)]
         y = keep.tile([P, S], F32, name="y")
         ys = keep.tile([P, T], F32, name="ys")
         g1 = keep.tile([P, T], F32, name="g1")
         g2 = keep.tile([P, T], F32, name="g2")
-        ot = keep.tile([P, T], F32, name="ot")
 
-        ps_sa = psum.tile([P, 512], F32, name="ps_sa")
-        ps_sb = psum.tile([P, 512], F32, name="ps_sb")
-        ps = {lo: psum.tile([P, 512], F32, name="ps%d" % lo) for lo, n in GROUPS}
+        ps_sa = psum.tile([P, BANK], F32, name="ps_sa")
+        ps_sb = psum.tile([P, BANK], F32, name="ps_sb")
+        ps = [psum.tile([P, BANK], F32, name="ps%d" % i) for i in range(S // BANK)]
 
+        nc.vector.memset(arena[:, (PASSES + 2) * BLOCK:], 0)
         nc.gpsimd.memset(wsc[:].rearrange("p a n -> p (a n)").bitcast(I32), 0)
 
         xv = xT.rearrange("(a p j) t -> a p j t", a=PASSES, j=4)
         xr = {}
         H = T // 2
 
+        def block(k):
+            return (PASSES + 1 - k) * BLOCK
+
         def load_x(a, u):
-            t = xpool.tile([P, 2, T], F32, name="xr")
-            if a == 0 and u == 0:
+            if u == 1 and a > 0:
+                t = arena[:, block(a + 2):block(a + 2) + BLOCK].bitcast(F32).rearrange("p (j t) -> p j t", j=2)
+            elif u == 0 and 0 < a < LAST:
+                t = picked[:, (a - 1) * S:a * S].bitcast(F32).rearrange("p (j t) -> p j t", j=2)
+            else:
+                t = keep.tile([P, 2, T], F32, name="x%d%d" % (a, u))[:]
+            if (a, u) == (0, 1):
                 nc.sync.dma_start(out=t[:, :, :H], in_=xv[a][:, 2 * u:2 * u + 2, :H])
                 nc.sync.dma_start(out=t[:, :, H:], in_=xv[a][:, 2 * u:2 * u + 2, H:])
             else:
-                nc.sync.dma_start(out=t[:], in_=xv[a][:, 2 * u:2 * u + 2, :])
+                nc.sync.dma_start(out=t, in_=xv[a][:, 2 * u:2 * u + 2, :])
             xr[a, u] = t
 
         def late_loads():
-            load_x(4, 0)
-            load_x(4, 1)
             nc.sync.dma_start(out=bias[:], in_=b)
             wsv = w_scales.bitcast(I32).rearrange("e a q n -> q (e a) n")
             for q in range(4):
@@ -86,37 +93,57 @@ def tile_moe_shr_lin_relu2_kernel(tc, xT, w_words, w_scales, b, gate, offs, pos1
             nc.sync.dma_start(pos1_t[:], pos1)
             nc.sync.dma_start(pos2_t[:], pos2)
 
-        gi, sh, scodes = {}, {}, {}
+        sh, codes, cscale, scodes = {}, {}, {}, {}
+        rows = picked[:].rearrange("p (q s) -> p s q", s=BANK)
+
+        def pick_start(a, u):
+            return (3 + u * (1 + a % 2)) * S
+
+        def grouped(a):
+            start = block(min(a, LAST - 1) + 3)
+            return arena[:, start:start + 2 * BLOCK]
 
         def cast(a, u):
-            d = win[a][:, u, :].rearrange("p (t j) -> p t j", j=2)
-            s = xr[a, u][:].rearrange("p j t -> p t j")
-            if a == 0 and u == 0:
+            d = arena[:, block(a) + u * T:block(a) + (u + 1) * T].bitcast(BF16).rearrange("p (t j) -> p t j", j=2)
+            s = xr[a, u].rearrange("p j t -> p t j")
+            if (a, u) == (0, 1):
                 nc.vector.tensor_copy(out=d[:, :H, :], in_=s[:, :H, :])
                 nc.vector.tensor_copy(out=d[:, H:H + 256, :], in_=s[:, H:H + 256, :])
                 nc.scalar.copy(out=d[:, H + 256:, :], in_=s[:, H + 256:, :])
-            else:
+            elif a == 0:
                 nc.scalar.copy(out=d, in_=s)
+            else:
+                nc.gpsimd.tensor_scalar(out=d, in0=s, scalar1=1.0, scalar2=0.0, op0=MULT, op1=ADD)
 
-        def gather(i, a, lo, n):
-            g = gp.tile([P, 2, 512], U32, name="g", tag="ring%d" % slot[i], align_bytes=64)
-            for u in range(2):
-                nc.vector.tensor_copy(g[:, u, :n], win[a][:, u, :].bitcast(U32).indirect(offs_t[:, lo // 16:(lo + n) // 16]))
-            return g
+        def gather(a, u):
+            start = block(a) + u * T
+            nc.vector.tensor_copy(picked[:, pick_start(a, u):pick_start(a, u) + S], arena[:, start:start + WINDOW].indirect(offs_t[:]))
 
-        def inter(g, a, lo, n):
-            t = gip.tile([P, 2 * 1024], BF16, name="gi", align_bytes=64)
-            gi[a, lo] = t
-            nc.scalar.copy(out=t[:].bitcast(U32)[:, :2 * n].rearrange("p (s u) -> p s u", u=2),
-                           in_=g[:, :, :n].rearrange("p u s -> p s u"))
+        def scalar_gather(k):
+            v = picked[:, k * S:k * S + BANK].bitcast(BF16).rearrange("p (s j) -> p s j", j=2)
+            for j in range(2):
+                nc.scalar.activation(v[:, :, j], planes[:, j * T:(j + 1) * T].indirect(offs_t[:, k * BANK // 16:(k + 1) * BANK // 16]), COPY)
+
+        def inter(a, lo, n):
+            dst = grouped(a)[:, 2 * lo:2 * (lo + n)].rearrange("p (s u) -> p s u", u=2)
+            if a == LAST:
+                r0, r1 = 3 * (lo // BANK), (pick_start(a, 1) + lo) // BANK
+                src = rows[:, :, r0:r1 + 1:r1 - r0]
+            else:
+                src = picked[:, 3 * S:].rearrange("p (q s) -> p s q", s=S)[:, lo:lo + n, 0:2 + a % 2:1 + a % 2]
+            nc.scalar.copy(out=dst, in_=src)
 
         def quant(a, lo, n):
-            nc.vector.quantize_mx(out=codes[a][:, lo:lo + n].bitcast(FP8), scales=cscale[a][:, lo:lo + n], in_=gi[a, lo][:, :4 * n])
+            if lo == 0:
+                codes[a] = cdp.tile([P, S], U32, name="codes", align_bytes=64)
+                cscale[a] = cdp.tile([P, S], U8, name="cscale", align_bytes=64)
+            nc.vector.quantize_mx(out=codes[a][:, lo:lo + n].bitcast(FP8), scales=cscale[a][:, lo:lo + n],
+                                  in_=grouped(a)[:, 2 * lo:2 * (lo + n)].bitcast(BF16))
 
         def sh_inter(a):
             t = shp.tile([P, 4 * T], BF16, name="sh", align_bytes=64)
             nc.scalar.copy(out=t[:].bitcast(U32).rearrange("p (s u) -> p s u", u=2),
-                           in_=win[a][:].rearrange("p u t -> p (u t)").bitcast(U32).rearrange("p (u s) -> p s u", u=2))
+                           in_=arena[:, block(a):block(a) + BLOCK].rearrange("p (u s) -> p s u", u=2))
             sh[a] = t
 
         def sh_quant(a, dst):
@@ -130,68 +157,61 @@ def tile_moe_shr_lin_relu2_kernel(tc, xT, w_words, w_scales, b, gate, offs, pos1
                                 rhs=cd[a][:, cols].bitcast(FP8), rhs_scale=cs[a][:, cols], start=start, stop=stop)
 
         def shared_mm(a):
-            mm(ps_sa[:], E, a, scodes, sscale, slice(0, 512), a == 0, a == PASSES - 1)
-            mm(ps_sb[:], E, a, scodes, sscale, slice(256, 768), a == 0, a == PASSES - 1)
+            mm(ps_sa[:], E, a, scodes, sscale, slice(0, BANK), a == 0, a == LAST)
+            mm(ps_sb[:], E, a, scodes, sscale, slice(T - BANK, T), a == 0, a == LAST)
 
         def routed_mm(a, lo, n):
-            for glo, gn in GROUPS:
-                if lo <= glo < lo + n:
-                    for c0 in range(0, gn, C):
-                        mm(ps[glo][:, c0:c0 + C], (glo + c0) // C, a, codes, cscale, slice(glo + c0, glo + c0 + C),
-                           a == 0 and c0 == 0, a == PASSES - 1 and c0 + C == gn)
+            for s0 in range(lo, lo + n, C):
+                c0 = s0 % BANK
+                mm(ps[s0 // BANK][:, c0:c0 + C], s0 // C, a, codes, cscale, slice(s0, s0 + C),
+                   a == 0 and c0 == 0, a == LAST and c0 + C == BANK)
 
-        def routed_out(lo, n):
-            for c0 in range(0, n, C):
+        def routed_relu(lo):
+            for c0 in range(0, BANK, C):
                 e = (lo + c0) // C
-                nc.scalar.activation(out=y[:, lo + c0:lo + c0 + C], in_=ps[lo][:, c0:c0 + C], func=RELU, bias=bias[:, e:e + 1])
-            nc.scalar.activation(out=y[:, lo:lo + n], in_=y[:, lo:lo + n], func=SQUARE)
+                nc.scalar.activation(out=y[:, lo + c0:lo + c0 + C], in_=ps[lo // BANK][:, c0:c0 + C], func=RELU, bias=bias[:, e:e + 1])
 
-        def early_shared(a):
-            sh_inter(a)
-            t = keep.tile([P, T], U32, name="scodes%d" % a, align_bytes=64)
-            sh_quant(a, t)
-            shared_mm(a)
+        def routed_square(lo):
+            nc.scalar.activation(out=y[:, lo:lo + BANK], in_=y[:, lo:lo + BANK], func=SQUARE)
 
-        def finish(a, lo, n):
-            quant(a, lo, n)
-            routed_mm(a, lo, n)
+        def finish(a, pieces):
+            for lo, n in pieces:
+                inter(a, lo, n)
+            for lo, n in pieces:
+                quant(a, lo, n)
+                routed_mm(a, lo, n)
 
         nc.sync.dma_start(offs_t[:], offs)
-        for a in range(4):
-            load_x(a, 0)
-            load_x(a, 1)
-        cast(0, 0)
-        cast(0, 1)
+        for a, u in ((0, 1), (0, 0), (1, 1), (1, 0), (LAST, 0), (2, 1), (2, 0), (3, 1), (3, 0), (LAST, 1)):
+            load_x(a, u)
         late_loads()
-
-        steps = [(a, lo, 512) for a in range(PASSES - 1) for lo in (0, 512, 1024)] + [(PASSES - 1, lo, n) for lo, n in GROUPS]
-        jobs = []
-        for a in range(PASSES - 1):
-            jobs += [lambda a=a: cast(a + 1, 0), lambda a=a: cast(a + 1, 1),
-                     lambda a=a: early_shared(a) if a < HELD else sh_inter(a)]
-        jobs += [lambda: sh_inter(PASSES - 1)]
-        last = len(steps) - 1
-        slot = [i % RING for i in range(last - 2)]
-        while len(slot) <= last:
-            slot.append(slot[-2])
-        for i, (a, lo, n) in enumerate(steps):
-            g = gather(i, a, lo, n)
-            if jobs:
-                jobs.pop(0)()
-            inter(g, a, lo, n)
-            if i > 0:
-                finish(*steps[i - 1])
-            if i == last - 2:
-                routed_out(*GROUPS[0])
-        held = gp.tile([P, T], U32, name="held", tag="ring%d" % slot[last - 1], align_bytes=64)
-        sh_quant(HELD, held)
-        finish(*steps[last])
-        for lo, n in GROUPS[1:]:
-            routed_out(lo, n)
-        shared_mm(HELD)
-        held = gp.tile([P, 2 * T], U32, name="held", tag="ring%d" % slot[last], align_bytes=64)
-        for a in range(HELD + 1, PASSES):
-            sh_quant(a, held[:, (a - HELD - 1) * T:(a - HELD) * T])
+        cast(0, 1)
+        for a in range(LAST):
+            gather(a, 1)
+            if a == 0:
+                cast(0, 0)
+            else:
+                finish(a - 1, ((0, 1024), (1024, 512)))
+                scalar_gather(a - 1)
+            gather(a, 0)
+            cast(a + 1, 1)
+            cast(a + 1, 0)
+            if a == 0:
+                nc.gpsimd.tensor_scalar(out=planes[:], in0=xr[LAST, 0].rearrange("p j t -> p (j t)"), scalar1=1.0, scalar2=0.0, op0=MULT, op1=ADD)
+            sh_inter(a)
+        gather(LAST, 1)
+        finish(LAST - 1, ((0, 1024), (1024, 512)))
+        sh_inter(LAST)
+        banks = [(lo, BANK) for lo in range(0, S, BANK)]
+        finish(LAST, banks)
+        for lo, n in banks:
+            routed_relu(lo)
+            if lo > 0:
+                routed_square(lo - BANK)
+        routed_square(S - BANK)
+        held = keep.tile([P, (PASSES - EARLY) * T], U32, name="held", tag="picked", align_bytes=64)
+        for a in range(EARLY, PASSES):
+            sh_quant(a, held[:, (a - EARLY) * T:(a - EARLY + 1) * T])
             shared_mm(a)
 
         halves = (slice(0, H), slice(H, T))
@@ -206,5 +226,5 @@ def tile_moe_shr_lin_relu2_kernel(tc, xT, w_words, w_scales, b, gate, offs, pos1
         for c in halves:
             nc.vector.tensor_tensor(g1[:, c], g1[:, c], g2[:, c], ADD)
         for c in halves:
-            nc.vector.tensor_tensor(ot[:, c], g1[:, c], ys[:, c], ADD)
-            nc.sync.dma_start(out=out[:, c], in_=ot[:, c])
+            nc.vector.tensor_tensor(g2[:, c], g1[:, c], ys[:, c], ADD)
+            nc.sync.dma_start(out=out[:, c], in_=g2[:, c])

@@ -43,8 +43,9 @@ def tile_moe_shr_lin_relu2_kernel(tc, xT, w_words, w_scales, b, gate, offs, pos1
         wt = keep.tile([P, (E + 1) * PASSES, 2 * N], U8, name="wt", align_bytes=64)
         wsc = keep.tile([P, (E + 1) * PASSES, N], U8, name="wsc", align_bytes=64)
         arena = keep.tile([P, (PASSES + 2) * BLOCK - T + WINDOW], U32, name="arena", align_bytes=64)
-        picked = keep.tile([P, 6 * S], U32, name="picked", tag="picked", align_bytes=64)
-        planes = keep.tile([P, 2 * T], BF16, name="planes", align_bytes=64)
+        picked = keep.tile([P, BANK + 6 * S], U32, name="picked", tag="picked", align_bytes=64)
+        planes = {LAST: keep.tile([P, 2 * T], BF16, name="planes", align_bytes=64)[:],
+                  LAST - 1: picked[:, 5 * BANK:5 * BANK + T].bitcast(BF16)}
         sscale = [keep.tile([P, T], U8, name="sscale%d" % a, align_bytes=64) for a in range(PASSES)]
         y = keep.tile([P, S], F32, name="y")
         ys = keep.tile([P, T], F32, name="ys")
@@ -66,10 +67,10 @@ def tile_moe_shr_lin_relu2_kernel(tc, xT, w_words, w_scales, b, gate, offs, pos1
             return (PASSES + 1 - k) * BLOCK
 
         def load_x(a, u):
-            if u == 1 and a > 0:
+            if u == 1 and 0 < a < LAST:
                 t = arena[:, block(a + 2):block(a + 2) + BLOCK].bitcast(F32).rearrange("p (j t) -> p j t", j=2)
             elif u == 0 and 0 < a < LAST:
-                t = picked[:, (a - 1) * S:a * S].bitcast(F32).rearrange("p (j t) -> p j t", j=2)
+                t = picked[:, BANK + (a - 1) * S:BANK + a * S].bitcast(F32).rearrange("p (j t) -> p j t", j=2)
             else:
                 t = keep.tile([P, 2, T], F32, name="x%d%d" % (a, u))[:]
             if (a, u) == (0, 1):
@@ -97,10 +98,10 @@ def tile_moe_shr_lin_relu2_kernel(tc, xT, w_words, w_scales, b, gate, offs, pos1
         rows = picked[:].rearrange("p (q s) -> p s q", s=BANK)
 
         def pick_start(a, u):
-            return (3 + u * (1 + a % 2)) * S
+            return BANK + (3 + u * (1 + a % 2)) * S
 
         def grouped(a):
-            start = block(min(a, LAST - 1) + 3)
+            start = (block(3), block(4), block(6) + T, block(6), block(1))[a]
             return arena[:, start:start + 2 * BLOCK]
 
         def cast(a, u):
@@ -115,26 +116,36 @@ def tile_moe_shr_lin_relu2_kernel(tc, xT, w_words, w_scales, b, gate, offs, pos1
             else:
                 nc.gpsimd.tensor_scalar(out=d, in0=s, scalar1=1.0, scalar2=0.0, op0=MULT, op1=ADD)
 
-        def gather(a, u):
-            start = block(a) + u * T
-            nc.vector.tensor_copy(picked[:, pick_start(a, u):pick_start(a, u) + S], arena[:, start:start + WINDOW].indirect(offs_t[:]))
+        def split(a):
+            nc.gpsimd.tensor_scalar(out=planes[a], in0=xr[a, 0].rearrange("p j t -> p (j t)"), scalar1=1.0, scalar2=0.0, op0=MULT, op1=ADD)
 
-        def scalar_gather(k):
-            v = picked[:, k * S:k * S + BANK].bitcast(BF16).rearrange("p (s j) -> p s j", j=2)
+        def gather(a, u, lo, n, window):
+            start = block(a) + u * T
+            nc.vector.tensor_copy(picked[:, pick_start(a, u) + lo:pick_start(a, u) + lo + n],
+                                  arena[:, start:start + window].indirect(offs_t[:, lo // 16:(lo + n) // 16]))
+
+        def scalar_row(a, k):
+            if a == LAST:
+                return (0, 1, 4)[k]
+            return 7
+
+        def scalar_gather(a, k):
+            r = scalar_row(a, k)
+            v = picked[:, r * BANK:(r + 1) * BANK].bitcast(BF16).rearrange("p (s j) -> p s j", j=2)
             for j in range(2):
-                nc.scalar.activation(v[:, :, j], planes[:, j * T:(j + 1) * T].indirect(offs_t[:, k * BANK // 16:(k + 1) * BANK // 16]), COPY)
+                nc.scalar.activation(v[:, :, j], planes[a][:, j * T:(j + 1) * T].indirect(offs_t[:, k * BANK // 16:(k + 1) * BANK // 16]), COPY)
 
         def inter(a, lo, n):
             dst = grouped(a)[:, 2 * lo:2 * (lo + n)].rearrange("p (s u) -> p s u", u=2)
-            if a == LAST:
-                r0, r1 = 3 * (lo // BANK), (pick_start(a, 1) + lo) // BANK
+            if a == LAST or (a, lo) == (LAST - 1, 0):
+                r0, r1 = scalar_row(a, lo // BANK), (pick_start(a, 1) + lo) // BANK
                 src = rows[:, :, r0:r1 + 1:r1 - r0]
             else:
-                src = picked[:, 3 * S:].rearrange("p (q s) -> p s q", s=S)[:, lo:lo + n, 0:2 + a % 2:1 + a % 2]
+                src = picked[:, BANK + 3 * S:].rearrange("p (q s) -> p s q", s=S)[:, lo:lo + n, 0:2 + a % 2:1 + a % 2]
             nc.scalar.copy(out=dst, in_=src)
 
         def quant(a, lo, n):
-            if lo == 0:
+            if a not in codes:
                 codes[a] = cdp.tile([P, S], U32, name="codes", align_bytes=64)
                 cscale[a] = cdp.tile([P, S], U8, name="cscale", align_bytes=64)
             nc.vector.quantize_mx(out=codes[a][:, lo:lo + n].bitcast(FP8), scales=cscale[a][:, lo:lo + n],
@@ -142,8 +153,9 @@ def tile_moe_shr_lin_relu2_kernel(tc, xT, w_words, w_scales, b, gate, offs, pos1
 
         def sh_inter(a):
             t = shp.tile([P, 4 * T], BF16, name="sh", align_bytes=64)
-            nc.scalar.copy(out=t[:].bitcast(U32).rearrange("p (s u) -> p s u", u=2),
-                           in_=arena[:, block(a):block(a) + BLOCK].rearrange("p (u s) -> p s u", u=2))
+            move = nc.gpsimd.tensor_copy if a == LAST else nc.scalar.copy
+            move(out=t[:].bitcast(U32).rearrange("p (s u) -> p s u", u=2),
+                 in_=arena[:, block(a):block(a) + BLOCK].rearrange("p (u s) -> p s u", u=2))
             sh[a] = t
 
         def sh_quant(a, dst):
@@ -182,28 +194,49 @@ def tile_moe_shr_lin_relu2_kernel(tc, xT, w_words, w_scales, b, gate, offs, pos1
                 routed_mm(a, lo, n)
 
         nc.sync.dma_start(offs_t[:], offs)
-        for a, u in ((0, 1), (0, 0), (1, 1), (1, 0), (LAST, 0), (2, 1), (2, 0), (3, 1), (3, 0), (LAST, 1)):
+        for a, u in ((0, 1), (0, 0), (4, 0), (1, 1), (1, 0), (2, 1), (2, 0), (3, 0), (3, 1), (4, 1)):
             load_x(a, u)
         late_loads()
+        pieces = ((BANK, S - BANK), (0, BANK))
         cast(0, 1)
-        for a in range(LAST):
-            gather(a, 1)
-            if a == 0:
-                cast(0, 0)
-            else:
-                finish(a - 1, ((0, 1024), (1024, 512)))
-                scalar_gather(a - 1)
-            gather(a, 0)
+        gather(0, 1, 0, S, WINDOW)
+        cast(0, 0)
+        gather(0, 0, 0, S, WINDOW)
+        split(4)
+        cast(1, 1)
+        cast(1, 0)
+        sh_inter(0)
+        scalar_gather(4, 0)
+        for a in (1, 2):
+            gather(a, 1, 0, S, WINDOW)
+            finish(a - 1, pieces)
+            gather(a, 0, 0, S, WINDOW)
+            scalar_gather(4, a)
+            sh_inter(a)
             cast(a + 1, 1)
             cast(a + 1, 0)
-            if a == 0:
-                nc.gpsimd.tensor_scalar(out=planes[:], in0=xr[LAST, 0].rearrange("p j t -> p (j t)"), scalar1=1.0, scalar2=0.0, op0=MULT, op1=ADD)
-            sh_inter(a)
-        gather(LAST, 1)
-        finish(LAST - 1, ((0, 1024), (1024, 512)))
-        sh_inter(LAST)
+            if a == 1:
+                split(3)
+        cast(4, 1)
+        gather(3, 1, 0, S, WINDOW)
+        finish(2, pieces)
+        gather(3, 0, BANK, S - BANK, WINDOW)
+        sh_inter(3)
+        scalar_gather(3, 0)
+        cast(4, 0)
+        sh_inter(4)
         banks = [(lo, BANK) for lo in range(0, S, BANK)]
-        finish(LAST, banks)
+        for lo, n in banks:
+            gather(4, 1, lo, n, 2 * BANK)
+        inter(3, 0, BANK)
+        for lo, n in banks:
+            if lo + BANK < S:
+                inter(3, lo + BANK, n)
+            inter(4, lo, n)
+        for lo, n in banks:
+            for a in (3, 4):
+                quant(a, lo, n)
+                routed_mm(a, lo, n)
         for lo, n in banks:
             routed_relu(lo)
             if lo > 0:

@@ -11,6 +11,8 @@ WINDOW = 2048
 BANK = 512
 EARLY = 0
 BLOCK = 2 * T
+PICKS = 11 * BANK
+SHARE = 2 * BANK
 FLOPS = 2 * K * N * (S + T)
 
 F32 = mybir.dt.float32
@@ -43,9 +45,9 @@ def tile_moe_shr_lin_relu2_kernel(tc, xT, w_words, w_scales, b, gate, offs, pos1
         wt = keep.tile([P, (E + 1) * PASSES, 2 * N], U8, name="wt", align_bytes=64)
         wsc = keep.tile([P, (E + 1) * PASSES, N], U8, name="wsc", align_bytes=64)
         arena = keep.tile([P, (PASSES + 2) * BLOCK - T + WINDOW], U32, name="arena", align_bytes=64)
-        picked = keep.tile([P, BANK + 6 * S], U32, name="picked", tag="picked", align_bytes=64)
+        picked = keep.tile([P, PICKS + 3 * S], U32, name="picked", tag="picked", align_bytes=64)
         planes = {LAST: keep.tile([P, 2 * T], BF16, name="planes", align_bytes=64)[:],
-                  LAST - 1: picked[:, 5 * BANK:5 * BANK + T].bitcast(BF16)}
+                  LAST - 1: picked[:, 3 * T:4 * T].bitcast(BF16)}
         sscale = [keep.tile([P, T], U8, name="sscale%d" % a, align_bytes=64) for a in range(PASSES)]
         y = keep.tile([P, S], F32, name="y")
         ys = keep.tile([P, T], F32, name="ys")
@@ -70,7 +72,7 @@ def tile_moe_shr_lin_relu2_kernel(tc, xT, w_words, w_scales, b, gate, offs, pos1
             if u == 1 and 0 < a < LAST:
                 t = arena[:, block(a + 2):block(a + 2) + BLOCK].bitcast(F32).rearrange("p (j t) -> p j t", j=2)
             elif u == 0 and 0 < a < LAST:
-                t = picked[:, BANK + (a - 1) * S:BANK + a * S].bitcast(F32).rearrange("p (j t) -> p j t", j=2)
+                t = picked[:, (2 * a - 1) * T:(2 * a + 1) * T].bitcast(F32).rearrange("p (j t) -> p j t", j=2)
             else:
                 t = keep.tile([P, 2, T], F32, name="x%d%d" % (a, u))[:]
             if (a, u) == (0, 1):
@@ -98,7 +100,7 @@ def tile_moe_shr_lin_relu2_kernel(tc, xT, w_words, w_scales, b, gate, offs, pos1
         rows = picked[:].rearrange("p (q s) -> p s q", s=BANK)
 
         def pick_start(a, u):
-            return BANK + (3 + u * (1 + a % 2)) * S
+            return PICKS + u * (1 + a % 2) * S
 
         def grouped(a):
             start = (block(3), block(4), block(6) + T, block(6), block(1))[a]
@@ -117,31 +119,34 @@ def tile_moe_shr_lin_relu2_kernel(tc, xT, w_words, w_scales, b, gate, offs, pos1
                 nc.gpsimd.tensor_scalar(out=d, in0=s, scalar1=1.0, scalar2=0.0, op0=MULT, op1=ADD)
 
         def split(a):
-            nc.gpsimd.tensor_scalar(out=planes[a], in0=xr[a, 0].rearrange("p j t -> p (j t)"), scalar1=1.0, scalar2=0.0, op0=MULT, op1=ADD)
+            for j in range(2):
+                if (a, j) == (LAST, 0):
+                    nc.scalar.copy(out=planes[a][:, :T], in_=xr[a, 0][:, 0, :])
+                elif a == LAST:
+                    nc.gpsimd.tensor_scalar(out=planes[a][:, T:], in0=xr[a, 0][:, 1, :], scalar1=1.0, scalar2=0.0, op0=MULT, op1=ADD)
+            if a < LAST:
+                nc.gpsimd.tensor_scalar(out=planes[a], in0=xr[a, 0].rearrange("p j t -> p (j t)"), scalar1=1.0, scalar2=0.0, op0=MULT, op1=ADD)
 
         def gather(a, u, lo, n, window):
             start = block(a) + u * T
             nc.vector.tensor_copy(picked[:, pick_start(a, u) + lo:pick_start(a, u) + lo + n],
                                   arena[:, start:start + window].indirect(offs_t[:, lo // 16:(lo + n) // 16]))
 
-        def scalar_row(a, k):
-            if a == LAST:
-                return (0, 1, 4)[k]
-            return 7
+        def scalar_start(a):
+            return 0 if a == LAST else 4 * T
 
-        def scalar_gather(a, k):
-            r = scalar_row(a, k)
-            v = picked[:, r * BANK:(r + 1) * BANK].bitcast(BF16).rearrange("p (s j) -> p s j", j=2)
+        def scalar_gather(a, lo, n):
+            v = picked[:, scalar_start(a) + lo:scalar_start(a) + lo + n].bitcast(BF16).rearrange("p (s j) -> p s j", j=2)
             for j in range(2):
-                nc.scalar.activation(v[:, :, j], planes[a][:, j * T:(j + 1) * T].indirect(offs_t[:, k * BANK // 16:(k + 1) * BANK // 16]), COPY)
+                nc.scalar.activation(v[:, :, j], planes[a][:, j * T:(j + 1) * T].indirect(offs_t[:, lo // 16:(lo + n) // 16]), COPY)
 
         def inter(a, lo, n):
             dst = grouped(a)[:, 2 * lo:2 * (lo + n)].rearrange("p (s u) -> p s u", u=2)
-            if a == LAST or (a, lo) == (LAST - 1, 0):
-                r0, r1 = scalar_row(a, lo // BANK), (pick_start(a, 1) + lo) // BANK
+            if a == LAST or (a == LAST - 1 and lo < SHARE):
+                r0, r1 = (scalar_start(a) + lo) // BANK, (pick_start(a, 1) + lo) // BANK
                 src = rows[:, :, r0:r1 + 1:r1 - r0]
             else:
-                src = picked[:, BANK + 3 * S:].rearrange("p (q s) -> p s q", s=S)[:, lo:lo + n, 0:2 + a % 2:1 + a % 2]
+                src = picked[:, PICKS:].rearrange("p (q s) -> p s q", s=S)[:, lo:lo + n, 0:2 + a % 2:1 + a % 2]
             nc.scalar.copy(out=dst, in_=src)
 
         def quant(a, lo, n):
@@ -153,9 +158,15 @@ def tile_moe_shr_lin_relu2_kernel(tc, xT, w_words, w_scales, b, gate, offs, pos1
 
         def sh_inter(a):
             t = shp.tile([P, 4 * T], BF16, name="sh", align_bytes=64)
-            move = nc.gpsimd.tensor_copy if a == LAST else nc.scalar.copy
-            move(out=t[:].bitcast(U32).rearrange("p (s u) -> p s u", u=2),
-                 in_=arena[:, block(a):block(a) + BLOCK].rearrange("p (u s) -> p s u", u=2))
+            dst = t[:].bitcast(U32).rearrange("p (s u) -> p s u", u=2)
+            src = arena[:, block(a):block(a) + BLOCK].rearrange("p (u s) -> p s u", u=2)
+            if a == 0:
+                nc.gpsimd.tensor_copy(out=dst[:, :H, :], in_=src[:, :H, :])
+                nc.gpsimd.tensor_copy(out=dst[:, H:, :], in_=src[:, H:, :])
+            elif a == LAST:
+                nc.gpsimd.tensor_copy(out=dst, in_=src)
+            else:
+                nc.scalar.copy(out=dst, in_=src)
             sh[a] = t
 
         def sh_quant(a, dst):
@@ -193,8 +204,9 @@ def tile_moe_shr_lin_relu2_kernel(tc, xT, w_words, w_scales, b, gate, offs, pos1
                 quant(a, lo, n)
                 routed_mm(a, lo, n)
 
+        load_x(0, 1)
         nc.sync.dma_start(offs_t[:], offs)
-        for a, u in ((0, 1), (0, 0), (4, 0), (1, 1), (1, 0), (2, 1), (2, 0), (3, 0), (3, 1), (4, 1)):
+        for a, u in ((0, 0), (4, 0), (1, 1), (1, 0), (2, 1), (2, 0), (3, 0), (3, 1), (4, 1)):
             load_x(a, u)
         late_loads()
         pieces = ((BANK, S - BANK), (0, BANK))
@@ -206,12 +218,14 @@ def tile_moe_shr_lin_relu2_kernel(tc, xT, w_words, w_scales, b, gate, offs, pos1
         cast(1, 1)
         cast(1, 0)
         sh_inter(0)
-        scalar_gather(4, 0)
+        scalar_gather(4, 0, H)
+        scalar_gather(4, H, H)
         for a in (1, 2):
             gather(a, 1, 0, S, WINDOW)
             finish(a - 1, pieces)
             gather(a, 0, 0, S, WINDOW)
-            scalar_gather(4, a)
+            for lo in (0, H):
+                scalar_gather(*((4, T + lo, H) if a == 1 else (3, lo, H)))
             sh_inter(a)
             cast(a + 1, 1)
             cast(a + 1, 0)
@@ -220,9 +234,9 @@ def tile_moe_shr_lin_relu2_kernel(tc, xT, w_words, w_scales, b, gate, offs, pos1
         cast(4, 1)
         gather(3, 1, 0, S, WINDOW)
         finish(2, pieces)
-        gather(3, 0, BANK, S - BANK, WINDOW)
+        gather(3, 0, SHARE, S - SHARE, WINDOW)
         sh_inter(3)
-        scalar_gather(3, 0)
+        scalar_gather(3, T, SHARE - T)
         cast(4, 0)
         sh_inter(4)
         banks = [(lo, BANK) for lo in range(0, S, BANK)]

@@ -6,13 +6,17 @@ K, T, E, C, N = 2560, 768, 12, 128, 128
 S = E * C
 P = 128
 PASSES = K // 512
-LAST = PASSES - 1
+X = PASSES - 1
 WINDOW = 2048
 BANK = 512
-EARLY = 0
-BLOCK = 2 * T
-PICKS = 11 * BANK
-SHARE = 2 * BANK
+H = T // 2
+HEAD = 448
+HEAD_TAIL = 704
+SPLIT = 416
+ROW = T // 2
+RAW = 4 * T
+TAIL = 128
+STEP = ROW + TAIL + RAW
 FLOPS = 2 * K * N * (S + T)
 
 F32 = mybir.dt.float32
@@ -33,8 +37,6 @@ def tile_moe_shr_lin_relu2_kernel(tc, xT, w_words, w_scales, b, gate, offs, pos1
     nc = tc.nc
     with ExitStack() as ctx:
         keep = ctx.enter_context(tc.tile_pool(name="keep", bufs=1))
-        cdp = ctx.enter_context(tc.tile_pool(name="cdp", bufs=PASSES))
-        shp = ctx.enter_context(tc.tile_pool(name="shp", bufs=PASSES - EARLY))
         psum = ctx.enter_context(tc.psum_pool(name="psum", bufs=1))
 
         offs_t = keep.tile([P, S // 16], U16, name="offs_t")
@@ -44,11 +46,12 @@ def tile_moe_shr_lin_relu2_kernel(tc, xT, w_words, w_scales, b, gate, offs, pos1
         gate_t = keep.tile([P, 2, T], F32, name="gate_t")
         wt = keep.tile([P, (E + 1) * PASSES, 2 * N], U8, name="wt", align_bytes=64)
         wsc = keep.tile([P, (E + 1) * PASSES, N], U8, name="wsc", align_bytes=64)
-        arena = keep.tile([P, (PASSES + 2) * BLOCK - T + WINDOW], U32, name="arena", align_bytes=64)
-        picked = keep.tile([P, PICKS + 3 * S], U32, name="picked", tag="picked", align_bytes=64)
-        planes = {LAST: keep.tile([P, 2 * T], BF16, name="planes", align_bytes=64)[:],
-                  LAST - 1: picked[:, 3 * T:4 * T].bitcast(BF16)}
-        sscale = [keep.tile([P, T], U8, name="sscale%d" % a, align_bytes=64) for a in range(PASSES)]
+        base = 4 * T + HEAD_TAIL
+        arena = keep.tile([P, base + 4 * STEP + RAW], U32, name="arena", tag="arena", align_bytes=64)
+        late = keep.tile([P, 3 * T + WINDOW], U32, name="late", tag="late", align_bytes=64)
+        picked = keep.tile([P, PASSES * 2 * S], U32, name="picked", align_bytes=64)
+        cscale = keep.tile([P, PASSES * S], U8, name="cscale", align_bytes=64)
+        sscale = keep.tile([P, PASSES * T], U8, name="sscale", align_bytes=64)
         y = keep.tile([P, S], F32, name="y")
         ys = keep.tile([P, T], F32, name="ys")
         g1 = keep.tile([P, T], F32, name="g1")
@@ -58,29 +61,34 @@ def tile_moe_shr_lin_relu2_kernel(tc, xT, w_words, w_scales, b, gate, offs, pos1
         ps_sb = psum.tile([P, BANK], F32, name="ps_sb")
         ps = [psum.tile([P, BANK], F32, name="ps%d" % i) for i in range(S // BANK)]
 
-        nc.vector.memset(arena[:, (PASSES + 2) * BLOCK:], 0)
+        nc.vector.memset(arena[:, 4 * T:base], 0)
+        for j in range(4):
+            nc.scalar.copy(out=arena[:, base + j * STEP + ROW:base + j * STEP + ROW + TAIL], in_=arena[:, 4 * T:4 * T + TAIL])
+        nc.vector.memset(late[:, 4 * T:], 0)
         nc.gpsimd.memset(wsc[:].rearrange("p a n -> p (a n)").bitcast(I32), 0)
 
         xv = xT.rearrange("(a p j) t -> a p j t", a=PASSES, j=4)
-        xr = {}
-        H = T // 2
 
-        def block(k):
-            return (PASSES + 1 - k) * BLOCK
+        def plane_start(j):
+            return base + j * STEP
 
-        def load_x(a, u):
-            if u == 1 and 0 < a < LAST:
-                t = arena[:, block(a + 2):block(a + 2) + BLOCK].bitcast(F32).rearrange("p (j t) -> p j t", j=2)
-            elif u == 0 and 0 < a < LAST:
-                t = picked[:, (2 * a - 1) * T:(2 * a + 1) * T].bitcast(F32).rearrange("p (j t) -> p j t", j=2)
-            else:
-                t = keep.tile([P, 2, T], F32, name="x%d%d" % (a, u))[:]
-            if (a, u) == (0, 1):
-                nc.sync.dma_start(out=t[:, :, :H], in_=xv[a][:, 2 * u:2 * u + 2, :H])
-                nc.sync.dma_start(out=t[:, :, H:], in_=xv[a][:, 2 * u:2 * u + 2, H:])
-            else:
-                nc.sync.dma_start(out=t, in_=xv[a][:, 2 * u:2 * u + 2, :])
-            xr[a, u] = t
+        def raw_start(a):
+            return base + ROW + TAIL if a == X else base + (a + 1) * STEP + (ROW + TAIL if a < 3 else 0)
+
+        def raw(a, j, n):
+            s = raw_start(a) + j * T
+            return arena[:, s:s + n * T].bitcast(F32)
+
+        def pairs(a, u, n):
+            tile = arena if a < 2 else late
+            s = (1 - a % 2) * 2 * T + u * T
+            return tile[:, s:s + n]
+
+        def load_rows(a, j, n):
+            nc.sync.dma_start(out=raw(a, j, n).rearrange("p (j t) -> p j t", j=n), in_=xv[a][:, j:j + n, :])
+
+        def load_cols(a, u, lo, hi):
+            nc.sync.dma_start(out=raw(a, 2 * u, 2).rearrange("p (j t) -> p j t", j=2)[:, :, lo:hi], in_=xv[a][:, 2 * u:2 * u + 2, lo:hi])
 
         def late_loads():
             nc.sync.dma_start(out=bias[:], in_=b)
@@ -96,170 +104,139 @@ def tile_moe_shr_lin_relu2_kernel(tc, xT, w_words, w_scales, b, gate, offs, pos1
             nc.sync.dma_start(pos1_t[:], pos1)
             nc.sync.dma_start(pos2_t[:], pos2)
 
-        sh, codes, cscale, scodes = {}, {}, {}, {}
-        rows = picked[:].rearrange("p (q s) -> p s q", s=BANK)
+        def pool_round(dst, src):
+            nc.gpsimd.tensor_scalar(out=dst, in0=src, scalar1=1.0, scalar2=0.0, op0=MULT, op1=ADD)
 
-        def pick_start(a, u):
-            return PICKS + u * (1 + a % 2) * S
+        def cast(a, u, lo, hi, rnd):
+            d = pairs(a, u, T).bitcast(BF16).rearrange("p (t j) -> p t j", j=2)
+            s = raw(a, 2 * u, 2).rearrange("p (j t) -> p t j", j=2)
+            rnd(d[:, lo:hi, :], s[:, lo:hi, :])
 
-        def grouped(a):
-            start = (block(3), block(4), block(6) + T, block(6), block(1))[a]
-            return arena[:, start:start + 2 * BLOCK]
+        def plane(j, rnd):
+            rnd(arena[:, plane_start(j):plane_start(j) + ROW].bitcast(BF16), raw(X, j, 1))
 
-        def cast(a, u):
-            d = arena[:, block(a) + u * T:block(a) + (u + 1) * T].bitcast(BF16).rearrange("p (t j) -> p t j", j=2)
-            s = xr[a, u].rearrange("p j t -> p t j")
-            if (a, u) == (0, 1):
-                nc.vector.tensor_copy(out=d[:, :H, :], in_=s[:, :H, :])
-                nc.vector.tensor_copy(out=d[:, H:H + 256, :], in_=s[:, H:H + 256, :])
-                nc.scalar.copy(out=d[:, H + 256:, :], in_=s[:, H + 256:, :])
-            elif a == 0:
-                nc.scalar.copy(out=d, in_=s)
-            else:
-                nc.gpsimd.tensor_scalar(out=d, in0=s, scalar1=1.0, scalar2=0.0, op0=MULT, op1=ADD)
+        def picks(a, u, lo, n):
+            s = (2 * a + u) * S + lo
+            return picked[:, s:s + n]
 
-        def split(a):
-            for j in range(2):
-                if (a, j) == (LAST, 0):
-                    nc.scalar.copy(out=planes[a][:, :T], in_=xr[a, 0][:, 0, :])
-                elif a == LAST:
-                    nc.gpsimd.tensor_scalar(out=planes[a][:, T:], in0=xr[a, 0][:, 1, :], scalar1=1.0, scalar2=0.0, op0=MULT, op1=ADD)
-            if a < LAST:
-                nc.gpsimd.tensor_scalar(out=planes[a], in0=xr[a, 0].rearrange("p j t -> p (j t)"), scalar1=1.0, scalar2=0.0, op0=MULT, op1=ADD)
+        def gather(a, u, lo, window):
+            nc.vector.tensor_copy(picks(a, u, lo, S - lo), pairs(a, u, window).indirect(offs_t[:, lo // 16:]))
 
-        def gather(a, u, lo, n, window):
-            start = block(a) + u * T
-            nc.vector.tensor_copy(picked[:, pick_start(a, u) + lo:pick_start(a, u) + lo + n],
-                                  arena[:, start:start + window].indirect(offs_t[:, lo // 16:(lo + n) // 16]))
+        def head_gather(j):
+            v = picks(0, 1, 0, HEAD).bitcast(BF16).rearrange("p (s j) -> p s j", j=2)
+            nc.vector.tensor_copy(v[:, :, j], raw(0, 2 + j, 1).indirect(offs_t[:, :HEAD // 16]))
 
-        def scalar_start(a):
-            return 0 if a == LAST else 4 * T
+        def scalar_gather(j):
+            v = picks(X, j // 2, 0, S).bitcast(BF16).rearrange("p (s j) -> p s j", j=2)
+            w = arena[:, plane_start(j):plane_start(j) + ROW + TAIL].bitcast(BF16)
+            for lo in (0, T):
+                nc.scalar.activation(v[:, lo:lo + T, j % 2], w.indirect(offs_t[:, lo // 16:(lo + T) // 16]), COPY)
 
-        def scalar_gather(a, lo, n):
-            v = picked[:, scalar_start(a) + lo:scalar_start(a) + lo + n].bitcast(BF16).rearrange("p (s j) -> p s j", j=2)
-            for j in range(2):
-                nc.scalar.activation(v[:, :, j], planes[a][:, j * T:(j + 1) * T].indirect(offs_t[:, lo // 16:(lo + n) // 16]), COPY)
+        def quads(a, lo, n):
+            s = raw_start(a) - (0 if a == 3 else TAIL)
+            return arena[:, s + 2 * lo:s + 2 * (lo + n)]
 
-        def inter(a, lo, n):
-            dst = grouped(a)[:, 2 * lo:2 * (lo + n)].rearrange("p (s u) -> p s u", u=2)
-            if a == LAST or (a == LAST - 1 and lo < SHARE):
-                r0, r1 = (scalar_start(a) + lo) // BANK, (pick_start(a, 1) + lo) // BANK
-                src = rows[:, :, r0:r1 + 1:r1 - r0]
-            else:
-                src = picked[:, PICKS:].rearrange("p (q s) -> p s q", s=S)[:, lo:lo + n, 0:2 + a % 2:1 + a % 2]
-            nc.scalar.copy(out=dst, in_=src)
+        def weave(a, lo, n):
+            src = picked[:, 2 * a * S:2 * (a + 1) * S].rearrange("p (u s) -> p s u", u=2)[:, lo:lo + n, :]
+            nc.scalar.copy(out=quads(a, lo, n).rearrange("p (s u) -> p s u", u=2), in_=src)
 
-        def quant(a, lo, n):
-            if a not in codes:
-                codes[a] = cdp.tile([P, S], U32, name="codes", align_bytes=64)
-                cscale[a] = cdp.tile([P, S], U8, name="cscale", align_bytes=64)
-            nc.vector.quantize_mx(out=codes[a][:, lo:lo + n].bitcast(FP8), scales=cscale[a][:, lo:lo + n],
-                                  in_=grouped(a)[:, 2 * lo:2 * (lo + n)].bitcast(BF16))
+        shared_order = (X, 2, 3, 0, 1)
+        shared_start = {X: 0, 2: 2 * T, 3: 2 * S, 0: 6 * S, 1: 6 * S + 2 * T}
 
-        def sh_inter(a):
-            t = shp.tile([P, 4 * T], BF16, name="sh", align_bytes=64)
-            dst = t[:].bitcast(U32).rearrange("p (s u) -> p s u", u=2)
-            src = arena[:, block(a):block(a) + BLOCK].rearrange("p (u s) -> p s u", u=2)
-            if a == 0:
-                nc.gpsimd.tensor_copy(out=dst[:, :H, :], in_=src[:, :H, :])
-                nc.gpsimd.tensor_copy(out=dst[:, H:, :], in_=src[:, H:, :])
-            elif a == LAST:
-                nc.gpsimd.tensor_copy(out=dst, in_=src)
-            else:
-                nc.scalar.copy(out=dst, in_=src)
-            sh[a] = t
+        def shared_quads(a):
+            return picked[:, shared_start[a]:shared_start[a] + 2 * T]
 
-        def sh_quant(a, dst):
-            scodes[a] = dst
-            for lo, n in ((0, 512), (512, 256)):
-                nc.vector.quantize_mx(out=dst[:, lo:lo + n].bitcast(FP8), scales=sscale[a][:, lo:lo + n],
-                                      in_=sh[a][:, 4 * lo:4 * (lo + n)])
+        def shared_weave(a, copy):
+            copy(out=shared_quads(a).rearrange("p (s u) -> p s u", u=2), in_=pairs(a, 0, 2 * T).rearrange("p (u s) -> p s u", u=2))
 
-        def mm(dst, e, a, cd, cs, cols, start, stop):
+        def mm(dst, e, a, cd, cs, lo, n, start, stop):
             nc.tensor.matmul_mx(out=dst, lhsT=wt[:, e * PASSES + a, :].bitcast(FP4), lhsT_scale=wsc[:, e * PASSES + a, :],
-                                rhs=cd[a][:, cols].bitcast(FP8), rhs_scale=cs[a][:, cols], start=start, stop=stop)
+                                rhs=cd[:, lo:lo + n].bitcast(FP8), rhs_scale=cs[:, lo:lo + n], start=start, stop=stop)
 
-        def shared_mm(a):
-            mm(ps_sa[:], E, a, scodes, sscale, slice(0, BANK), a == 0, a == LAST)
-            mm(ps_sb[:], E, a, scodes, sscale, slice(T - BANK, T), a == 0, a == LAST)
+        load_rows(0, 2, 1)
+        nc.sync.dma_start(offs_t[:], offs)
+        load_rows(0, 3, 1)
+        load_rows(X, 0, 1)
+        load_cols(0, 0, 0, H)
+        load_cols(0, 0, H, T)
+        load_rows(X, 1, 1)
+        load_rows(1, 2, 2)
+        load_rows(X, 2, 1)
+        load_rows(1, 0, 2)
+        load_rows(2, 2, 2)
+        load_rows(X, 3, 1)
+        load_rows(2, 0, 2)
+        load_rows(3, 2, 2)
+        load_rows(3, 0, 2)
+        late_loads()
 
-        def routed_mm(a, lo, n):
-            for s0 in range(lo, lo + n, C):
-                c0 = s0 % BANK
-                mm(ps[s0 // BANK][:, c0:c0 + C], s0 // C, a, codes, cscale, slice(s0, s0 + C),
-                   a == 0 and c0 == 0, a == LAST and c0 + C == BANK)
+        head_gather(0)
+        head_gather(1)
+        cast(0, 1, 0, SPLIT, nc.scalar.copy)
+        cast(0, 1, SPLIT, T, pool_round)
+        plane(0, nc.scalar.copy)
+        gather(0, 1, HEAD, T + HEAD_TAIL)
+        scalar_gather(0)
+        cast(0, 0, 0, H, pool_round)
+        cast(0, 0, H, T, pool_round)
+        gather(0, 0, 0, WINDOW)
+        plane(1, pool_round)
+        scalar_gather(1)
+        weave(0, 0, S)
+        cast(1, 1, 0, T, pool_round)
+        gather(1, 1, 0, WINDOW)
+        plane(2, pool_round)
+        scalar_gather(2)
+        cast(1, 0, 0, T, pool_round)
+        gather(1, 0, 0, WINDOW)
+        weave(1, 0, S)
+        cast(2, 1, 0, T, pool_round)
+        gather(2, 1, 0, WINDOW)
+        plane(3, pool_round)
+        scalar_gather(3)
+        cast(2, 0, 0, T, pool_round)
+        gather(2, 0, 0, WINDOW)
+        weave(2, 0, S)
+        pool_round(shared_quads(X).bitcast(BF16).rearrange("p (t j) -> p t j", j=4), raw(X, 0, 4).rearrange("p (j t) -> p t j", j=4))
+        weave(X, 0, S)
+        cast(3, 1, 0, T, pool_round)
+        gather(3, 1, 0, WINDOW)
+        cast(3, 0, 0, T, pool_round)
+        gather(3, 0, 0, WINDOW)
+        shared_weave(2, nc.gpsimd.tensor_copy)
+        shared_weave(3, nc.gpsimd.tensor_copy)
+        weave(3, 0, S)
+        shared_weave(0, nc.scalar.copy)
+        shared_weave(1, nc.scalar.copy)
 
-        def routed_relu(lo):
+        codes = keep.tile([P, PASSES * S], U32, name="codes", tag="late", align_bytes=64)
+        order = (0, 1, 2, X, 3)
+        for a in order:
+            pieces = ((0, 2 * BANK), (2 * BANK, BANK)) if a != order[-1] else ((0, BANK), (BANK, BANK), (2 * BANK, BANK))
+            for lo, n in pieces:
+                nc.vector.quantize_mx(out=codes[:, a * S + lo:a * S + lo + n].bitcast(FP8), scales=cscale[:, a * S + lo:a * S + lo + n],
+                                      in_=quads(a, lo, n).bitcast(BF16))
+                for s0 in range(lo, lo + n, C):
+                    c0 = s0 % BANK
+                    mm(ps[s0 // BANK][:, c0:c0 + C], s0 // C, a, codes, cscale, a * S + s0, C,
+                       a == order[0] and c0 == 0, a == order[-1] and c0 + C == BANK)
+        for lo in range(0, S, BANK):
             for c0 in range(0, BANK, C):
                 e = (lo + c0) // C
                 nc.scalar.activation(out=y[:, lo + c0:lo + c0 + C], in_=ps[lo // BANK][:, c0:c0 + C], func=RELU, bias=bias[:, e:e + 1])
-
-        def routed_square(lo):
-            nc.scalar.activation(out=y[:, lo:lo + BANK], in_=y[:, lo:lo + BANK], func=SQUARE)
-
-        def finish(a, pieces):
-            for lo, n in pieces:
-                inter(a, lo, n)
-            for lo, n in pieces:
-                quant(a, lo, n)
-                routed_mm(a, lo, n)
-
-        load_x(0, 1)
-        nc.sync.dma_start(offs_t[:], offs)
-        for a, u in ((0, 0), (4, 0), (1, 1), (1, 0), (2, 1), (2, 0), (3, 0), (3, 1), (4, 1)):
-            load_x(a, u)
-        late_loads()
-        pieces = ((BANK, S - BANK), (0, BANK))
-        cast(0, 1)
-        gather(0, 1, 0, S, WINDOW)
-        cast(0, 0)
-        gather(0, 0, 0, S, WINDOW)
-        split(4)
-        cast(1, 1)
-        cast(1, 0)
-        sh_inter(0)
-        scalar_gather(4, 0, H)
-        scalar_gather(4, H, H)
-        for a in (1, 2):
-            gather(a, 1, 0, S, WINDOW)
-            finish(a - 1, pieces)
-            gather(a, 0, 0, S, WINDOW)
-            for lo in (0, H):
-                scalar_gather(*((4, T + lo, H) if a == 1 else (3, lo, H)))
-            sh_inter(a)
-            cast(a + 1, 1)
-            cast(a + 1, 0)
-            if a == 1:
-                split(3)
-        cast(4, 1)
-        gather(3, 1, 0, S, WINDOW)
-        finish(2, pieces)
-        gather(3, 0, SHARE, S - SHARE, WINDOW)
-        sh_inter(3)
-        scalar_gather(3, T, SHARE - T)
-        cast(4, 0)
-        sh_inter(4)
-        banks = [(lo, BANK) for lo in range(0, S, BANK)]
-        for lo, n in banks:
-            gather(4, 1, lo, n, 2 * BANK)
-        inter(3, 0, BANK)
-        for lo, n in banks:
-            if lo + BANK < S:
-                inter(3, lo + BANK, n)
-            inter(4, lo, n)
-        for lo, n in banks:
-            for a in (3, 4):
-                quant(a, lo, n)
-                routed_mm(a, lo, n)
-        for lo, n in banks:
-            routed_relu(lo)
             if lo > 0:
-                routed_square(lo - BANK)
-        routed_square(S - BANK)
-        held = keep.tile([P, (PASSES - EARLY) * T], U32, name="held", tag="picked", align_bytes=64)
-        for a in range(EARLY, PASSES):
-            sh_quant(a, held[:, (a - EARLY) * T:(a - EARLY + 1) * T])
-            shared_mm(a)
+                nc.scalar.activation(out=y[:, lo - BANK:lo], in_=y[:, lo - BANK:lo], func=SQUARE)
+        nc.scalar.activation(out=y[:, S - BANK:], in_=y[:, S - BANK:], func=SQUARE)
+
+        scodes = keep.tile([P, PASSES * T], U32, name="scodes", tag="arena", align_bytes=64)
+        runs = {0: ((0, 1024),), 1: ((256, 512),), 2: ((0, 512), (512, 256)), 3: ((0, 1024),), 4: ((256, 512),)}
+        for i, a in enumerate(shared_order):
+            for lo, n in runs[i]:
+                s0 = shared_start[a] + 2 * lo
+                nc.vector.quantize_mx(out=scodes[:, i * T + lo:i * T + lo + n].bitcast(FP8), scales=sscale[:, i * T + lo:i * T + lo + n],
+                                      in_=picked[:, s0:s0 + 2 * n].bitcast(BF16))
+            mm(ps_sa[:], E, a, scodes, sscale, i * T, BANK, i == 0, i == PASSES - 1)
+            mm(ps_sb[:], E, a, scodes, sscale, i * T + T - BANK, BANK, i == 0, i == PASSES - 1)
 
         halves = (slice(0, H), slice(H, T))
         nc.scalar.activation(out=ys[:, :H], in_=ps_sa[:, :H], func=RELU, bias=bias[:, E:E + 1])

@@ -10,9 +10,7 @@ X = PASSES - 1
 WINDOW = 2048
 BANK = 512
 H = T // 2
-HEAD = 448
-HEAD_TAIL = 704
-SPLIT = 416
+HEAD_TAIL = WINDOW - T
 ROW = T // 2
 RAW = 4 * T
 TAIL = 128
@@ -122,10 +120,6 @@ def tile_moe_shr_lin_relu2_kernel(tc, xT, w_words, w_scales, b, gate, offs, pos1
         def gather(a, u, lo, window):
             nc.vector.tensor_copy(picks(a, u, lo, S - lo), pairs(a, u, window).indirect(offs_t[:, lo // 16:]))
 
-        def head_gather(j):
-            v = picks(0, 1, 0, HEAD).bitcast(BF16).rearrange("p (s j) -> p s j", j=2)
-            nc.vector.tensor_copy(v[:, :, j], raw(0, 2 + j, 1).indirect(offs_t[:, :HEAD // 16]))
-
         def scalar_gather(j):
             v = picks(X, j // 2, 0, S).bitcast(BF16).rearrange("p (s j) -> p s j", j=2)
             w = arena[:, plane_start(j):plane_start(j) + ROW + TAIL].bitcast(BF16)
@@ -141,7 +135,7 @@ def tile_moe_shr_lin_relu2_kernel(tc, xT, w_words, w_scales, b, gate, offs, pos1
             nc.scalar.copy(out=quads(a, lo, n).rearrange("p (s u) -> p s u", u=2), in_=src)
 
         shared_order = (X, 2, 3, 0, 1)
-        shared_start = {X: 0, 2: 2 * T, 3: 2 * S, 0: 6 * S, 1: 6 * S + 2 * T}
+        shared_start = {X: 0, 2: 2 * T, 3: 2 * S, 0: 2 * S + 2 * T, 1: 6 * S}
 
         def shared_quads(a):
             return picked[:, shared_start[a]:shared_start[a] + 2 * T]
@@ -153,9 +147,9 @@ def tile_moe_shr_lin_relu2_kernel(tc, xT, w_words, w_scales, b, gate, offs, pos1
             nc.tensor.matmul_mx(out=dst, lhsT=wt[:, e * PASSES + a, :].bitcast(FP4), lhsT_scale=wsc[:, e * PASSES + a, :],
                                 rhs=cd[:, lo:lo + n].bitcast(FP8), rhs_scale=cs[:, lo:lo + n], start=start, stop=stop)
 
-        load_rows(0, 2, 1)
+        load_cols(0, 1, 0, H)
         nc.sync.dma_start(offs_t[:], offs)
-        load_rows(0, 3, 1)
+        load_cols(0, 1, H, T)
         load_rows(X, 0, 1)
         load_cols(0, 0, 0, H)
         load_cols(0, 0, H, T)
@@ -170,12 +164,10 @@ def tile_moe_shr_lin_relu2_kernel(tc, xT, w_words, w_scales, b, gate, offs, pos1
         load_rows(3, 0, 2)
         late_loads()
 
-        head_gather(0)
-        head_gather(1)
-        cast(0, 1, 0, SPLIT, nc.scalar.copy)
-        cast(0, 1, SPLIT, T, pool_round)
+        cast(0, 1, 0, H, nc.vector.tensor_copy)
+        cast(0, 1, H, T, nc.vector.tensor_copy)
         plane(0, nc.scalar.copy)
-        gather(0, 1, HEAD, T + HEAD_TAIL)
+        gather(0, 1, 0, WINDOW)
         scalar_gather(0)
         cast(0, 0, 0, H, pool_round)
         cast(0, 0, H, T, pool_round)
@@ -203,10 +195,10 @@ def tile_moe_shr_lin_relu2_kernel(tc, xT, w_words, w_scales, b, gate, offs, pos1
         gather(3, 1, 0, WINDOW)
         cast(3, 0, 0, T, pool_round)
         gather(3, 0, 0, WINDOW)
+        shared_weave(0, nc.gpsimd.tensor_copy)
         shared_weave(2, nc.gpsimd.tensor_copy)
         shared_weave(3, nc.gpsimd.tensor_copy)
         weave(3, 0, S)
-        shared_weave(0, nc.scalar.copy)
         shared_weave(1, nc.scalar.copy)
 
         codes = keep.tile([P, PASSES * S], U32, name="codes", tag="late", align_bytes=64)
@@ -229,7 +221,7 @@ def tile_moe_shr_lin_relu2_kernel(tc, xT, w_words, w_scales, b, gate, offs, pos1
         nc.scalar.activation(out=y[:, S - BANK:], in_=y[:, S - BANK:], func=SQUARE)
 
         scodes = keep.tile([P, PASSES * T], U32, name="scodes", tag="arena", align_bytes=64)
-        runs = {0: ((0, 1024),), 1: ((256, 512),), 2: ((0, 512), (512, 256)), 3: ((0, 1024),), 4: ((256, 512),)}
+        runs = {0: ((0, 1024),), 1: ((256, 512),), 2: ((0, 1024),), 3: ((256, 512),), 4: ((0, 512), (512, 256))}
         for i, a in enumerate(shared_order):
             for lo, n in runs[i]:
                 s0 = shared_start[a] + 2 * lo

@@ -51,9 +51,7 @@ def tile_moe_shr_lin_relu2_kernel(tc, xT, w_words, w_scales, b, gate, offs, pos1
         cscale = keep.tile([P, PASSES * S], U8, name="cscale", align_bytes=64)
         sscale = keep.tile([P, PASSES * T], U8, name="sscale", align_bytes=64)
         y = keep.tile([P, S], F32, name="y")
-        ys = keep.tile([P, T], F32, name="ys")
-        g1 = keep.tile([P, T], F32, name="g1")
-        g2 = keep.tile([P, T], F32, name="g2")
+        early = keep.tile([P, 4 * T], U32, name="early", align_bytes=64)
 
         ps_sa = psum.tile([P, BANK], F32, name="ps_sa")
         ps_sb = psum.tile([P, BANK], F32, name="ps_sb")
@@ -71,7 +69,7 @@ def tile_moe_shr_lin_relu2_kernel(tc, xT, w_words, w_scales, b, gate, offs, pos1
             return base + j * STEP
 
         def raw_start(a):
-            return base + ROW + TAIL if a == X else base + (a + 1) * STEP + (ROW + TAIL if a < 3 else 0)
+            return base + 4 * STEP if a == 3 else base + (a + 1) % PASSES * STEP + ROW + TAIL
 
         def raw(a, j, n):
             s = raw_start(a) + j * T
@@ -135,10 +133,11 @@ def tile_moe_shr_lin_relu2_kernel(tc, xT, w_words, w_scales, b, gate, offs, pos1
             nc.scalar.copy(out=quads(a, lo, n).rearrange("p (s u) -> p s u", u=2), in_=src)
 
         shared_order = (X, 2, 3, 0, 1)
-        shared_start = {X: 0, 2: 2 * T, 3: 2 * S, 0: 2 * S + 2 * T, 1: 6 * S}
+        shared_home = {X: (early, 0), 2: (early, 2 * T), 3: (picked, 0), 0: (picked, 6 * S), 1: (picked, 6 * S + 2 * T)}
 
-        def shared_quads(a):
-            return picked[:, shared_start[a]:shared_start[a] + 2 * T]
+        def shared_quads(a, lo=0, n=T):
+            tile, start = shared_home[a]
+            return tile[:, start + 2 * lo:start + 2 * (lo + n)]
 
         def shared_weave(a, copy):
             copy(out=shared_quads(a).rearrange("p (s u) -> p s u", u=2), in_=pairs(a, 0, 2 * T).rearrange("p (u s) -> p s u", u=2))
@@ -165,7 +164,8 @@ def tile_moe_shr_lin_relu2_kernel(tc, xT, w_words, w_scales, b, gate, offs, pos1
         late_loads()
 
         cast(0, 1, 0, H, nc.vector.tensor_copy)
-        cast(0, 1, H, T, nc.vector.tensor_copy)
+        cast(0, 1, H, H + 256, nc.vector.tensor_copy)
+        cast(0, 1, H + 256, T, nc.scalar.copy)
         plane(0, nc.scalar.copy)
         gather(0, 1, 0, WINDOW)
         scalar_gather(0)
@@ -184,7 +184,7 @@ def tile_moe_shr_lin_relu2_kernel(tc, xT, w_words, w_scales, b, gate, offs, pos1
         weave(1, 0, S)
         cast(2, 1, 0, T, pool_round)
         gather(2, 1, 0, WINDOW)
-        plane(3, pool_round)
+        plane(3, nc.scalar.copy)
         scalar_gather(3)
         cast(2, 0, 0, T, pool_round)
         gather(2, 0, 0, WINDOW)
@@ -195,10 +195,10 @@ def tile_moe_shr_lin_relu2_kernel(tc, xT, w_words, w_scales, b, gate, offs, pos1
         gather(3, 1, 0, WINDOW)
         cast(3, 0, 0, T, pool_round)
         gather(3, 0, 0, WINDOW)
-        shared_weave(0, nc.gpsimd.tensor_copy)
         shared_weave(2, nc.gpsimd.tensor_copy)
         shared_weave(3, nc.gpsimd.tensor_copy)
         weave(3, 0, S)
+        shared_weave(0, nc.scalar.copy)
         shared_weave(1, nc.scalar.copy)
 
         codes = keep.tile([P, PASSES * S], U32, name="codes", tag="late", align_bytes=64)
@@ -221,22 +221,23 @@ def tile_moe_shr_lin_relu2_kernel(tc, xT, w_words, w_scales, b, gate, offs, pos1
         nc.scalar.activation(out=y[:, S - BANK:], in_=y[:, S - BANK:], func=SQUARE)
 
         scodes = keep.tile([P, PASSES * T], U32, name="scodes", tag="arena", align_bytes=64)
-        runs = {0: ((0, 1024),), 1: ((256, 512),), 2: ((0, 1024),), 3: ((256, 512),), 4: ((0, 512), (512, 256))}
+        runs = {0: ((0, 1024),), 1: ((256, 512),), 2: ((0, 512), (512, 256)), 3: ((0, 1024),), 4: ((256, 512),)}
         for i, a in enumerate(shared_order):
             for lo, n in runs[i]:
-                s0 = shared_start[a] + 2 * lo
                 nc.vector.quantize_mx(out=scodes[:, i * T + lo:i * T + lo + n].bitcast(FP8), scales=sscale[:, i * T + lo:i * T + lo + n],
-                                      in_=picked[:, s0:s0 + 2 * n].bitcast(BF16))
+                                      in_=shared_quads(a, lo, n).bitcast(BF16))
             mm(ps_sa[:], E, a, scodes, sscale, i * T, BANK, i == 0, i == PASSES - 1)
             mm(ps_sb[:], E, a, scodes, sscale, i * T + T - BANK, BANK, i == 0, i == PASSES - 1)
 
+        sums = keep.tile([P, 3, T], F32, name="sums", tag="late", align_bytes=64)
+        ys, g1, g2 = sums[:, 0, :], sums[:, 1, :], sums[:, 2, :]
         halves = (slice(0, H), slice(H, T))
         nc.scalar.activation(out=ys[:, :H], in_=ps_sa[:, :H], func=RELU, bias=bias[:, E:E + 1])
         nc.scalar.activation(out=ys[:, H:], in_=ps_sb[:, 512 - H:], func=RELU, bias=bias[:, E:E + 1])
         for c in halves:
             nc.scalar.activation(out=ys[:, c], in_=ys[:, c], func=SQUARE)
 
-        nc.vector.tensor_tensor(g1[:], y[:].indirect(pos1_t[:]), gate_t[:, 0, :], MULT)
+        nc.vector.tensor_tensor(g1, y[:].indirect(pos1_t[:]), gate_t[:, 0, :], MULT)
         nc.vector.tensor_tensor(g2[:, :H], y[:].indirect(pos2_t[:, :H // 16]), gate_t[:, 1, :H], MULT)
         nc.vector.tensor_tensor(g2[:, H:], y[:].indirect(pos2_t[:, H // 16:]), gate_t[:, 1, H:], MULT)
         for c in halves:

@@ -86,16 +86,20 @@ def tile_moe_shr_lin_relu2_kernel(tc, xT, w_words, w_scales, b, gate, offs, pos1
         def load_cols(a, u, lo, hi):
             nc.sync.dma_start(out=raw(a, 2 * u, 2).rearrange("p (j t) -> p j t", j=2)[:, :, lo:hi], in_=xv[a][:, 2 * u:2 * u + 2, lo:hi])
 
+        order = (0, 1, 2, X, 3)
+
         def late_loads():
             nc.sync.dma_start(out=bias[:], in_=b)
-            wsv = w_scales.bitcast(I32).rearrange("e a q n -> q (e a) n")
-            for q in range(4):
-                nc.sync.dma_start(out=wsc[32 * q:32 * q + 4].rearrange("p a n -> p (a n)").bitcast(I32).rearrange("p (a n) -> p a n", n=N // 4),
-                                  in_=wsv[4 * q:4 * q + 4])
-            wv = w_words.bitcast(I32).rearrange("e a p n -> p (e a) n")
-            wd = wt[:].rearrange("p a n -> p (a n)").bitcast(I32).rearrange("p (a n) -> p a n", n=N // 2)
-            for lo, hi in ((0, 20), (20, 40), (40, 65)):
-                nc.sync.dma_start(out=wd[:, lo:hi, :], in_=wv[:, lo:hi, :])
+            rows = wsc[:].rearrange("p a n -> p (a n)").bitcast(I32)
+            nc.sync.dma_start(out=rows[0:16].rearrange("p (a n) -> p a n", n=N // 4), in_=w_scales.bitcast(I32).rearrange("e a q n -> q (e a) n"))
+            wv = w_words.bitcast(I32).rearrange("e a p n -> a p e n")
+            wd = wt[:].rearrange("p a n -> p (a n)").bitcast(I32).rearrange("p (a e n) -> p a e n", a=PASSES, n=N // 2)
+            for i, a in enumerate(order):
+                nc.sync.dma_start(out=wd[:, a, :E], in_=wv[a][:, :E])
+                if i == 1:
+                    for q in range(1, 4):
+                        nc.sync.dma_start(out=rows[32 * q:32 * q + 4], in_=rows[4 * q:4 * q + 4])
+            nc.sync.dma_start(out=wd[:, :, E], in_=w_words.bitcast(I32)[E].rearrange("a p n -> p a n"))
             nc.sync.dma_start(out=gate_t[:], in_=gate.rearrange("g p t -> p g t"))
             nc.sync.dma_start(pos1_t[:], pos1)
             nc.sync.dma_start(pos2_t[:], pos2)
@@ -143,7 +147,7 @@ def tile_moe_shr_lin_relu2_kernel(tc, xT, w_words, w_scales, b, gate, offs, pos1
             copy(out=shared_quads(a).rearrange("p (s u) -> p s u", u=2), in_=pairs(a, 0, 2 * T).rearrange("p (u s) -> p s u", u=2))
 
         def mm(dst, e, a, cd, cs, lo, n, start, stop):
-            nc.tensor.matmul_mx(out=dst, lhsT=wt[:, e * PASSES + a, :].bitcast(FP4), lhsT_scale=wsc[:, e * PASSES + a, :],
+            nc.tensor.matmul_mx(out=dst, lhsT=wt[:, a * (E + 1) + e, :].bitcast(FP4), lhsT_scale=wsc[:, e * PASSES + a, :],
                                 rhs=cd[:, lo:lo + n].bitcast(FP8), rhs_scale=cs[:, lo:lo + n], start=start, stop=stop)
 
         load_cols(0, 1, 0, H)
@@ -202,7 +206,6 @@ def tile_moe_shr_lin_relu2_kernel(tc, xT, w_words, w_scales, b, gate, offs, pos1
         shared_weave(1, nc.scalar.copy)
 
         codes = keep.tile([P, PASSES * S], U32, name="codes", tag="late", align_bytes=64)
-        order = (0, 1, 2, X, 3)
         for a in order:
             pieces = ((0, 2 * BANK), (2 * BANK, BANK)) if a != order[-1] else ((0, BANK), (BANK, BANK), (2 * BANK, BANK))
             for lo, n in pieces:

@@ -51,6 +51,7 @@ def tile_moe_shr_lin_relu2_kernel(tc, xT, w_words, w_scales, b, gate, offs, pos1
         cscale = keep.tile([P, PASSES * S], U8, name="cscale", align_bytes=64)
         sscale = keep.tile([P, PASSES * T], U8, name="sscale", align_bytes=64)
         y = keep.tile([P, S], F32, name="y")
+        last = keep.tile([P, 2 * BANK], U32, name="last", align_bytes=64)
         early = keep.tile([P, 4 * T], U32, name="early", align_bytes=64)
 
         ps_sa = psum.tile([P, BANK], F32, name="ps_sa")
@@ -129,6 +130,8 @@ def tile_moe_shr_lin_relu2_kernel(tc, xT, w_words, w_scales, b, gate, offs, pos1
                 nc.scalar.activation(v[:, lo:lo + T, j % 2], w.indirect(offs_t[:, lo // 16:(lo + T) // 16]), COPY)
 
         def quads(a, lo, n):
+            if (a, lo) == (3, 2 * BANK):
+                return last[:]
             s = raw_start(a) - (0 if a == 3 else TAIL)
             return arena[:, s + 2 * lo:s + 2 * (lo + n)]
 
@@ -137,14 +140,15 @@ def tile_moe_shr_lin_relu2_kernel(tc, xT, w_words, w_scales, b, gate, offs, pos1
             nc.scalar.copy(out=quads(a, lo, n).rearrange("p (s u) -> p s u", u=2), in_=src)
 
         shared_order = (X, 2, 3, 0, 1)
-        shared_home = {X: (early, 0), 2: (early, 2 * T), 3: (picked, 0), 0: (picked, 6 * S), 1: (picked, 6 * S + 2 * T)}
+        shared_home = {X: (early, 0), 2: (early, 2 * T), 3: (picked, 0), 0: (picked, 2 * T), 1: (picked, 6 * S)}
 
         def shared_quads(a, lo=0, n=T):
             tile, start = shared_home[a]
             return tile[:, start + 2 * lo:start + 2 * (lo + n)]
 
-        def shared_weave(a, copy):
-            copy(out=shared_quads(a).rearrange("p (s u) -> p s u", u=2), in_=pairs(a, 0, 2 * T).rearrange("p (u s) -> p s u", u=2))
+        def shared_weave(a, copy, lo=0, n=T, dtype=U32):
+            copy(out=shared_quads(a, lo, n).bitcast(dtype).rearrange("p (s u) -> p s u", u=2),
+                 in_=pairs(a, 0, 2 * T).bitcast(dtype).rearrange("p (u s) -> p s u", u=2)[:, lo:lo + n, :])
 
         def mm(dst, e, a, cd, cs, lo, n, start, stop):
             nc.tensor.matmul_mx(out=dst, lhsT=wt[:, a * (E + 1) + e, :].bitcast(FP4), lhsT_scale=wsc[:, e * PASSES + a, :],
@@ -199,14 +203,18 @@ def tile_moe_shr_lin_relu2_kernel(tc, xT, w_words, w_scales, b, gate, offs, pos1
         gather(3, 1, 0, WINDOW)
         cast(3, 0, 0, T, pool_round)
         gather(3, 0, 0, WINDOW)
+        shared_weave(0, nc.gpsimd.tensor_copy, 0, H)
         shared_weave(2, nc.gpsimd.tensor_copy)
         shared_weave(3, nc.gpsimd.tensor_copy)
-        weave(3, 0, S)
-        shared_weave(0, nc.scalar.copy)
-        shared_weave(1, nc.scalar.copy)
+        weave(3, 0, 2 * BANK)
+        weave(3, 2 * BANK, BANK)
+        shared_weave(0, nc.scalar.copy, H, H)
+        shared_weave(1, nc.scalar.copy, 0, H)
 
         codes = keep.tile([P, PASSES * S], U32, name="codes", tag="late", align_bytes=64)
         for a in order:
+            if a == order[-1]:
+                shared_weave(1, nc.vector.tensor_copy, H, H, I32)
             pieces = ((0, 2 * BANK), (2 * BANK, BANK)) if a != order[-1] else ((0, BANK), (BANK, BANK), (2 * BANK, BANK))
             for lo, n in pieces:
                 nc.vector.quantize_mx(out=codes[:, a * S + lo:a * S + lo + n].bitcast(FP8), scales=cscale[:, a * S + lo:a * S + lo + n],
@@ -224,7 +232,7 @@ def tile_moe_shr_lin_relu2_kernel(tc, xT, w_words, w_scales, b, gate, offs, pos1
         nc.scalar.activation(out=y[:, S - BANK:], in_=y[:, S - BANK:], func=SQUARE)
 
         scodes = keep.tile([P, PASSES * T], U32, name="scodes", tag="arena", align_bytes=64)
-        runs = {0: ((0, 1024),), 1: ((256, 512),), 2: ((0, 512), (512, 256)), 3: ((0, 1024),), 4: ((256, 512),)}
+        runs = {0: ((0, 1024),), 1: ((256, 512),), 2: ((0, 1024),), 3: ((256, 512),), 4: ((0, 512), (512, 256))}
         for i, a in enumerate(shared_order):
             for lo, n in runs[i]:
                 nc.vector.quantize_mx(out=scodes[:, i * T + lo:i * T + lo + n].bitcast(FP8), scales=sscale[:, i * T + lo:i * T + lo + n],

@@ -7,15 +7,18 @@ S = E * C
 P = 128
 PASSES = K // 512
 X = PASSES - 1
-WINDOW = 2048
 BANK = 512
 H = T // 2
-HEAD_TAIL = WINDOW - T
-ROW = T // 2
-RAW = 4 * T
-TAIL = 128
-STEP = ROW + TAIL + RAW
 FLOPS = 2 * K * N * (S + T)
+
+WINDOW = 2048
+ROW = T // 2
+TAIL = 128
+RAW = 4 * T
+STEP = ROW + TAIL + RAW
+HEAD = 448
+SPLIT = 416
+HEAD_TAIL = 704
 
 F32 = mybir.dt.float32
 BF16 = mybir.dt.bfloat16
@@ -46,13 +49,13 @@ def tile_moe_shr_lin_relu2_kernel(tc, xT, w_words, w_scales, b, gate, offs, pos1
         wsc = keep.tile([P, (E + 1) * PASSES, N], U8, name="wsc", align_bytes=64)
         base = 4 * T + HEAD_TAIL
         arena = keep.tile([P, base + 4 * STEP + RAW], U32, name="arena", tag="arena", align_bytes=64)
-        late = keep.tile([P, 3 * T + WINDOW], U32, name="late", tag="late", align_bytes=64)
+        pairs2 = keep.tile([P, T + WINDOW], U32, name="pairs2", tag="pairs2", align_bytes=64)
         picked = keep.tile([P, PASSES * 2 * S], U32, name="picked", align_bytes=64)
         cscale = keep.tile([P, PASSES * S], U8, name="cscale", align_bytes=64)
         sscale = keep.tile([P, PASSES * T], U8, name="sscale", align_bytes=64)
         y = keep.tile([P, S], F32, name="y")
-        last = keep.tile([P, 2 * BANK], U32, name="last", align_bytes=64)
-        early = keep.tile([P, 4 * T], U32, name="early", align_bytes=64)
+        last_quads = keep.tile([P, 2 * BANK], U32, name="last_quads", align_bytes=64)
+        own_quads = keep.tile([P, 4 * T], U32, name="own_quads", align_bytes=64)
 
         ps_sa = psum.tile([P, BANK], F32, name="ps_sa")
         ps_sb = psum.tile([P, BANK], F32, name="ps_sb")
@@ -61,12 +64,12 @@ def tile_moe_shr_lin_relu2_kernel(tc, xT, w_words, w_scales, b, gate, offs, pos1
         nc.vector.memset(arena[:, 4 * T:base], 0)
         for j in range(4):
             nc.scalar.copy(out=arena[:, base + j * STEP + ROW:base + j * STEP + ROW + TAIL], in_=arena[:, 4 * T:4 * T + TAIL])
-        nc.vector.memset(late[:, 4 * T:], 0)
+        nc.vector.memset(pairs2[:, 2 * T:], 0)
         nc.gpsimd.memset(wsc[:].rearrange("p a n -> p (a n)").bitcast(I32), 0)
 
         xv = xT.rearrange("(a p j) t -> a p j t", a=PASSES, j=4)
 
-        def plane_start(j):
+        def row_start(j):
             return base + j * STEP
 
         def raw_start(a):
@@ -77,9 +80,8 @@ def tile_moe_shr_lin_relu2_kernel(tc, xT, w_words, w_scales, b, gate, offs, pos1
             return arena[:, s:s + n * T].bitcast(F32)
 
         def pairs(a, u, n):
-            tile = arena if a < 2 else late
-            s = (1 - a % 2) * 2 * T + u * T
-            return tile[:, s:s + n]
+            tile, s = ((arena, 2 * T), (arena, 0), (pairs2, 0), (picked, 0))[a]
+            return tile[:, s + u * T:s + u * T + n]
 
         def load_rows(a, j, n):
             nc.sync.dma_start(out=raw(a, j, n).rearrange("p (j t) -> p j t", j=n), in_=xv[a][:, j:j + n, :])
@@ -91,15 +93,15 @@ def tile_moe_shr_lin_relu2_kernel(tc, xT, w_words, w_scales, b, gate, offs, pos1
 
         def late_loads():
             nc.sync.dma_start(out=bias[:], in_=b)
-            rows = wsc[:].rearrange("p a n -> p (a n)").bitcast(I32)
-            nc.sync.dma_start(out=rows[0:16].rearrange("p (a n) -> p a n", n=N // 4), in_=w_scales.bitcast(I32).rearrange("e a q n -> q (e a) n"))
+            scale_rows = wsc[:].rearrange("p a n -> p (a n)").bitcast(I32)
+            nc.sync.dma_start(out=scale_rows[0:16].rearrange("p (a n) -> p a n", n=N // 4), in_=w_scales.bitcast(I32).rearrange("e a q n -> q (e a) n"))
             wv = w_words.bitcast(I32).rearrange("e a p n -> a p e n")
             wd = wt[:].rearrange("p a n -> p (a n)").bitcast(I32).rearrange("p (a e n) -> p a e n", a=PASSES, n=N // 2)
             for i, a in enumerate(order):
                 nc.sync.dma_start(out=wd[:, a, :E], in_=wv[a][:, :E])
                 if i == 1:
                     for q in range(1, 4):
-                        nc.sync.dma_start(out=rows[32 * q:32 * q + 4], in_=rows[4 * q:4 * q + 4])
+                        nc.sync.dma_start(out=scale_rows[32 * q:32 * q + 4], in_=scale_rows[4 * q:4 * q + 4])
             nc.sync.dma_start(out=wd[:, :, E], in_=w_words.bitcast(I32)[E].rearrange("a p n -> p a n"))
             nc.sync.dma_start(out=gate_t[:], in_=gate.rearrange("g p t -> p g t"))
             nc.sync.dma_start(pos1_t[:], pos1)
@@ -108,13 +110,13 @@ def tile_moe_shr_lin_relu2_kernel(tc, xT, w_words, w_scales, b, gate, offs, pos1
         def pool_round(dst, src):
             nc.gpsimd.tensor_scalar(out=dst, in0=src, scalar1=1.0, scalar2=0.0, op0=MULT, op1=ADD)
 
-        def cast(a, u, lo, hi, rnd):
+        def round_pairs(a, u, lo, hi, rnd):
             d = pairs(a, u, T).bitcast(BF16).rearrange("p (t j) -> p t j", j=2)
             s = raw(a, 2 * u, 2).rearrange("p (j t) -> p t j", j=2)
             rnd(d[:, lo:hi, :], s[:, lo:hi, :])
 
-        def plane(j, rnd):
-            rnd(arena[:, plane_start(j):plane_start(j) + ROW].bitcast(BF16), raw(X, j, 1))
+        def round_row(j, rnd):
+            rnd(arena[:, row_start(j):row_start(j) + ROW].bitcast(BF16), raw(X, j, 1))
 
         def picks(a, u, lo, n):
             s = (2 * a + u) * S + lo
@@ -123,15 +125,19 @@ def tile_moe_shr_lin_relu2_kernel(tc, xT, w_words, w_scales, b, gate, offs, pos1
         def gather(a, u, lo, window):
             nc.vector.tensor_copy(picks(a, u, lo, S - lo), pairs(a, u, window).indirect(offs_t[:, lo // 16:]))
 
+        def head_gather(j):
+            v = picks(0, 1, 0, HEAD).bitcast(BF16).rearrange("p (s j) -> p s j", j=2)
+            nc.vector.tensor_copy(v[:, :, j], raw(0, 2 + j, 1).indirect(offs_t[:, :HEAD // 16]))
+
         def scalar_gather(j):
             v = picks(X, j // 2, 0, S).bitcast(BF16).rearrange("p (s j) -> p s j", j=2)
-            w = arena[:, plane_start(j):plane_start(j) + ROW + TAIL].bitcast(BF16)
+            w = arena[:, row_start(j):row_start(j) + ROW + TAIL].bitcast(BF16)
             for lo in (0, T):
                 nc.scalar.activation(v[:, lo:lo + T, j % 2], w.indirect(offs_t[:, lo // 16:(lo + T) // 16]), COPY)
 
         def quads(a, lo, n):
             if (a, lo) == (3, 2 * BANK):
-                return last[:]
+                return last_quads[:]
             s = raw_start(a) - (0 if a == 3 else TAIL)
             return arena[:, s + 2 * lo:s + 2 * (lo + n)]
 
@@ -140,23 +146,23 @@ def tile_moe_shr_lin_relu2_kernel(tc, xT, w_words, w_scales, b, gate, offs, pos1
             nc.scalar.copy(out=quads(a, lo, n).rearrange("p (s u) -> p s u", u=2), in_=src)
 
         shared_order = (X, 2, 3, 0, 1)
-        shared_home = {X: (early, 0), 2: (early, 2 * T), 3: (picked, 0), 0: (picked, 2 * T), 1: (picked, 6 * S)}
+        shared_home = {X: (own_quads, 0), 2: (own_quads, 2 * T), 3: (picked, 2 * S), 0: (picked, 2 * S + 2 * T), 1: (picked, 6 * S)}
 
         def shared_quads(a, lo=0, n=T):
             tile, start = shared_home[a]
             return tile[:, start + 2 * lo:start + 2 * (lo + n)]
 
-        def shared_weave(a, copy, lo=0, n=T, dtype=U32):
-            copy(out=shared_quads(a, lo, n).bitcast(dtype).rearrange("p (s u) -> p s u", u=2),
-                 in_=pairs(a, 0, 2 * T).bitcast(dtype).rearrange("p (u s) -> p s u", u=2)[:, lo:lo + n, :])
+        def shared_weave(a, copy, lo=0, n=T):
+            copy(out=shared_quads(a, lo, n).rearrange("p (s u) -> p s u", u=2),
+                 in_=pairs(a, 0, 2 * T).rearrange("p (u s) -> p s u", u=2)[:, lo:lo + n, :])
 
         def mm(dst, e, a, cd, cs, lo, n, start, stop):
             nc.tensor.matmul_mx(out=dst, lhsT=wt[:, a * (E + 1) + e, :].bitcast(FP4), lhsT_scale=wsc[:, e * PASSES + a, :],
                                 rhs=cd[:, lo:lo + n].bitcast(FP8), rhs_scale=cs[:, lo:lo + n], start=start, stop=stop)
 
-        load_cols(0, 1, 0, H)
+        load_rows(0, 2, 1)
         nc.sync.dma_start(offs_t[:], offs)
-        load_cols(0, 1, H, T)
+        load_rows(0, 3, 1)
         load_rows(X, 0, 1)
         load_cols(0, 0, 0, H)
         load_cols(0, 0, H, T)
@@ -171,50 +177,49 @@ def tile_moe_shr_lin_relu2_kernel(tc, xT, w_words, w_scales, b, gate, offs, pos1
         load_rows(3, 0, 2)
         late_loads()
 
-        cast(0, 1, 0, H, nc.vector.tensor_copy)
-        cast(0, 1, H, H + 256, nc.vector.tensor_copy)
-        cast(0, 1, H + 256, T, nc.scalar.copy)
-        plane(0, nc.scalar.copy)
-        gather(0, 1, 0, WINDOW)
+        head_gather(0)
+        head_gather(1)
+        round_pairs(0, 1, 0, SPLIT, nc.scalar.copy)
+        round_pairs(0, 1, SPLIT, T, pool_round)
+        round_row(0, nc.scalar.copy)
+        gather(0, 1, HEAD, T + HEAD_TAIL)
         scalar_gather(0)
-        cast(0, 0, 0, H, pool_round)
-        cast(0, 0, H, T, pool_round)
+        round_pairs(0, 0, 0, H, pool_round)
+        round_pairs(0, 0, H, T, pool_round)
         gather(0, 0, 0, WINDOW)
-        plane(1, pool_round)
+        round_row(1, pool_round)
         scalar_gather(1)
         weave(0, 0, S)
-        cast(1, 1, 0, T, pool_round)
+        round_pairs(1, 1, 0, T, pool_round)
         gather(1, 1, 0, WINDOW)
-        plane(2, pool_round)
+        round_row(2, pool_round)
         scalar_gather(2)
-        cast(1, 0, 0, T, pool_round)
+        round_pairs(1, 0, 0, T, pool_round)
         gather(1, 0, 0, WINDOW)
         weave(1, 0, S)
-        cast(2, 1, 0, T, pool_round)
+        round_pairs(2, 1, 0, T, pool_round)
         gather(2, 1, 0, WINDOW)
-        plane(3, nc.scalar.copy)
+        round_row(3, nc.scalar.copy)
         scalar_gather(3)
-        cast(2, 0, 0, T, pool_round)
+        round_pairs(2, 0, 0, T, pool_round)
         gather(2, 0, 0, WINDOW)
         weave(2, 0, S)
         pool_round(shared_quads(X).bitcast(BF16).rearrange("p (t j) -> p t j", j=4), raw(X, 0, 4).rearrange("p (j t) -> p t j", j=4))
         weave(X, 0, S)
-        cast(3, 1, 0, T, pool_round)
+        round_pairs(3, 1, 0, T, pool_round)
         gather(3, 1, 0, WINDOW)
-        cast(3, 0, 0, T, pool_round)
+        round_pairs(3, 0, 0, T, pool_round)
         gather(3, 0, 0, WINDOW)
         shared_weave(0, nc.gpsimd.tensor_copy, 0, H)
-        shared_weave(2, nc.gpsimd.tensor_copy)
         shared_weave(3, nc.gpsimd.tensor_copy)
+        shared_weave(2, nc.gpsimd.tensor_copy)
         weave(3, 0, 2 * BANK)
         weave(3, 2 * BANK, BANK)
         shared_weave(0, nc.scalar.copy, H, H)
-        shared_weave(1, nc.scalar.copy, 0, H)
+        shared_weave(1, nc.scalar.copy)
 
-        codes = keep.tile([P, PASSES * S], U32, name="codes", tag="late", align_bytes=64)
+        codes = keep.tile([P, PASSES * S], U32, name="codes", tag="pairs2", align_bytes=64)
         for a in order:
-            if a == order[-1]:
-                shared_weave(1, nc.vector.tensor_copy, H, H, I32)
             pieces = ((0, 2 * BANK), (2 * BANK, BANK)) if a != order[-1] else ((0, BANK), (BANK, BANK), (2 * BANK, BANK))
             for lo, n in pieces:
                 nc.vector.quantize_mx(out=codes[:, a * S + lo:a * S + lo + n].bitcast(FP8), scales=cscale[:, a * S + lo:a * S + lo + n],
@@ -232,7 +237,7 @@ def tile_moe_shr_lin_relu2_kernel(tc, xT, w_words, w_scales, b, gate, offs, pos1
         nc.scalar.activation(out=y[:, S - BANK:], in_=y[:, S - BANK:], func=SQUARE)
 
         scodes = keep.tile([P, PASSES * T], U32, name="scodes", tag="arena", align_bytes=64)
-        runs = {0: ((0, 1024),), 1: ((256, 512),), 2: ((0, 1024),), 3: ((256, 512),), 4: ((0, 512), (512, 256))}
+        runs = (((0, 1024),), ((1024 - T, 512),)) * 2 + (((0, 512), (512, T - 512)),)
         for i, a in enumerate(shared_order):
             for lo, n in runs[i]:
                 nc.vector.quantize_mx(out=scodes[:, i * T + lo:i * T + lo + n].bitcast(FP8), scales=sscale[:, i * T + lo:i * T + lo + n],
@@ -240,11 +245,11 @@ def tile_moe_shr_lin_relu2_kernel(tc, xT, w_words, w_scales, b, gate, offs, pos1
             mm(ps_sa[:], E, a, scodes, sscale, i * T, BANK, i == 0, i == PASSES - 1)
             mm(ps_sb[:], E, a, scodes, sscale, i * T + T - BANK, BANK, i == 0, i == PASSES - 1)
 
-        sums = keep.tile([P, 3, T], F32, name="sums", tag="late", align_bytes=64)
+        sums = keep.tile([P, 3, T], F32, name="sums", tag="pairs2", align_bytes=64)
         ys, g1, g2 = sums[:, 0, :], sums[:, 1, :], sums[:, 2, :]
         halves = (slice(0, H), slice(H, T))
         nc.scalar.activation(out=ys[:, :H], in_=ps_sa[:, :H], func=RELU, bias=bias[:, E:E + 1])
-        nc.scalar.activation(out=ys[:, H:], in_=ps_sb[:, 512 - H:], func=RELU, bias=bias[:, E:E + 1])
+        nc.scalar.activation(out=ys[:, H:], in_=ps_sb[:, BANK - H:], func=RELU, bias=bias[:, E:E + 1])
         for c in halves:
             nc.scalar.activation(out=ys[:, c], in_=ys[:, c], func=SQUARE)
 

@@ -9,6 +9,8 @@ PASSES = K // 512
 X = PASSES - 1
 BANK = 512
 H = T // 2
+LAST = S - BANK // 2
+GROUPS = ((0, BANK), (BANK, BANK), (2 * BANK, BANK // 2), (LAST, BANK // 2))
 FLOPS = 2 * K * N * (S + T)
 
 WINDOW = 2048
@@ -53,13 +55,13 @@ def tile_moe_shr_lin_relu2_kernel(tc, xT, w_words, w_scales, b, gate, offs, pos1
         picked = keep.tile([P, PASSES * 2 * S], U32, name="picked", align_bytes=64)
         cscale = keep.tile([P, PASSES * S], U8, name="cscale", align_bytes=64)
         sscale = keep.tile([P, PASSES * T], U8, name="sscale", align_bytes=64)
-        y = keep.tile([P, S], F32, name="y")
-        last_quads = keep.tile([P, 2 * BANK], U32, name="last_quads", align_bytes=64)
+        y = keep.tile([P, S], F32, name="y", tag="y")
+        last_quads = keep.tile([P, BANK], U32, name="last_quads", align_bytes=64)
         own_quads = keep.tile([P, 4 * T], U32, name="own_quads", align_bytes=64)
 
         ps_sa = psum.tile([P, BANK], F32, name="ps_sa")
         ps_sb = psum.tile([P, BANK], F32, name="ps_sb")
-        ps = [psum.tile([P, BANK], F32, name="ps%d" % i) for i in range(S // BANK)]
+        ps = [psum.tile([P, n], F32, name="ps%d" % i) for i, (lo, n) in enumerate(GROUPS)]
 
         nc.vector.memset(arena[:, 4 * T:base], 0)
         for j in range(4):
@@ -136,8 +138,11 @@ def tile_moe_shr_lin_relu2_kernel(tc, xT, w_words, w_scales, b, gate, offs, pos1
                 nc.scalar.activation(v[:, lo:lo + T, j % 2], w.indirect(offs_t[:, lo // 16:(lo + T) // 16]), COPY)
 
         def quads(a, lo, n):
-            if (a, lo) == (3, 2 * BANK):
+            if (a, lo) == (3, LAST):
                 return last_quads[:]
+            if a in (2, X) and lo == 2 * BANK:
+                s = (6 if a == 2 else 7) * S
+                return picked[:, s:s + 2 * n]
             s = raw_start(a) - (0 if a == 3 else TAIL)
             return arena[:, s + 2 * lo:s + 2 * (lo + n)]
 
@@ -146,7 +151,7 @@ def tile_moe_shr_lin_relu2_kernel(tc, xT, w_words, w_scales, b, gate, offs, pos1
             nc.scalar.copy(out=quads(a, lo, n).rearrange("p (s u) -> p s u", u=2), in_=src)
 
         shared_order = (X, 2, 3, 0, 1)
-        shared_home = {X: (own_quads, 0), 2: (own_quads, 2 * T), 3: (picked, 2 * S), 0: (picked, 2 * S + 2 * T), 1: (picked, 6 * S)}
+        shared_home = {X: (own_quads, 0), 2: (own_quads, 2 * T), 3: (picked, 2 * S), 0: (picked, 2 * S + 2 * T), 1: (picked, 8 * S)}
 
         def shared_quads(a, lo=0, n=T):
             tile, start = shared_home[a]
@@ -199,42 +204,56 @@ def tile_moe_shr_lin_relu2_kernel(tc, xT, w_words, w_scales, b, gate, offs, pos1
         weave(1, 0, S)
         round_pairs(2, 1, 0, T, pool_round)
         gather(2, 1, 0, WINDOW)
-        round_row(3, nc.scalar.copy)
+        round_row(3, pool_round)
         scalar_gather(3)
         round_pairs(2, 0, 0, T, pool_round)
         gather(2, 0, 0, WINDOW)
-        weave(2, 0, S)
+        weave(2, 0, 2 * BANK)
         pool_round(shared_quads(X).bitcast(BF16).rearrange("p (t j) -> p t j", j=4), raw(X, 0, 4).rearrange("p (j t) -> p t j", j=4))
-        weave(X, 0, S)
+        weave(X, 0, 2 * BANK)
         round_pairs(3, 1, 0, T, pool_round)
         gather(3, 1, 0, WINDOW)
         round_pairs(3, 0, 0, T, pool_round)
         gather(3, 0, 0, WINDOW)
-        shared_weave(0, nc.gpsimd.tensor_copy, 0, H)
+        shared_weave(0, nc.gpsimd.tensor_copy)
         shared_weave(3, nc.gpsimd.tensor_copy)
         shared_weave(2, nc.gpsimd.tensor_copy)
         weave(3, 0, 2 * BANK)
-        weave(3, 2 * BANK, BANK)
-        shared_weave(0, nc.scalar.copy, H, H)
+        weave(2, 2 * BANK, BANK)
+        weave(X, 2 * BANK, BANK)
+        for lo, n in GROUPS[2:]:
+            weave(3, lo, n)
         shared_weave(1, nc.scalar.copy)
 
         codes = keep.tile([P, PASSES * S], U32, name="codes", tag="pairs2", align_bytes=64)
-        for a in order:
-            pieces = ((0, 2 * BANK), (2 * BANK, BANK)) if a != order[-1] else ((0, BANK), (BANK, BANK), (2 * BANK, BANK))
-            for lo, n in pieces:
-                nc.vector.quantize_mx(out=codes[:, a * S + lo:a * S + lo + n].bitcast(FP8), scales=cscale[:, a * S + lo:a * S + lo + n],
-                                      in_=quads(a, lo, n).bitcast(BF16))
-                for s0 in range(lo, lo + n, C):
-                    c0 = s0 % BANK
-                    mm(ps[s0 // BANK][:, c0:c0 + C], s0 // C, a, codes, cscale, a * S + s0, C,
-                       a == order[0] and c0 == 0, a == order[-1] and c0 + C == BANK)
-        for lo in range(0, S, BANK):
-            for c0 in range(0, BANK, C):
+        def routed(a, lo, n):
+            nc.vector.quantize_mx(out=codes[:, a * S + lo:a * S + lo + n].bitcast(FP8), scales=cscale[:, a * S + lo:a * S + lo + n],
+                                  in_=quads(a, lo, n).bitcast(BF16))
+            for s0 in range(lo, lo + n, C):
+                g = max(i for i in range(len(GROUPS)) if GROUPS[i][0] <= s0)
+                c0 = s0 - GROUPS[g][0]
+                mm(ps[g][:, c0:c0 + C], s0 // C, a, codes, cscale, a * S + s0, C,
+                   a == order[0] and c0 == 0, a == order[-1] and c0 + C == GROUPS[g][1])
+
+        for a in order[:2]:
+            routed(a, 0, 2 * BANK)
+            routed(a, 2 * BANK, BANK)
+        for a in order[2:-1]:
+            routed(a, 0, 2 * BANK)
+        for lo, n in GROUPS[:2]:
+            routed(order[-1], lo, n)
+        for a in order[2:-1]:
+            routed(a, 2 * BANK, BANK)
+        for lo, n in GROUPS[2:]:
+            routed(order[-1], lo, n)
+        for g, (lo, n) in enumerate(GROUPS):
+            for c0 in range(0, n, C):
                 e = (lo + c0) // C
-                nc.scalar.activation(out=y[:, lo + c0:lo + c0 + C], in_=ps[lo // BANK][:, c0:c0 + C], func=RELU, bias=bias[:, e:e + 1])
-            if lo > 0:
-                nc.scalar.activation(out=y[:, lo - BANK:lo], in_=y[:, lo - BANK:lo], func=SQUARE)
-        nc.scalar.activation(out=y[:, S - BANK:], in_=y[:, S - BANK:], func=SQUARE)
+                nc.scalar.activation(out=y[:, lo + c0:lo + c0 + C], in_=ps[g][:, c0:c0 + C], func=RELU, bias=bias[:, e:e + 1])
+            if n == BANK:
+                nc.scalar.activation(out=y[:, lo:lo + n], in_=y[:, lo:lo + n], func=SQUARE)
+        for lo, n in GROUPS[2:]:
+            nc.scalar.activation(out=y[:, lo:lo + n], in_=y[:, lo:lo + n], func=SQUARE)
 
         scodes = keep.tile([P, PASSES * T], U32, name="scodes", tag="arena", align_bytes=64)
         runs = (((0, 1024),), ((1024 - T, 512),)) * 2 + (((0, 512), (512, T - 512)),)
@@ -245,17 +264,20 @@ def tile_moe_shr_lin_relu2_kernel(tc, xT, w_words, w_scales, b, gate, offs, pos1
             mm(ps_sa[:], E, a, scodes, sscale, i * T, BANK, i == 0, i == PASSES - 1)
             mm(ps_sb[:], E, a, scodes, sscale, i * T + T - BANK, BANK, i == 0, i == PASSES - 1)
 
-        sums = keep.tile([P, 3, T], F32, name="sums", tag="pairs2", align_bytes=64)
-        ys, g1, g2 = sums[:, 0, :], sums[:, 1, :], sums[:, 2, :]
+        sums = keep.tile([P, 2, T], F32, name="sums", tag="pairs2", align_bytes=64)
+        g1, g2 = sums[:, 0, :], sums[:, 1, :]
         halves = (slice(0, H), slice(H, T))
+        nc.scalar.activation(g1, y[:].indirect(pos1_t[:]), COPY)
+        nc.scalar.activation(g2, y[:].indirect(pos2_t[:]), COPY)
+        ys = keep.tile([P, T], F32, name="ys", tag="y")
         nc.scalar.activation(out=ys[:, :H], in_=ps_sa[:, :H], func=RELU, bias=bias[:, E:E + 1])
         nc.scalar.activation(out=ys[:, H:], in_=ps_sb[:, BANK - H:], func=RELU, bias=bias[:, E:E + 1])
         for c in halves:
             nc.scalar.activation(out=ys[:, c], in_=ys[:, c], func=SQUARE)
 
-        nc.vector.tensor_tensor(g1, y[:].indirect(pos1_t[:]), gate_t[:, 0, :], MULT)
-        nc.vector.tensor_tensor(g2[:, :H], y[:].indirect(pos2_t[:, :H // 16]), gate_t[:, 1, :H], MULT)
-        nc.vector.tensor_tensor(g2[:, H:], y[:].indirect(pos2_t[:, H // 16:]), gate_t[:, 1, H:], MULT)
+        nc.vector.tensor_tensor(g1, g1, gate_t[:, 0, :], MULT)
+        for c in halves:
+            nc.vector.tensor_tensor(g2[:, c], g2[:, c], gate_t[:, 1, c], MULT)
         for c in halves:
             nc.vector.tensor_tensor(g1[:, c], g1[:, c], g2[:, c], ADD)
         for c in halves:

@@ -204,7 +204,7 @@ def tile_moe_shr_lin_relu2_kernel(tc, xT, w_words, w_scales, b, gate, offs, pos1
         weave(1, 0, S)
         round_pairs(2, 1, 0, T, pool_round)
         gather(2, 1, 0, WINDOW)
-        round_row(3, pool_round)
+        round_row(3, nc.scalar.copy)
         scalar_gather(3)
         round_pairs(2, 0, 0, T, pool_round)
         gather(2, 0, 0, WINDOW)
@@ -215,7 +215,7 @@ def tile_moe_shr_lin_relu2_kernel(tc, xT, w_words, w_scales, b, gate, offs, pos1
         gather(3, 1, 0, WINDOW)
         round_pairs(3, 0, 0, T, pool_round)
         gather(3, 0, 0, WINDOW)
-        shared_weave(0, nc.gpsimd.tensor_copy)
+        shared_weave(0, nc.gpsimd.tensor_copy, 0, H)
         shared_weave(3, nc.gpsimd.tensor_copy)
         shared_weave(2, nc.gpsimd.tensor_copy)
         weave(3, 0, 2 * BANK)
@@ -223,6 +223,7 @@ def tile_moe_shr_lin_relu2_kernel(tc, xT, w_words, w_scales, b, gate, offs, pos1
         weave(X, 2 * BANK, BANK)
         for lo, n in GROUPS[2:]:
             weave(3, lo, n)
+        shared_weave(0, nc.scalar.copy, H, H)
         shared_weave(1, nc.scalar.copy)
 
         codes = keep.tile([P, PASSES * S], U32, name="codes", tag="pairs2", align_bytes=64)

@@ -140,9 +140,8 @@ def tile_moe_shr_lin_relu2_kernel(tc, xT, w_words, w_scales, b, gate, offs, pos1
         def quads(a, lo, n):
             if (a, lo) == (3, LAST):
                 return last_quads[:]
-            if a in (2, X) and lo == 2 * BANK:
-                s = (6 if a == 2 else 7) * S
-                return picked[:, s:s + 2 * n]
+            if (a, lo) == (X, 2 * BANK):
+                return picked[:, 6 * S:6 * S + 2 * n]
             s = raw_start(a) - (0 if a == 3 else TAIL)
             return arena[:, s + 2 * lo:s + 2 * (lo + n)]
 
@@ -208,7 +207,7 @@ def tile_moe_shr_lin_relu2_kernel(tc, xT, w_words, w_scales, b, gate, offs, pos1
         scalar_gather(3)
         round_pairs(2, 0, 0, T, pool_round)
         gather(2, 0, 0, WINDOW)
-        weave(2, 0, 2 * BANK)
+        weave(2, 0, S)
         pool_round(shared_quads(X).bitcast(BF16).rearrange("p (t j) -> p t j", j=4), raw(X, 0, 4).rearrange("p (j t) -> p t j", j=4))
         weave(X, 0, 2 * BANK)
         round_pairs(3, 1, 0, T, pool_round)
@@ -219,7 +218,6 @@ def tile_moe_shr_lin_relu2_kernel(tc, xT, w_words, w_scales, b, gate, offs, pos1
         shared_weave(3, nc.gpsimd.tensor_copy)
         shared_weave(2, nc.gpsimd.tensor_copy)
         weave(3, 0, 2 * BANK)
-        weave(2, 2 * BANK, BANK)
         weave(X, 2 * BANK, BANK)
         for lo, n in GROUPS[2:]:
             weave(3, lo, n)
@@ -236,15 +234,13 @@ def tile_moe_shr_lin_relu2_kernel(tc, xT, w_words, w_scales, b, gate, offs, pos1
                 mm(ps[g][:, c0:c0 + C], s0 // C, a, codes, cscale, a * S + s0, C,
                    a == order[0] and c0 == 0, a == order[-1] and c0 + C == GROUPS[g][1])
 
-        for a in order[:2]:
+        for a in order[:3]:
             routed(a, 0, 2 * BANK)
             routed(a, 2 * BANK, BANK)
-        for a in order[2:-1]:
-            routed(a, 0, 2 * BANK)
+        routed(X, 0, 2 * BANK)
         for lo, n in GROUPS[:2]:
             routed(order[-1], lo, n)
-        for a in order[2:-1]:
-            routed(a, 2 * BANK, BANK)
+        routed(X, 2 * BANK, BANK)
         for lo, n in GROUPS[2:]:
             routed(order[-1], lo, n)
         for g, (lo, n) in enumerate(GROUPS):

@@ -55,7 +55,8 @@ def tile_moe_shr_lin_relu2_kernel(tc, xT, w_words, w_scales, b, gate, offs, pos1
         picked = keep.tile([P, PASSES * 2 * S], U32, name="picked", align_bytes=64)
         cscale = keep.tile([P, PASSES * S], U8, name="cscale", align_bytes=64)
         sscale = keep.tile([P, PASSES * T], U8, name="sscale", align_bytes=64)
-        y = keep.tile([P, S], F32, name="y", tag="y")
+        y = keep.tile([P, S], F32, name="y")
+        ys = keep.tile([P, T], F32, name="ys")
         last_quads = keep.tile([P, BANK], U32, name="last_quads", align_bytes=64)
         own_quads = keep.tile([P, 4 * T], U32, name="own_quads", align_bytes=64)
 
@@ -244,13 +245,14 @@ def tile_moe_shr_lin_relu2_kernel(tc, xT, w_words, w_scales, b, gate, offs, pos1
         for lo, n in GROUPS[2:]:
             routed(order[-1], lo, n)
         for g, (lo, n) in enumerate(GROUPS):
+            r = y[:, lo:lo + n] if n == BANK else ys[:, lo - 2 * BANK:lo - 2 * BANK + n]
             for c0 in range(0, n, C):
                 e = (lo + c0) // C
-                nc.scalar.activation(out=y[:, lo + c0:lo + c0 + C], in_=ps[g][:, c0:c0 + C], func=RELU, bias=bias[:, e:e + 1])
+                nc.scalar.activation(out=r[:, c0:c0 + C], in_=ps[g][:, c0:c0 + C], func=RELU, bias=bias[:, e:e + 1])
             if n == BANK:
-                nc.scalar.activation(out=y[:, lo:lo + n], in_=y[:, lo:lo + n], func=SQUARE)
+                nc.scalar.activation(out=r, in_=r, func=SQUARE)
         for lo, n in GROUPS[2:]:
-            nc.scalar.activation(out=y[:, lo:lo + n], in_=y[:, lo:lo + n], func=SQUARE)
+            nc.scalar.activation(out=y[:, lo:lo + n], in_=ys[:, lo - 2 * BANK:lo - 2 * BANK + n], func=SQUARE)
 
         scodes = keep.tile([P, PASSES * T], U32, name="scodes", tag="arena", align_bytes=64)
         runs = (((0, 1024),), ((1024 - T, 512),)) * 2 + (((0, 512), (512, T - 512)),)
@@ -264,15 +266,13 @@ def tile_moe_shr_lin_relu2_kernel(tc, xT, w_words, w_scales, b, gate, offs, pos1
         sums = keep.tile([P, 2, T], F32, name="sums", tag="pairs2", align_bytes=64)
         g1, g2 = sums[:, 0, :], sums[:, 1, :]
         halves = (slice(0, H), slice(H, T))
-        nc.scalar.activation(g1, y[:].indirect(pos1_t[:]), COPY)
         nc.scalar.activation(g2, y[:].indirect(pos2_t[:]), COPY)
-        ys = keep.tile([P, T], F32, name="ys", tag="y")
+        nc.vector.tensor_tensor(g1, y[:].indirect(pos1_t[:]), gate_t[:, 0, :], MULT)
         nc.scalar.activation(out=ys[:, :H], in_=ps_sa[:, :H], func=RELU, bias=bias[:, E:E + 1])
         nc.scalar.activation(out=ys[:, H:], in_=ps_sb[:, BANK - H:], func=RELU, bias=bias[:, E:E + 1])
         for c in halves:
             nc.scalar.activation(out=ys[:, c], in_=ys[:, c], func=SQUARE)
 
-        nc.vector.tensor_tensor(g1, g1, gate_t[:, 0, :], MULT)
         for c in halves:
             nc.vector.tensor_tensor(g2[:, c], g2[:, c], gate_t[:, 1, c], MULT)
         for c in halves:

@@ -20,6 +20,7 @@ RAW = 4 * T
 STEP = ROW + TAIL + RAW
 HEAD = 448
 SPLIT = 416
+EXTRA = 256
 HEAD_TAIL = 704
 
 F32 = mybir.dt.float32
@@ -267,14 +268,16 @@ def tile_moe_shr_lin_relu2_kernel(tc, xT, w_words, w_scales, b, gate, offs, pos1
         g1, g2 = sums[:, 0, :], sums[:, 1, :]
         halves = (slice(0, H), slice(H, T))
         nc.scalar.activation(g2, y[:].indirect(pos2_t[:]), COPY)
-        nc.vector.tensor_tensor(g1, y[:].indirect(pos1_t[:]), gate_t[:, 0, :], MULT)
+        nc.scalar.activation(g1[:, :EXTRA], y[:].indirect(pos1_t[:, :EXTRA // 16]), COPY)
+        nc.vector.tensor_tensor(g1[:, EXTRA:], y[:].indirect(pos1_t[:, EXTRA // 16:]), gate_t[:, 0, EXTRA:], MULT)
         nc.scalar.activation(out=ys[:, :H], in_=ps_sa[:, :H], func=RELU, bias=bias[:, E:E + 1])
         nc.scalar.activation(out=ys[:, H:], in_=ps_sb[:, BANK - H:], func=RELU, bias=bias[:, E:E + 1])
         for c in halves:
             nc.scalar.activation(out=ys[:, c], in_=ys[:, c], func=SQUARE)
 
-        for c in halves:
-            nc.vector.tensor_tensor(g2[:, c], g2[:, c], gate_t[:, 1, c], MULT)
+        nc.vector.tensor_tensor(g2[:, :H], g2[:, :H], gate_t[:, 1, :H], MULT)
+        nc.vector.tensor_tensor(g1[:, :EXTRA], g1[:, :EXTRA], gate_t[:, 0, :EXTRA], MULT)
+        nc.vector.tensor_tensor(g2[:, H:], g2[:, H:], gate_t[:, 1, H:], MULT)
         for c in halves:
             nc.vector.tensor_tensor(g1[:, c], g1[:, c], g2[:, c], ADD)
         for c in halves:

@@ -9,18 +9,19 @@ PASSES = K // 512
 X = PASSES - 1
 BANK = 512
 H = T // 2
-LAST = S - BANK // 2
-GROUPS = ((0, BANK), (BANK, BANK), (2 * BANK, BANK // 2), (LAST, BANK // 2))
+LAST = S - 2 * C
+GROUPS = ((0, BANK), (BANK, BANK), (2 * BANK, 2 * C), (LAST, C), (LAST + C, C))
 FLOPS = 2 * K * N * (S + T)
 
 WINDOW = 2048
 ROW = T // 2
-TAIL = 128
+TAIL = 256
+FIRST = 960
 RAW = 4 * T
 STEP = ROW + TAIL + RAW
 HEAD = 448
 SPLIT = 416
-EXTRA = 256
+EXTRA = 512
 HEAD_TAIL = 704
 
 F32 = mybir.dt.float32
@@ -50,41 +51,37 @@ def tile_moe_shr_lin_relu2_kernel(tc, xT, w_words, w_scales, b, gate, offs, pos1
         gate_t = keep.tile([P, 2, T], F32, name="gate_t")
         wt = keep.tile([P, (E + 1) * PASSES, 2 * N], U8, name="wt", align_bytes=64)
         wsc = keep.tile([P, (E + 1) * PASSES, N], U8, name="wsc", align_bytes=64)
-        base = 4 * T + HEAD_TAIL
-        arena = keep.tile([P, base + 4 * STEP + RAW], U32, name="arena", tag="arena", align_bytes=64)
-        pairs2 = keep.tile([P, T + WINDOW], U32, name="pairs2", tag="pairs2", align_bytes=64)
+        arena = keep.tile([P, 4 * STEP + RAW], U32, name="arena", tag="arena", align_bytes=64)
+        early = keep.tile([P, 6 * T + HEAD_TAIL], U32, name="early", tag="early", align_bytes=64)
         picked = keep.tile([P, PASSES * 2 * S], U32, name="picked", align_bytes=64)
         cscale = keep.tile([P, PASSES * S], U8, name="cscale", align_bytes=64)
         sscale = keep.tile([P, PASSES * T], U8, name="sscale", align_bytes=64)
         y = keep.tile([P, S], F32, name="y")
         ys = keep.tile([P, T], F32, name="ys")
-        last_quads = keep.tile([P, BANK], U32, name="last_quads", align_bytes=64)
-        own_quads = keep.tile([P, 4 * T], U32, name="own_quads", align_bytes=64)
+        last_quads = keep.tile([P, 4 * C], U32, name="last_quads", align_bytes=64)
+        first_quads = keep.tile([P, 2 * BANK], U32, name="first_quads", tag="first", align_bytes=64)
+        own_quads = keep.tile([P, 8 * T], U32, name="own_quads", align_bytes=64)
 
         ps_sa = psum.tile([P, BANK], F32, name="ps_sa")
         ps_sb = psum.tile([P, BANK], F32, name="ps_sb")
         ps = [psum.tile([P, n], F32, name="ps%d" % i) for i, (lo, n) in enumerate(GROUPS)]
 
-        nc.vector.memset(arena[:, 4 * T:base], 0)
+        nc.vector.memset(early[:, 6 * T:], 0)
         for j in range(4):
-            nc.scalar.copy(out=arena[:, base + j * STEP + ROW:base + j * STEP + ROW + TAIL], in_=arena[:, 4 * T:4 * T + TAIL])
-        nc.vector.memset(pairs2[:, 2 * T:], 0)
+            nc.scalar.copy(out=arena[:, j * STEP + ROW:j * STEP + ROW + TAIL], in_=early[:, 6 * T:6 * T + TAIL])
         nc.gpsimd.memset(wsc[:].rearrange("p a n -> p (a n)").bitcast(I32), 0)
 
         xv = xT.rearrange("(a p j) t -> a p j t", a=PASSES, j=4)
 
-        def row_start(j):
-            return base + j * STEP
-
         def raw_start(a):
-            return base + 4 * STEP if a == 3 else base + (a + 1) % PASSES * STEP + ROW + TAIL
+            return 4 * STEP if a == 3 else (a + 1) % PASSES * STEP + ROW + TAIL
 
         def raw(a, j, n):
             s = raw_start(a) + j * T
             return arena[:, s:s + n * T].bitcast(F32)
 
         def pairs(a, u, n):
-            tile, s = ((arena, 2 * T), (arena, 0), (pairs2, 0), (picked, 0))[a]
+            tile, s = (picked, 0) if a == 3 else (early, 2 * T * (2 - a))
             return tile[:, s + u * T:s + u * T + n]
 
         def load_rows(a, j, n):
@@ -99,14 +96,13 @@ def tile_moe_shr_lin_relu2_kernel(tc, xT, w_words, w_scales, b, gate, offs, pos1
             nc.sync.dma_start(out=bias[:], in_=b)
             scale_rows = wsc[:].rearrange("p a n -> p (a n)").bitcast(I32)
             nc.sync.dma_start(out=scale_rows[0:16].rearrange("p (a n) -> p a n", n=N // 4), in_=w_scales.bitcast(I32).rearrange("e a q n -> q (e a) n"))
-            wv = w_words.bitcast(I32).rearrange("e a p n -> a p e n")
-            wd = wt[:].rearrange("p a n -> p (a n)").bitcast(I32).rearrange("p (a e n) -> p a e n", a=PASSES, n=N // 2)
-            for i, a in enumerate(order):
-                nc.sync.dma_start(out=wd[:, a, :E], in_=wv[a][:, :E])
-                if i == 1:
+            wv = w_words.bitcast(I32).rearrange("e a p n -> p (e a) n")
+            wd = wt[:].rearrange("p a n -> p (a n)").bitcast(I32).rearrange("p (a n) -> p a n", n=N // 2)
+            for lo, hi in ((0, 2 * BANK // C), (2 * BANK // C, E), (E, E + 1)):
+                nc.sync.dma_start(out=wd[:, lo * PASSES:hi * PASSES], in_=wv[:, lo * PASSES:hi * PASSES])
+                if lo == 0:
                     for q in range(1, 4):
                         nc.sync.dma_start(out=scale_rows[32 * q:32 * q + 4], in_=scale_rows[4 * q:4 * q + 4])
-            nc.sync.dma_start(out=wd[:, :, E], in_=w_words.bitcast(I32)[E].rearrange("a p n -> p a n"))
             nc.sync.dma_start(out=gate_t[:], in_=gate.rearrange("g p t -> p g t"))
             nc.sync.dma_start(pos1_t[:], pos1)
             nc.sync.dma_start(pos2_t[:], pos2)
@@ -120,7 +116,7 @@ def tile_moe_shr_lin_relu2_kernel(tc, xT, w_words, w_scales, b, gate, offs, pos1
             rnd(d[:, lo:hi, :], s[:, lo:hi, :])
 
         def round_row(j, rnd):
-            rnd(arena[:, row_start(j):row_start(j) + ROW].bitcast(BF16), raw(X, j, 1))
+            rnd(arena[:, j * STEP:j * STEP + ROW].bitcast(BF16), raw(X, j, 1))
 
         def picks(a, u, lo, n):
             s = (2 * a + u) * S + lo
@@ -135,15 +131,15 @@ def tile_moe_shr_lin_relu2_kernel(tc, xT, w_words, w_scales, b, gate, offs, pos1
 
         def scalar_gather(j):
             v = picks(X, j // 2, 0, S).bitcast(BF16).rearrange("p (s j) -> p s j", j=2)
-            w = arena[:, row_start(j):row_start(j) + ROW + TAIL].bitcast(BF16)
-            for lo in (0, T):
-                nc.scalar.activation(v[:, lo:lo + T, j % 2], w.indirect(offs_t[:, lo // 16:(lo + T) // 16]), COPY)
+            for lo, hi, words in ((0, FIRST, ROW + TAIL), (FIRST, S, ROW)):
+                w = arena[:, j * STEP:j * STEP + words].bitcast(BF16)
+                nc.scalar.activation(v[:, lo:hi, j % 2], w.indirect(offs_t[:, lo // 16:hi // 16]), COPY)
 
         def quads(a, lo, n):
-            if (a, lo) == (3, LAST):
-                return last_quads[:]
-            if (a, lo) == (X, 2 * BANK):
-                return picked[:, 6 * S:6 * S + 2 * n]
+            if (a, lo) == (3, 0):
+                return first_quads[:]
+            if a == 3 and lo >= LAST:
+                return last_quads[:, 2 * (lo - LAST):2 * (lo - LAST + n)]
             s = raw_start(a) - (0 if a == 3 else TAIL)
             return arena[:, s + 2 * lo:s + 2 * (lo + n)]
 
@@ -151,19 +147,8 @@ def tile_moe_shr_lin_relu2_kernel(tc, xT, w_words, w_scales, b, gate, offs, pos1
             src = picked[:, 2 * a * S:2 * (a + 1) * S].rearrange("p (u s) -> p s u", u=2)[:, lo:lo + n, :]
             nc.scalar.copy(out=quads(a, lo, n).rearrange("p (s u) -> p s u", u=2), in_=src)
 
-        shared_order = (X, 2, 3, 0, 1)
-        shared_home = {X: (own_quads, 0), 2: (own_quads, 2 * T), 3: (picked, 2 * S), 0: (picked, 2 * S + 2 * T), 1: (picked, 8 * S)}
-
-        def shared_quads(a, lo=0, n=T):
-            tile, start = shared_home[a]
-            return tile[:, start + 2 * lo:start + 2 * (lo + n)]
-
-        def shared_weave(a, copy, lo=0, n=T):
-            copy(out=shared_quads(a, lo, n).rearrange("p (s u) -> p s u", u=2),
-                 in_=pairs(a, 0, 2 * T).rearrange("p (u s) -> p s u", u=2)[:, lo:lo + n, :])
-
         def mm(dst, e, a, cd, cs, lo, n, start, stop):
-            nc.tensor.matmul_mx(out=dst, lhsT=wt[:, a * (E + 1) + e, :].bitcast(FP4), lhsT_scale=wsc[:, e * PASSES + a, :],
+            nc.tensor.matmul_mx(out=dst, lhsT=wt[:, e * PASSES + a, :].bitcast(FP4), lhsT_scale=wsc[:, e * PASSES + a, :],
                                 rhs=cd[:, lo:lo + n].bitcast(FP8), rhs_scale=cs[:, lo:lo + n], start=start, stop=stop)
 
         load_rows(0, 2, 1)
@@ -202,69 +187,68 @@ def tile_moe_shr_lin_relu2_kernel(tc, xT, w_words, w_scales, b, gate, offs, pos1
         scalar_gather(2)
         round_pairs(1, 0, 0, T, pool_round)
         gather(1, 0, 0, WINDOW)
+        round_row(3, nc.scalar.copy)
         weave(1, 0, S)
         round_pairs(2, 1, 0, T, pool_round)
         gather(2, 1, 0, WINDOW)
-        round_row(3, nc.scalar.copy)
         scalar_gather(3)
         round_pairs(2, 0, 0, T, pool_round)
         gather(2, 0, 0, WINDOW)
         weave(2, 0, S)
-        pool_round(shared_quads(X).bitcast(BF16).rearrange("p (t j) -> p t j", j=4), raw(X, 0, 4).rearrange("p (j t) -> p t j", j=4))
-        weave(X, 0, 2 * BANK)
+        pool_round(own_quads[:, :2 * T].bitcast(BF16).rearrange("p (t j) -> p t j", j=4), raw(X, 0, 4).rearrange("p (j t) -> p t j", j=4))
+        weave(X, 0, S)
         round_pairs(3, 1, 0, T, pool_round)
         gather(3, 1, 0, WINDOW)
         round_pairs(3, 0, 0, T, pool_round)
         gather(3, 0, 0, WINDOW)
-        shared_weave(0, nc.gpsimd.tensor_copy, 0, H)
-        shared_weave(3, nc.gpsimd.tensor_copy)
-        shared_weave(2, nc.gpsimd.tensor_copy)
-        weave(3, 0, 2 * BANK)
-        weave(X, 2 * BANK, BANK)
-        for lo, n in GROUPS[2:]:
+        nc.gpsimd.tensor_copy(out=own_quads[:, 2 * T:].rearrange("p (a t u) -> p a t u", a=3, u=2),
+                              in_=early[:, :6 * T].rearrange("p (a u t) -> p a t u", a=3, u=2))
+        for lo, n in GROUPS[:3]:
             weave(3, lo, n)
-        shared_weave(0, nc.scalar.copy, H, H)
-        shared_weave(1, nc.scalar.copy)
+        weave(3, LAST, S - LAST)
+        late_quads = picked[:, 6 * S + 2 * BANK - 2 * T:6 * S + 2 * BANK]
+        nc.scalar.copy(out=late_quads.rearrange("p (t u) -> p t u", u=2), in_=pairs(3, 0, 2 * T).rearrange("p (u t) -> p t u", u=2))
 
-        codes = keep.tile([P, PASSES * S], U32, name="codes", tag="pairs2", align_bytes=64)
-        def routed(a, lo, n):
-            nc.vector.quantize_mx(out=codes[:, a * S + lo:a * S + lo + n].bitcast(FP8), scales=cscale[:, a * S + lo:a * S + lo + n],
-                                  in_=quads(a, lo, n).bitcast(BF16))
+        def routed(codes, scales, a, lo, n):
+            nc.vector.quantize_mx(out=codes.bitcast(FP8), scales=scales, in_=quads(a, lo, n).bitcast(BF16))
             for s0 in range(lo, lo + n, C):
                 g = max(i for i in range(len(GROUPS)) if GROUPS[i][0] <= s0)
                 c0 = s0 - GROUPS[g][0]
-                mm(ps[g][:, c0:c0 + C], s0 // C, a, codes, cscale, a * S + s0, C,
+                mm(ps[g][:, c0:c0 + C], s0 // C, a, codes, scales, s0 - lo, C,
                    a == order[0] and c0 == 0, a == order[-1] and c0 + C == GROUPS[g][1])
 
-        for a in order[:3]:
-            routed(a, 0, 2 * BANK)
-            routed(a, 2 * BANK, BANK)
-        routed(X, 0, 2 * BANK)
-        for lo, n in GROUPS[:2]:
-            routed(order[-1], lo, n)
-        routed(X, 2 * BANK, BANK)
-        for lo, n in GROUPS[2:]:
-            routed(order[-1], lo, n)
+        for first, width, groups, tag in ((0, 2 * BANK, GROUPS[:2], "early"), (2 * BANK, BANK, GROUPS[2:], "first")):
+            codes = keep.tile([P, PASSES * width], U32, name="codes_" + tag, tag=tag, align_bytes=64)
+            for a, lo, n in [(a, first, width) for a in order[:-1]] + [(order[-1], lo, n) for lo, n in groups]:
+                at = a * width + lo - first
+                routed(codes[:, at:at + n], cscale[:, a * S + lo:a * S + lo + n], a, lo, n)
         for g, (lo, n) in enumerate(GROUPS):
             r = y[:, lo:lo + n] if n == BANK else ys[:, lo - 2 * BANK:lo - 2 * BANK + n]
             for c0 in range(0, n, C):
                 e = (lo + c0) // C
                 nc.scalar.activation(out=r[:, c0:c0 + C], in_=ps[g][:, c0:c0 + C], func=RELU, bias=bias[:, e:e + 1])
             if n == BANK:
-                nc.scalar.activation(out=r, in_=r, func=SQUARE)
+                for c0 in (0, n // 2):
+                    nc.scalar.activation(out=r[:, c0:c0 + n // 2], in_=r[:, c0:c0 + n // 2], func=SQUARE)
         for lo, n in GROUPS[2:]:
             nc.scalar.activation(out=y[:, lo:lo + n], in_=ys[:, lo - 2 * BANK:lo - 2 * BANK + n], func=SQUARE)
 
         scodes = keep.tile([P, PASSES * T], U32, name="scodes", tag="arena", align_bytes=64)
-        runs = (((0, 1024),), ((1024 - T, 512),)) * 2 + (((0, 512), (512, T - 512)),)
+        shared_order = (X, 2, 1, 0, 3)
+
+        def shared_quantise(lo, n, src):
+            nc.vector.quantize_mx(out=scodes[:, lo:lo + n].bitcast(FP8), scales=sscale[:, lo:lo + n], in_=src.bitcast(BF16))
+
         for i, a in enumerate(shared_order):
-            for lo, n in runs[i]:
-                nc.vector.quantize_mx(out=scodes[:, i * T + lo:i * T + lo + n].bitcast(FP8), scales=sscale[:, i * T + lo:i * T + lo + n],
-                                      in_=shared_quads(a, lo, n).bitcast(BF16))
+            if i < 3:
+                shared_quantise(2 * BANK * i, 2 * BANK, own_quads[:, 4 * BANK * i:4 * BANK * (i + 1)])
+            if a == 3:
+                for lo, n in ((0, BANK), (BANK, T - BANK)):
+                    shared_quantise(4 * T + lo, n, late_quads[:, 2 * lo:2 * (lo + n)])
             mm(ps_sa[:], E, a, scodes, sscale, i * T, BANK, i == 0, i == PASSES - 1)
             mm(ps_sb[:], E, a, scodes, sscale, i * T + T - BANK, BANK, i == 0, i == PASSES - 1)
 
-        sums = keep.tile([P, 2, T], F32, name="sums", tag="pairs2", align_bytes=64)
+        sums = keep.tile([P, 2, T], F32, name="sums", tag="early", align_bytes=64)
         g1, g2 = sums[:, 0, :], sums[:, 1, :]
         halves = (slice(0, H), slice(H, T))
         nc.scalar.activation(g2, y[:].indirect(pos2_t[:]), COPY)

@@ -187,10 +187,10 @@ def tile_moe_shr_lin_relu2_kernel(tc, xT, w_words, w_scales, b, gate, offs, pos1
         scalar_gather(2)
         round_pairs(1, 0, 0, T, pool_round)
         gather(1, 0, 0, WINDOW)
-        round_row(3, nc.scalar.copy)
         weave(1, 0, S)
         round_pairs(2, 1, 0, T, pool_round)
         gather(2, 1, 0, WINDOW)
+        round_row(3, pool_round)
         scalar_gather(3)
         round_pairs(2, 0, 0, T, pool_round)
         gather(2, 0, 0, WINDOW)

@@ -66,9 +66,10 @@ def tile_moe_shr_lin_relu2_kernel(tc, xT, w_words, w_scales, b, gate, offs, pos1
         ps_sb = psum.tile([P, BANK], F32, name="ps_sb")
         ps = [psum.tile([P, n], F32, name="ps%d" % i) for i, (lo, n) in enumerate(GROUPS)]
 
-        nc.vector.memset(early[:, 6 * T:], 0)
-        for j in range(4):
-            nc.scalar.copy(out=arena[:, j * STEP + ROW:j * STEP + ROW + TAIL], in_=early[:, 6 * T:6 * T + TAIL])
+        nc.gpsimd.memset(early[:, 6 * T:], 0)
+        tails = arena[:, :4 * STEP].rearrange("p (j w) -> p j w", j=4)[:, :, ROW:ROW + TAIL]
+        for j in (0, 2):
+            nc.scalar.copy(out=tails[:, j:j + 2, :], in_=early[:, 6 * T:6 * T + 2 * TAIL].rearrange("p (j w) -> p j w", j=2))
         nc.gpsimd.memset(wsc[:].rearrange("p a n -> p (a n)").bitcast(I32), 0)
 
         xv = xT.rearrange("(a p j) t -> a p j t", a=PASSES, j=4)

@@ -63,14 +63,18 @@ def tile_moe_shr_lin_relu2_kernel(tc, xT, w_words, w_scales, b, gate, offs, pos1
         own_quads = keep.tile([P, 8 * T], U32, name="own_quads", align_bytes=64)
 
         ps_sa = psum.tile([P, BANK], F32, name="ps_sa")
-        ps_sb = psum.tile([P, BANK], F32, name="ps_sb")
+        ps_sb = psum.tile([P, T - BANK], F32, name="ps_sb")
         ps = [psum.tile([P, n], F32, name="ps%d" % i) for i, (lo, n) in enumerate(GROUPS)]
 
-        nc.gpsimd.memset(early[:, 6 * T:], 0)
-        tails = arena[:, :4 * STEP].rearrange("p (j w) -> p j w", j=4)[:, :, ROW:ROW + TAIL]
-        for j in (0, 2):
-            nc.scalar.copy(out=tails[:, j:j + 2, :], in_=early[:, 6 * T:6 * T + 2 * TAIL].rearrange("p (j w) -> p j w", j=2))
+        def tail(j, more=0):
+            return arena[:, j * STEP + ROW - more:j * STEP + ROW + TAIL]
+
+        nc.gpsimd.memset(tail(1), 0)
+        nc.scalar.copy(out=tail(0), in_=tail(1))
         nc.gpsimd.memset(wsc[:].rearrange("p a n -> p (a n)").bitcast(I32), 0)
+        nc.vector.memset(early[:, 6 * T - 1:], 0)
+        for j in (2, 3):
+            nc.vector.memset(tail(j, 1), 0)
 
         xv = xT.rearrange("(a p j) t -> a p j t", a=PASSES, j=4)
 
@@ -247,7 +251,7 @@ def tile_moe_shr_lin_relu2_kernel(tc, xT, w_words, w_scales, b, gate, offs, pos1
                 for lo, n in ((0, BANK), (BANK, T - BANK)):
                     shared_quantise(4 * T + lo, n, late_quads[:, 2 * lo:2 * (lo + n)])
             mm(ps_sa[:], E, a, scodes, sscale, i * T, BANK, i == 0, i == PASSES - 1)
-            mm(ps_sb[:], E, a, scodes, sscale, i * T + T - BANK, BANK, i == 0, i == PASSES - 1)
+            mm(ps_sb[:], E, a, scodes, sscale, i * T + BANK, T - BANK, i == 0, i == PASSES - 1)
 
         sums = keep.tile([P, 2, T], F32, name="sums", tag="early", align_bytes=64)
         g1, g2 = sums[:, 0, :], sums[:, 1, :]
@@ -255,8 +259,8 @@ def tile_moe_shr_lin_relu2_kernel(tc, xT, w_words, w_scales, b, gate, offs, pos1
         nc.scalar.activation(g2, y[:].indirect(pos2_t[:]), COPY)
         nc.scalar.activation(g1[:, :EXTRA], y[:].indirect(pos1_t[:, :EXTRA // 16]), COPY)
         nc.vector.tensor_tensor(g1[:, EXTRA:], y[:].indirect(pos1_t[:, EXTRA // 16:]), gate_t[:, 0, EXTRA:], MULT)
-        nc.scalar.activation(out=ys[:, :H], in_=ps_sa[:, :H], func=RELU, bias=bias[:, E:E + 1])
-        nc.scalar.activation(out=ys[:, H:], in_=ps_sb[:, BANK - H:], func=RELU, bias=bias[:, E:E + 1])
+        nc.scalar.activation(out=ys[:, :BANK], in_=ps_sa[:], func=RELU, bias=bias[:, E:E + 1])
+        nc.scalar.activation(out=ys[:, BANK:], in_=ps_sb[:], func=RELU, bias=bias[:, E:E + 1])
         for c in halves:
             nc.scalar.activation(out=ys[:, c], in_=ys[:, c], func=SQUARE)
 

@@ -21,7 +21,6 @@ RAW = 4 * T
 STEP = ROW + TAIL + RAW
 HEAD = 448
 SPLIT = 416
-EXTRA = 512
 HEAD_TAIL = 704
 
 F32 = mybir.dt.float32
@@ -103,14 +102,15 @@ def tile_moe_shr_lin_relu2_kernel(tc, xT, w_words, w_scales, b, gate, offs, pos1
             nc.sync.dma_start(out=scale_rows[0:16].rearrange("p (a n) -> p a n", n=N // 4), in_=w_scales.bitcast(I32).rearrange("e a q n -> q (e a) n"))
             wv = w_words.bitcast(I32).rearrange("e a p n -> p (e a) n")
             wd = wt[:].rearrange("p a n -> p (a n)").bitcast(I32).rearrange("p (a n) -> p a n", n=N // 2)
-            for lo, hi in ((0, 2 * BANK // C), (2 * BANK // C, E), (E, E + 1)):
-                nc.sync.dma_start(out=wd[:, lo * PASSES:hi * PASSES], in_=wv[:, lo * PASSES:hi * PASSES])
-                if lo == 0:
-                    for q in range(1, 4):
-                        nc.sync.dma_start(out=scale_rows[32 * q:32 * q + 4], in_=scale_rows[4 * q:4 * q + 4])
-            nc.sync.dma_start(out=gate_t[:], in_=gate.rearrange("g p t -> p g t"))
-            nc.sync.dma_start(pos1_t[:], pos1)
+            first = 2 * BANK // C * PASSES
+            nc.sync.dma_start(out=wd[:, :first], in_=wv[:, :first])
+            for q in range(1, 4):
+                nc.sync.dma_start(out=scale_rows[32 * q:32 * q + 4], in_=scale_rows[4 * q:4 * q + 4])
+            nc.sync.dma_start(out=wd[:, first:E * PASSES], in_=wv[:, first:E * PASSES])
             nc.sync.dma_start(pos2_t[:], pos2)
+            nc.sync.dma_start(pos1_t[:], pos1)
+            nc.sync.dma_start(out=gate_t[:], in_=gate.rearrange("g p t -> p g t"))
+            nc.sync.dma_start(out=wd[:, E * PASSES:], in_=wv[:, E * PASSES:])
 
         def pool_round(dst, src):
             nc.gpsimd.tensor_scalar(out=dst, in0=src, scalar1=1.0, scalar2=0.0, op0=MULT, op1=ADD)
@@ -222,11 +222,12 @@ def tile_moe_shr_lin_relu2_kernel(tc, xT, w_words, w_scales, b, gate, offs, pos1
                 mm(ps[g][:, c0:c0 + C], s0 // C, a, codes, scales, s0 - lo, C,
                    a == order[0] and c0 == 0, a == order[-1] and c0 + C == GROUPS[g][1])
 
-        for first, width, groups, tag in ((0, 2 * BANK, GROUPS[:2], "early"), (2 * BANK, BANK, GROUPS[2:], "first")):
+        for first, width, sets, tag in ((0, 2 * BANK, (GROUPS[:2],), "early"), (2 * BANK, BANK, (GROUPS[2:3], GROUPS[3:]), "first")):
             codes = keep.tile([P, PASSES * width], U32, name="codes_" + tag, tag=tag, align_bytes=64)
-            for a, lo, n in [(a, first, width) for a in order[:-1]] + [(order[-1], lo, n) for lo, n in groups]:
-                at = a * width + lo - first
-                routed(codes[:, at:at + n], cscale[:, a * S + lo:a * S + lo + n], a, lo, n)
+            for groups in sets:
+                for a, lo, n in [(a, groups[0][0], width // len(sets)) for a in order[:-1]] + [(order[-1], lo, n) for lo, n in groups]:
+                    at = a * width + lo - first
+                    routed(codes[:, at:at + n], cscale[:, a * S + lo:a * S + lo + n], a, lo, n)
         for g, (lo, n) in enumerate(GROUPS):
             r = y[:, lo:lo + n] if n == BANK else ys[:, lo - 2 * BANK:lo - 2 * BANK + n]
             for c0 in range(0, n, C):
@@ -257,16 +258,16 @@ def tile_moe_shr_lin_relu2_kernel(tc, xT, w_words, w_scales, b, gate, offs, pos1
         g1, g2 = sums[:, 0, :], sums[:, 1, :]
         halves = (slice(0, H), slice(H, T))
         nc.scalar.activation(g2, y[:].indirect(pos2_t[:]), COPY)
-        nc.scalar.activation(g1[:, :EXTRA], y[:].indirect(pos1_t[:, :EXTRA // 16]), COPY)
-        nc.vector.tensor_tensor(g1[:, EXTRA:], y[:].indirect(pos1_t[:, EXTRA // 16:]), gate_t[:, 0, EXTRA:], MULT)
+        for c in halves:
+            nc.scalar.activation(g1[:, c], y[:].indirect(pos1_t[:, c.start // 16:c.stop // 16]), COPY)
         nc.scalar.activation(out=ys[:, :BANK], in_=ps_sa[:], func=RELU, bias=bias[:, E:E + 1])
         nc.scalar.activation(out=ys[:, BANK:], in_=ps_sb[:], func=RELU, bias=bias[:, E:E + 1])
         for c in halves:
             nc.scalar.activation(out=ys[:, c], in_=ys[:, c], func=SQUARE)
 
-        nc.vector.tensor_tensor(g2[:, :H], g2[:, :H], gate_t[:, 1, :H], MULT)
-        nc.vector.tensor_tensor(g1[:, :EXTRA], g1[:, :EXTRA], gate_t[:, 0, :EXTRA], MULT)
-        nc.vector.tensor_tensor(g2[:, H:], g2[:, H:], gate_t[:, 1, H:], MULT)
+        nc.vector.tensor_tensor(g2, g2, gate_t[:, 1, :], MULT)
+        for c in halves:
+            nc.vector.tensor_tensor(g1[:, c], g1[:, c], gate_t[:, 0, c], MULT)
         for c in halves:
             nc.vector.tensor_tensor(g1[:, c], g1[:, c], g2[:, c], ADD)
         for c in halves:

@@ -14,14 +14,11 @@ GROUPS = ((0, BANK), (BANK, BANK), (2 * BANK, 2 * C), (LAST, C), (LAST + C, C))
 FLOPS = 2 * K * N * (S + T)
 
 WINDOW = 2048
-ROW = T // 2
-TAIL = 256
-FIRST = 960
+PAD = 257
 RAW = 4 * T
-STEP = ROW + TAIL + RAW
 HEAD = 448
 SPLIT = 416
-HEAD_TAIL = 704
+HEAD_TAIL = 705
 
 F32 = mybir.dt.float32
 BF16 = mybir.dt.bfloat16
@@ -43,60 +40,61 @@ def tile_moe_shr_lin_relu2_kernel(tc, xT, w_words, w_scales, b, gate, offs, pos1
         keep = ctx.enter_context(tc.tile_pool(name="keep", bufs=1))
         psum = ctx.enter_context(tc.psum_pool(name="psum", bufs=1))
 
+        def tile(name, width, dtype, tag):
+            return keep.tile([P, width], dtype, name=name, tag=tag, align_bytes=64)
+
         offs_t = keep.tile([P, S // 16], U16, name="offs_t")
         pos1_t = keep.tile([P, T // 16], U16, name="pos1_t")
         pos2_t = keep.tile([P, T // 16], U16, name="pos2_t")
         bias = keep.tile([P, E + 1], F32, name="bias")
-        gate_t = keep.tile([P, 2, T], F32, name="gate_t")
         wt = keep.tile([P, (E + 1) * PASSES, 2 * N], U8, name="wt", align_bytes=64)
         wsc = keep.tile([P, (E + 1) * PASSES, N], U8, name="wsc", align_bytes=64)
-        arena = keep.tile([P, 4 * STEP + RAW], U32, name="arena", tag="arena", align_bytes=64)
-        early = keep.tile([P, 6 * T + HEAD_TAIL], U32, name="early", tag="early", align_bytes=64)
-        picked = keep.tile([P, PASSES * 2 * S], U32, name="picked", align_bytes=64)
-        cscale = keep.tile([P, PASSES * S], U8, name="cscale", align_bytes=64)
-        sscale = keep.tile([P, PASSES * T], U8, name="sscale", align_bytes=64)
-        y = keep.tile([P, S], F32, name="y")
-        ys = keep.tile([P, T], F32, name="ys")
-        last_quads = keep.tile([P, 4 * C], U32, name="last_quads", align_bytes=64)
-        first_quads = keep.tile([P, 2 * BANK], U32, name="first_quads", tag="first", align_bytes=64)
-        own_quads = keep.tile([P, 8 * T], U32, name="own_quads", align_bytes=64)
+        arena = tile("arena", 6 * RAW, U32, "arena")
+        early = tile("early", 8 * T + HEAD_TAIL, U32, "early")
+        rows = [tile("row%d" % j, T + PAD, F32, "row%d" % j) for j in range(4)]
+        x_last = tile("x_last", RAW, F32, "x_last")
+        own_quads = tile("own_quads", PASSES * 2 * T, U32, "own_quads")
+        first_quads = tile("first_quads", 2 * BANK, U32, "first")
+        cscale = tile("cscale", PASSES * S, U8, "cscale")
+        sscale = tile("sscale", PASSES * T, U8, "sscale")
 
         ps_sa = psum.tile([P, BANK], F32, name="ps_sa")
         ps_sb = psum.tile([P, T - BANK], F32, name="ps_sb")
         ps = [psum.tile([P, n], F32, name="ps%d" % i) for i, (lo, n) in enumerate(GROUPS)]
 
-        def tail(j, more=0):
-            return arena[:, j * STEP + ROW - more:j * STEP + ROW + TAIL]
+        def pad(j):
+            return rows[j][:, T:].bitcast(U32)
 
-        nc.gpsimd.memset(tail(1), 0)
-        nc.scalar.copy(out=tail(0), in_=tail(1))
+        nc.gpsimd.memset(pad(1), 0)
+        nc.scalar.copy(out=pad(0), in_=pad(1))
         nc.gpsimd.memset(wsc[:].rearrange("p a n -> p (a n)").bitcast(I32), 0)
-        nc.vector.memset(early[:, 6 * T - 1:], 0)
+        nc.vector.memset(early[:, 8 * T:], 0)
         for j in (2, 3):
-            nc.vector.memset(tail(j, 1), 0)
+            nc.vector.memset(pad(j), 0)
 
         xv = xT.rearrange("(a p j) t -> a p j t", a=PASSES, j=4)
 
-        def raw_start(a):
-            return 4 * STEP if a == 3 else (a + 1) % PASSES * STEP + ROW + TAIL
+        def region(i, lo, n):
+            return arena[:, i * RAW + lo:i * RAW + lo + n]
 
         def raw(a, j, n):
-            s = raw_start(a) + j * T
-            return arena[:, s:s + n * T].bitcast(F32)
+            return region(a, j * T, n * T).bitcast(F32)
 
         def pairs(a, u, n):
-            tile, s = (picked, 0) if a == 3 else (early, 2 * T * (2 - a))
-            return tile[:, s + u * T:s + u * T + n]
+            s = 2 * T * (3 - a) + u * T
+            return early[:, s:s + n]
 
-        def load_rows(a, j, n):
-            nc.sync.dma_start(out=raw(a, j, n).rearrange("p (j t) -> p j t", j=n), in_=xv[a][:, j:j + n, :])
-
-        def load_cols(a, u, lo, hi):
+        def load_plane(a, u, lo, hi):
             nc.sync.dma_start(out=raw(a, 2 * u, 2).rearrange("p (j t) -> p j t", j=2)[:, :, lo:hi], in_=xv[a][:, 2 * u:2 * u + 2, lo:hi])
 
-        order = (0, 1, 2, X, 3)
+        def load_row(dst, a, j):
+            nc.sync.dma_start(out=dst, in_=xv[a][:, j, :])
+
+        gate_t = region(3, 0, 2 * T).bitcast(F32)
+        order = (0, 1, X, 2, 3)
 
         def late_loads():
+            nc.sync.dma_start(out=x_last[:].rearrange("p (j t) -> p j t", j=4), in_=xv[X])
             nc.sync.dma_start(out=bias[:], in_=b)
             scale_rows = wsc[:].rearrange("p a n -> p (a n)").bitcast(I32)
             nc.sync.dma_start(out=scale_rows[0:16].rearrange("p (a n) -> p a n", n=N // 4), in_=w_scales.bitcast(I32).rearrange("e a q n -> q (e a) n"))
@@ -109,7 +107,7 @@ def tile_moe_shr_lin_relu2_kernel(tc, xT, w_words, w_scales, b, gate, offs, pos1
             nc.sync.dma_start(out=wd[:, first:E * PASSES], in_=wv[:, first:E * PASSES])
             nc.sync.dma_start(pos2_t[:], pos2)
             nc.sync.dma_start(pos1_t[:], pos1)
-            nc.sync.dma_start(out=gate_t[:], in_=gate.rearrange("g p t -> p g t"))
+            nc.sync.dma_start(out=gate_t.rearrange("p (g t) -> p g t", g=2), in_=gate.rearrange("g p t -> p g t"))
             nc.sync.dma_start(out=wd[:, E * PASSES:], in_=wv[:, E * PASSES:])
 
         def pool_round(dst, src):
@@ -120,12 +118,10 @@ def tile_moe_shr_lin_relu2_kernel(tc, xT, w_words, w_scales, b, gate, offs, pos1
             s = raw(a, 2 * u, 2).rearrange("p (j t) -> p t j", j=2)
             rnd(d[:, lo:hi, :], s[:, lo:hi, :])
 
-        def round_row(j, rnd):
-            rnd(arena[:, j * STEP:j * STEP + ROW].bitcast(BF16), raw(X, j, 1))
+        picks_in = {0: 4, 1: 0, 2: 1, 3: 2, X: 5}
 
         def picks(a, u, lo, n):
-            s = (2 * a + u) * S + lo
-            return picked[:, s:s + n]
+            return region(picks_in[a], u * S + lo, n)
 
         def gather(a, u, lo, window):
             nc.vector.tensor_copy(picks(a, u, lo, S - lo), pairs(a, u, window).indirect(offs_t[:, lo // 16:]))
@@ -136,83 +132,69 @@ def tile_moe_shr_lin_relu2_kernel(tc, xT, w_words, w_scales, b, gate, offs, pos1
 
         def scalar_gather(j):
             v = picks(X, j // 2, 0, S).bitcast(BF16).rearrange("p (s j) -> p s j", j=2)
-            for lo, hi, words in ((0, FIRST, ROW + TAIL), (FIRST, S, ROW)):
-                w = arena[:, j * STEP:j * STEP + words].bitcast(BF16)
-                nc.scalar.activation(v[:, lo:hi, j % 2], w.indirect(offs_t[:, lo // 16:hi // 16]), COPY)
+            for lo in range(0, S, BANK):
+                nc.scalar.activation(v[:, lo:lo + BANK, j % 2], rows[j][:].indirect(offs_t[:, lo // 16:(lo + BANK) // 16]), COPY)
+
+        quads_in = {2: region(0, 0, RAW), 3: region(1, 0, RAW), X: region(4, 0, RAW)}
 
         def quads(a, lo, n):
             if (a, lo) == (3, 0):
                 return first_quads[:]
-            if a == 3 and lo >= LAST:
-                return last_quads[:, 2 * (lo - LAST):2 * (lo - LAST + n)]
-            s = raw_start(a) - (0 if a == 3 else TAIL)
-            return arena[:, s + 2 * lo:s + 2 * (lo + n)]
+            return quads_in[a][:, 2 * lo:2 * (lo + n)]
 
         def weave(a, lo, n):
-            src = picked[:, 2 * a * S:2 * (a + 1) * S].rearrange("p (u s) -> p s u", u=2)[:, lo:lo + n, :]
+            src = region(picks_in[a], 0, RAW).rearrange("p (u s) -> p s u", u=2)[:, lo:lo + n, :]
             nc.scalar.copy(out=quads(a, lo, n).rearrange("p (s u) -> p s u", u=2), in_=src)
 
         def mm(dst, e, a, cd, cs, lo, n, start, stop):
             nc.tensor.matmul_mx(out=dst, lhsT=wt[:, e * PASSES + a, :].bitcast(FP4), lhsT_scale=wsc[:, e * PASSES + a, :],
                                 rhs=cd[:, lo:lo + n].bitcast(FP8), rhs_scale=cs[:, lo:lo + n], start=start, stop=stop)
 
-        load_rows(0, 2, 1)
+        load_row(raw(0, 2, 1), 0, 2)
         nc.sync.dma_start(offs_t[:], offs)
-        load_rows(0, 3, 1)
-        load_rows(X, 0, 1)
-        load_cols(0, 0, 0, H)
-        load_cols(0, 0, H, T)
-        load_rows(X, 1, 1)
-        load_rows(1, 2, 2)
-        load_rows(X, 2, 1)
-        load_rows(1, 0, 2)
-        load_rows(2, 2, 2)
-        load_rows(X, 3, 1)
-        load_rows(2, 0, 2)
-        load_rows(3, 2, 2)
-        load_rows(3, 0, 2)
-        late_loads()
+        load_row(raw(0, 3, 1), 0, 3)
+        load_row(rows[0][:, :T], X, 0)
+        load_plane(0, 0, 0, H)
+        load_plane(0, 0, H, T)
+        load_plane(1, 1, 0, T)
+        load_row(rows[1][:, :T], X, 1)
+        load_plane(1, 0, 0, T)
+        load_plane(2, 1, 0, T)
+        load_plane(2, 0, 0, T)
+        load_row(rows[2][:, :T], X, 2)
+        load_plane(3, 1, 0, T)
+        load_plane(3, 0, 0, T)
+        load_row(rows[3][:, :T], X, 3)
 
         head_gather(0)
         head_gather(1)
         round_pairs(0, 1, 0, SPLIT, nc.scalar.copy)
         round_pairs(0, 1, SPLIT, T, pool_round)
-        round_row(0, nc.scalar.copy)
         gather(0, 1, HEAD, T + HEAD_TAIL)
         scalar_gather(0)
         round_pairs(0, 0, 0, H, pool_round)
         round_pairs(0, 0, H, T, pool_round)
         gather(0, 0, 0, WINDOW)
-        round_row(1, pool_round)
         scalar_gather(1)
+        quads_in[0] = tile("quads0", RAW, U32, "row1")[:]
         weave(0, 0, S)
-        round_pairs(1, 1, 0, T, pool_round)
-        gather(1, 1, 0, WINDOW)
-        round_row(2, pool_round)
+        for a in (1, 2, 3):
+            for u in (1, 0):
+                round_pairs(a, u, 0, T, pool_round)
+                gather(a, u, 0, WINDOW)
+        late_loads()
         scalar_gather(2)
-        round_pairs(1, 0, 0, T, pool_round)
-        gather(1, 0, 0, WINDOW)
-        weave(1, 0, S)
-        round_pairs(2, 1, 0, T, pool_round)
-        gather(2, 1, 0, WINDOW)
-        round_row(3, pool_round)
         scalar_gather(3)
-        round_pairs(2, 0, 0, T, pool_round)
-        gather(2, 0, 0, WINDOW)
-        weave(2, 0, S)
-        pool_round(own_quads[:, :2 * T].bitcast(BF16).rearrange("p (t j) -> p t j", j=4), raw(X, 0, 4).rearrange("p (j t) -> p t j", j=4))
+        quads_in[1] = tile("quads1", RAW, U32, "row3")[:]
+        weave(1, 0, S)
         weave(X, 0, S)
-        round_pairs(3, 1, 0, T, pool_round)
-        gather(3, 1, 0, WINDOW)
-        round_pairs(3, 0, 0, T, pool_round)
-        gather(3, 0, 0, WINDOW)
-        nc.gpsimd.tensor_copy(out=own_quads[:, 2 * T:].rearrange("p (a t u) -> p a t u", a=3, u=2),
-                              in_=early[:, :6 * T].rearrange("p (a u t) -> p a t u", a=3, u=2))
+        weave(2, 0, S)
+        nc.gpsimd.tensor_copy(out=own_quads[:, :8 * T].rearrange("p (a t u) -> p a t u", a=4, u=2),
+                              in_=early[:, :8 * T].rearrange("p (a u t) -> p a t u", a=4, u=2))
+        pool_round(own_quads[:, 8 * T:].bitcast(BF16).rearrange("p (t j) -> p t j", j=4), x_last[:].rearrange("p (j t) -> p t j", j=4))
         for lo, n in GROUPS[:3]:
             weave(3, lo, n)
         weave(3, LAST, S - LAST)
-        late_quads = picked[:, 6 * S + 2 * BANK - 2 * T:6 * S + 2 * BANK]
-        nc.scalar.copy(out=late_quads.rearrange("p (t u) -> p t u", u=2), in_=pairs(3, 0, 2 * T).rearrange("p (u t) -> p t u", u=2))
 
         def routed(codes, scales, a, lo, n):
             nc.vector.quantize_mx(out=codes.bitcast(FP8), scales=scales, in_=quads(a, lo, n).bitcast(BF16))
@@ -222,12 +204,14 @@ def tile_moe_shr_lin_relu2_kernel(tc, xT, w_words, w_scales, b, gate, offs, pos1
                 mm(ps[g][:, c0:c0 + C], s0 // C, a, codes, scales, s0 - lo, C,
                    a == order[0] and c0 == 0, a == order[-1] and c0 + C == GROUPS[g][1])
 
-        for first, width, sets, tag in ((0, 2 * BANK, (GROUPS[:2],), "early"), (2 * BANK, BANK, (GROUPS[2:3], GROUPS[3:]), "first")):
-            codes = keep.tile([P, PASSES * width], U32, name="codes_" + tag, tag=tag, align_bytes=64)
+        for first, width, sets, tag in ((0, 2 * BANK, (GROUPS[:2],), "x_last"), (2 * BANK, BANK, (GROUPS[2:3], GROUPS[3:]), "first")):
+            codes = tile("codes_" + tag, PASSES * width, U32, tag)
             for groups in sets:
                 for a, lo, n in [(a, groups[0][0], width // len(sets)) for a in order[:-1]] + [(order[-1], lo, n) for lo, n in groups]:
                     at = a * width + lo - first
                     routed(codes[:, at:at + n], cscale[:, a * S + lo:a * S + lo + n], a, lo, n)
+        y = tile("y", S, F32, "row0")
+        ys = tile("ys", T, F32, "row2")
         for g, (lo, n) in enumerate(GROUPS):
             r = y[:, lo:lo + n] if n == BANK else ys[:, lo - 2 * BANK:lo - 2 * BANK + n]
             for c0 in range(0, n, C):
@@ -239,23 +223,22 @@ def tile_moe_shr_lin_relu2_kernel(tc, xT, w_words, w_scales, b, gate, offs, pos1
         for lo, n in GROUPS[2:]:
             nc.scalar.activation(out=y[:, lo:lo + n], in_=ys[:, lo - 2 * BANK:lo - 2 * BANK + n], func=SQUARE)
 
-        scodes = keep.tile([P, PASSES * T], U32, name="scodes", tag="arena", align_bytes=64)
-        shared_order = (X, 2, 1, 0, 3)
+        scodes = tile("scodes", PASSES * T, U32, "row3")
+        shared_order = (3, 2, 1, 0, X)
 
-        def shared_quantise(lo, n, src):
-            nc.vector.quantize_mx(out=scodes[:, lo:lo + n].bitcast(FP8), scales=sscale[:, lo:lo + n], in_=src.bitcast(BF16))
+        def shared_quantise(lo, n):
+            nc.vector.quantize_mx(out=scodes[:, lo:lo + n].bitcast(FP8), scales=sscale[:, lo:lo + n], in_=own_quads[:, 2 * lo:2 * (lo + n)].bitcast(BF16))
 
         for i, a in enumerate(shared_order):
             if i < 3:
-                shared_quantise(2 * BANK * i, 2 * BANK, own_quads[:, 4 * BANK * i:4 * BANK * (i + 1)])
-            if a == 3:
+                shared_quantise(2 * BANK * i, 2 * BANK)
+            if a == X:
                 for lo, n in ((0, BANK), (BANK, T - BANK)):
-                    shared_quantise(4 * T + lo, n, late_quads[:, 2 * lo:2 * (lo + n)])
+                    shared_quantise(4 * T + lo, n)
             mm(ps_sa[:], E, a, scodes, sscale, i * T, BANK, i == 0, i == PASSES - 1)
             mm(ps_sb[:], E, a, scodes, sscale, i * T + BANK, T - BANK, i == 0, i == PASSES - 1)
 
-        sums = keep.tile([P, 2, T], F32, name="sums", tag="early", align_bytes=64)
-        g1, g2 = sums[:, 0, :], sums[:, 1, :]
+        g1, g2 = region(3, 2 * T, T).bitcast(F32), region(3, 3 * T, T).bitcast(F32)
         halves = (slice(0, H), slice(H, T))
         nc.scalar.activation(g2, y[:].indirect(pos2_t[:]), COPY)
         for c in halves:
@@ -265,9 +248,9 @@ def tile_moe_shr_lin_relu2_kernel(tc, xT, w_words, w_scales, b, gate, offs, pos1
         for c in halves:
             nc.scalar.activation(out=ys[:, c], in_=ys[:, c], func=SQUARE)
 
-        nc.vector.tensor_tensor(g2, g2, gate_t[:, 1, :], MULT)
+        nc.vector.tensor_tensor(g2, g2, gate_t[:, T:], MULT)
         for c in halves:
-            nc.vector.tensor_tensor(g1[:, c], g1[:, c], gate_t[:, 0, c], MULT)
+            nc.vector.tensor_tensor(g1[:, c], g1[:, c], gate_t[:, c], MULT)
         for c in halves:
             nc.vector.tensor_tensor(g1[:, c], g1[:, c], g2[:, c], ADD)
         for c in halves:

@@ -77,8 +77,17 @@ def tile_moe_shr_lin_relu2_kernel(tc, xT, w_words, w_scales, b, gate, offs, pos1
         def region(i, lo, n):
             return arena[:, i * RAW + lo:i * RAW + lo + n]
 
+        lands = {(1, 2): 7 * T, (2, 0): 4 * T}
+
         def raw(a, j, n):
+            if (a, j) in lands:
+                return own_quads[:, lands[a, j]:lands[a, j] + n * T].bitcast(F32)
             return region(a, j * T, n * T).bitcast(F32)
+
+        def own_weave(first, n, lo, hi):
+            s = 2 * T * (3 - first)
+            nc.gpsimd.tensor_copy(out=own_quads[:, s:s + 2 * T * n].rearrange("p (a t u) -> p a t u", a=n, u=2)[:, :, lo:hi, :],
+                                  in_=early[:, s:s + 2 * T * n].rearrange("p (a u t) -> p a t u", a=n, u=2)[:, :, lo:hi, :])
 
         def pairs(a, u, n):
             s = 2 * T * (3 - a) + u * T
@@ -94,16 +103,17 @@ def tile_moe_shr_lin_relu2_kernel(tc, xT, w_words, w_scales, b, gate, offs, pos1
         order = (0, 1, X, 2, 3)
 
         def late_loads():
-            nc.sync.dma_start(out=x_last[:].rearrange("p (j t) -> p j t", j=4), in_=xv[X])
             nc.sync.dma_start(out=bias[:], in_=b)
             scale_rows = wsc[:].rearrange("p a n -> p (a n)").bitcast(I32)
             nc.sync.dma_start(out=scale_rows[0:16].rearrange("p (a n) -> p a n", n=N // 4), in_=w_scales.bitcast(I32).rearrange("e a q n -> q (e a) n"))
             wv = w_words.bitcast(I32).rearrange("e a p n -> p (e a) n")
             wd = wt[:].rearrange("p a n -> p (a n)").bitcast(I32).rearrange("p (a n) -> p a n", n=N // 2)
             first = 2 * BANK // C * PASSES
-            nc.sync.dma_start(out=wd[:, :first], in_=wv[:, :first])
+            nc.sync.dma_start(out=x_last[:].rearrange("p (j t) -> p j t", j=4), in_=xv[X])
             for q in range(1, 4):
                 nc.sync.dma_start(out=scale_rows[32 * q:32 * q + 4], in_=scale_rows[4 * q:4 * q + 4])
+            for a in order:
+                nc.sync.dma_start(out=wd[:, a:first:PASSES], in_=wv[:, a:first:PASSES])
             nc.sync.dma_start(out=wd[:, first:E * PASSES], in_=wv[:, first:E * PASSES])
             nc.sync.dma_start(pos2_t[:], pos2)
             nc.sync.dma_start(pos1_t[:], pos1)
@@ -162,8 +172,7 @@ def tile_moe_shr_lin_relu2_kernel(tc, xT, w_words, w_scales, b, gate, offs, pos1
         load_plane(2, 1, 0, T)
         load_plane(2, 0, 0, T)
         load_row(rows[2][:, :T], X, 2)
-        load_plane(3, 1, 0, T)
-        load_plane(3, 0, 0, T)
+        nc.sync.dma_start(out=raw(3, 0, 4).rearrange("p (j t) -> p j t", j=4), in_=xv[3])
         load_row(rows[3][:, :T], X, 3)
 
         head_gather(0)
@@ -178,10 +187,17 @@ def tile_moe_shr_lin_relu2_kernel(tc, xT, w_words, w_scales, b, gate, offs, pos1
         scalar_gather(1)
         quads_in[0] = tile("quads0", RAW, U32, "row1")[:]
         weave(0, 0, S)
-        for a in (1, 2, 3):
-            for u in (1, 0):
-                round_pairs(a, u, 0, T, pool_round)
-                gather(a, u, 0, WINDOW)
+        own_weave(0, 1, 0, H)
+        round_pairs(1, 1, 0, T, pool_round)
+        gather(1, 1, 0, WINDOW)
+        own_weave(0, 1, H, T)
+        for a, u in ((1, 0), (2, 1), (2, 0)):
+            round_pairs(a, u, 0, T, pool_round)
+            gather(a, u, 0, WINDOW)
+        own_weave(1, 1, 0, T)
+        pool_round(pairs(3, 0, 2 * T).bitcast(BF16).rearrange("p (u t j) -> p u t j", u=2, j=2), raw(3, 0, 4).rearrange("p (u j t) -> p u t j", u=2, j=2))
+        gather(3, 1, 0, WINDOW)
+        gather(3, 0, 0, WINDOW)
         late_loads()
         scalar_gather(2)
         scalar_gather(3)
@@ -189,8 +205,7 @@ def tile_moe_shr_lin_relu2_kernel(tc, xT, w_words, w_scales, b, gate, offs, pos1
         weave(1, 0, S)
         weave(X, 0, S)
         weave(2, 0, S)
-        nc.gpsimd.tensor_copy(out=own_quads[:, :8 * T].rearrange("p (a t u) -> p a t u", a=4, u=2),
-                              in_=early[:, :8 * T].rearrange("p (a u t) -> p a t u", a=4, u=2))
+        own_weave(3, 2, 0, T)
         pool_round(own_quads[:, 8 * T:].bitcast(BF16).rearrange("p (t j) -> p t j", j=4), x_last[:].rearrange("p (j t) -> p t j", j=4))
         for lo, n in GROUPS[:3]:
             weave(3, lo, n)

@@ -41,20 +41,20 @@ def tile_moe_shr_lin_relu2_kernel(tc, xT, w_words, w_scales, b, gate, offs, pos1
         psum = ctx.enter_context(tc.psum_pool(name="psum", bufs=1))
 
         def tile(name, width, dtype, tag):
-            return keep.tile([P, width], dtype, name=name, tag=tag, align_bytes=64)
+            return keep.tile([P, width], dtype, name=name, tag=tag, align_bytes=256)
 
         offs_t = keep.tile([P, S // 16], U16, name="offs_t")
         pos1_t = keep.tile([P, T // 16], U16, name="pos1_t")
         pos2_t = keep.tile([P, T // 16], U16, name="pos2_t")
         bias = keep.tile([P, E + 1], F32, name="bias")
-        wt = keep.tile([P, (E + 1) * PASSES, 2 * N], U8, name="wt", align_bytes=64)
-        wsc = keep.tile([P, (E + 1) * PASSES, N], U8, name="wsc", align_bytes=64)
+        wt = keep.tile([P, (E + 1) * PASSES, 2 * N], U8, name="wt", align_bytes=256)
+        wsc = keep.tile([P, (E + 1) * PASSES, N], U8, name="wsc", align_bytes=256)
         arena = tile("arena", 6 * RAW, U32, "arena")
         early = tile("early", 8 * T + HEAD_TAIL, U32, "early")
-        rows = [tile("row%d" % j, T + PAD, F32, "row%d" % j) for j in range(4)]
+        rows = {j: tile("row%d" % j, T + PAD, F32, "row%d" % j) for j in (1, 2, 3)}
         x_last = tile("x_last", RAW, F32, "x_last")
         own_quads = tile("own_quads", PASSES * 2 * T, U32, "own_quads")
-        first_quads = tile("first_quads", 2 * BANK, U32, "first")
+        first_picks = tile("first_picks", 2 * BANK, U32, "first")
         cscale = tile("cscale", PASSES * S, U8, "cscale")
         sscale = tile("sscale", PASSES * T, U8, "sscale")
 
@@ -65,12 +65,11 @@ def tile_moe_shr_lin_relu2_kernel(tc, xT, w_words, w_scales, b, gate, offs, pos1
         def pad(j):
             return rows[j][:, T:].bitcast(U32)
 
-        nc.gpsimd.memset(pad(1), 0)
-        nc.scalar.copy(out=pad(0), in_=pad(1))
+        nc.gpsimd.memset(pad(2), 0)
+        nc.scalar.copy(out=pad(1), in_=pad(2))
         nc.gpsimd.memset(wsc[:].rearrange("p a n -> p (a n)").bitcast(I32), 0)
         nc.vector.memset(early[:, 8 * T:], 0)
-        for j in (2, 3):
-            nc.vector.memset(pad(j), 0)
+        nc.vector.memset(pad(3), 0)
 
         xv = xT.rearrange("(a p j) t -> a p j t", a=PASSES, j=4)
 
@@ -103,17 +102,18 @@ def tile_moe_shr_lin_relu2_kernel(tc, xT, w_words, w_scales, b, gate, offs, pos1
         order = (0, 1, X, 2, 3)
 
         def late_loads():
+            nc.sync.dma_start(out=x_last[:].rearrange("p (j t) -> p j t", j=4), in_=xv[X])
             nc.sync.dma_start(out=bias[:], in_=b)
             scale_rows = wsc[:].rearrange("p a n -> p (a n)").bitcast(I32)
             nc.sync.dma_start(out=scale_rows[0:16].rearrange("p (a n) -> p a n", n=N // 4), in_=w_scales.bitcast(I32).rearrange("e a q n -> q (e a) n"))
             wv = w_words.bitcast(I32).rearrange("e a p n -> p (e a) n")
             wd = wt[:].rearrange("p a n -> p (a n)").bitcast(I32).rearrange("p (a n) -> p a n", n=N // 2)
             first = 2 * BANK // C * PASSES
-            nc.sync.dma_start(out=x_last[:].rearrange("p (j t) -> p j t", j=4), in_=xv[X])
-            for q in range(1, 4):
-                nc.sync.dma_start(out=scale_rows[32 * q:32 * q + 4], in_=scale_rows[4 * q:4 * q + 4])
             for a in order:
                 nc.sync.dma_start(out=wd[:, a:first:PASSES], in_=wv[:, a:first:PASSES])
+                if a == order[0]:
+                    for q in range(1, 4):
+                        nc.sync.dma_start(out=scale_rows[32 * q:32 * q + 4], in_=scale_rows[4 * q:4 * q + 4])
             nc.sync.dma_start(out=wd[:, first:E * PASSES], in_=wv[:, first:E * PASSES])
             nc.sync.dma_start(pos2_t[:], pos2)
             nc.sync.dma_start(pos1_t[:], pos1)
@@ -131,6 +131,8 @@ def tile_moe_shr_lin_relu2_kernel(tc, xT, w_words, w_scales, b, gate, offs, pos1
         picks_in = {0: 4, 1: 0, 2: 1, 3: 2, X: 5}
 
         def picks(a, u, lo, n):
+            if (a, lo) == (X, 0):
+                return first_picks[:, u * BANK:u * BANK + n]
             return region(picks_in[a], u * S + lo, n)
 
         def gather(a, u, lo, window):
@@ -141,19 +143,23 @@ def tile_moe_shr_lin_relu2_kernel(tc, xT, w_words, w_scales, b, gate, offs, pos1
             nc.vector.tensor_copy(v[:, :, j], raw(0, 2 + j, 1).indirect(offs_t[:, :HEAD // 16]))
 
         def scalar_gather(j):
-            v = picks(X, j // 2, 0, S).bitcast(BF16).rearrange("p (s j) -> p s j", j=2)
-            for lo in range(0, S, BANK):
-                nc.scalar.activation(v[:, lo:lo + BANK, j % 2], rows[j][:].indirect(offs_t[:, lo // 16:(lo + BANK) // 16]), COPY)
+            window, cuts = (rows[j], ((0, BANK), (BANK, 2 * BANK), (2 * BANK, S))) if j else (x_last, ((BANK, S), (0, BANK)))
+            for lo, hi in cuts:
+                v = picks(X, j // 2, lo, hi - lo).bitcast(BF16).rearrange("p (s j) -> p s j", j=2)
+                nc.scalar.activation(v[:, :, j % 2], window[:].indirect(offs_t[:, lo // 16:hi // 16]), COPY)
 
-        quads_in = {2: region(0, 0, RAW), 3: region(1, 0, RAW), X: region(4, 0, RAW)}
+        quads_in = {2: region(5, 0, RAW), 3: region(1, 0, RAW), X: region(4, 0, RAW)}
 
         def quads(a, lo, n):
             if (a, lo) == (3, 0):
-                return first_quads[:]
+                return quads_in["first"]
             return quads_in[a][:, 2 * lo:2 * (lo + n)]
 
         def weave(a, lo, n):
-            src = region(picks_in[a], 0, RAW).rearrange("p (u s) -> p s u", u=2)[:, lo:lo + n, :]
+            if (a, lo) == (X, 0):
+                src = first_picks[:].rearrange("p (u s) -> p s u", u=2)
+            else:
+                src = region(picks_in[a], 0, RAW).rearrange("p (u s) -> p s u", u=2)[:, lo:lo + n, :]
             nc.scalar.copy(out=quads(a, lo, n).rearrange("p (s u) -> p s u", u=2), in_=src)
 
         def mm(dst, e, a, cd, cs, lo, n, start, stop):
@@ -163,29 +169,28 @@ def tile_moe_shr_lin_relu2_kernel(tc, xT, w_words, w_scales, b, gate, offs, pos1
         load_row(raw(0, 2, 1), 0, 2)
         nc.sync.dma_start(offs_t[:], offs)
         load_row(raw(0, 3, 1), 0, 3)
-        load_row(rows[0][:, :T], X, 0)
+        load_row(rows[1][:, :T], X, 1)
         load_plane(0, 0, 0, H)
         load_plane(0, 0, H, T)
+        load_row(rows[2][:, :T], X, 2)
         load_plane(1, 1, 0, T)
-        load_row(rows[1][:, :T], X, 1)
         load_plane(1, 0, 0, T)
         load_plane(2, 1, 0, T)
-        load_plane(2, 0, 0, T)
-        load_row(rows[2][:, :T], X, 2)
-        nc.sync.dma_start(out=raw(3, 0, 4).rearrange("p (j t) -> p j t", j=4), in_=xv[3])
         load_row(rows[3][:, :T], X, 3)
+        load_plane(2, 0, 0, T)
+        nc.sync.dma_start(out=raw(3, 0, 4).rearrange("p (j t) -> p j t", j=4), in_=xv[3])
 
         head_gather(0)
         head_gather(1)
         round_pairs(0, 1, 0, SPLIT, nc.scalar.copy)
         round_pairs(0, 1, SPLIT, T, pool_round)
         gather(0, 1, HEAD, T + HEAD_TAIL)
-        scalar_gather(0)
+        scalar_gather(1)
         round_pairs(0, 0, 0, H, pool_round)
         round_pairs(0, 0, H, T, pool_round)
         gather(0, 0, 0, WINDOW)
-        scalar_gather(1)
-        quads_in[0] = tile("quads0", RAW, U32, "row1")[:]
+        scalar_gather(2)
+        quads_in[0] = tile("quads0", RAW, U32, "row2")[:]
         weave(0, 0, S)
         own_weave(0, 1, 0, H)
         round_pairs(1, 1, 0, T, pool_round)
@@ -199,11 +204,13 @@ def tile_moe_shr_lin_relu2_kernel(tc, xT, w_words, w_scales, b, gate, offs, pos1
         gather(3, 1, 0, WINDOW)
         gather(3, 0, 0, WINDOW)
         late_loads()
-        scalar_gather(2)
         scalar_gather(3)
         quads_in[1] = tile("quads1", RAW, U32, "row3")[:]
         weave(1, 0, S)
-        weave(X, 0, S)
+        scalar_gather(0)
+        weave(X, BANK, S - BANK)
+        weave(X, 0, BANK)
+        quads_in["first"] = tile("first_quads", 2 * BANK, U32, "first")[:]
         weave(2, 0, S)
         own_weave(3, 2, 0, T)
         pool_round(own_quads[:, 8 * T:].bitcast(BF16).rearrange("p (t j) -> p t j", j=4), x_last[:].rearrange("p (j t) -> p t j", j=4))
@@ -225,8 +232,8 @@ def tile_moe_shr_lin_relu2_kernel(tc, xT, w_words, w_scales, b, gate, offs, pos1
                 for a, lo, n in [(a, groups[0][0], width // len(sets)) for a in order[:-1]] + [(order[-1], lo, n) for lo, n in groups]:
                     at = a * width + lo - first
                     routed(codes[:, at:at + n], cscale[:, a * S + lo:a * S + lo + n], a, lo, n)
-        y = tile("y", S, F32, "row0")
-        ys = tile("ys", T, F32, "row2")
+        y = tile("y", S, F32, "row1")
+        ys = tile("ys", T, F32, "ys")
         for g, (lo, n) in enumerate(GROUPS):
             r = y[:, lo:lo + n] if n == BANK else ys[:, lo - 2 * BANK:lo - 2 * BANK + n]
             for c0 in range(0, n, C):

@@ -19,6 +19,7 @@ RAW = 4 * T
 HEAD = 448
 SPLIT = 416
 HEAD_TAIL = 705
+SHARE = 256
 
 F32 = mybir.dt.float32
 BF16 = mybir.dt.bfloat16
@@ -49,10 +50,12 @@ def tile_moe_shr_lin_relu2_kernel(tc, xT, w_words, w_scales, b, gate, offs, pos1
         bias = keep.tile([P, E + 1], F32, name="bias")
         wt = keep.tile([P, (E + 1) * PASSES, 2 * N], U8, name="wt", align_bytes=256)
         wsc = keep.tile([P, (E + 1) * PASSES, N], U8, name="wsc", align_bytes=256)
-        arena = tile("arena", 6 * RAW, U32, "arena")
+        arena = tile("arena", 5 * RAW, U32, "arena")
         early = tile("early", 8 * T + HEAD_TAIL, U32, "early")
         rows = {j: tile("row%d" % j, T + PAD, F32, "row%d" % j) for j in (1, 2, 3)}
         x_last = tile("x_last", RAW, F32, "x_last")
+        x3 = tile("x3", RAW, F32, "x3")
+        extra = tile("extra", T, F32, "extra")
         own_quads = tile("own_quads", PASSES * 2 * T, U32, "own_quads")
         first_picks = tile("first_picks", 2 * BANK, U32, "first")
         cscale = tile("cscale", PASSES * S, U8, "cscale")
@@ -79,6 +82,8 @@ def tile_moe_shr_lin_relu2_kernel(tc, xT, w_words, w_scales, b, gate, offs, pos1
         lands = {(1, 2): 7 * T, (2, 0): 4 * T}
 
         def raw(a, j, n):
+            if a == 3:
+                return x3[:, j * T:(j + n) * T]
             if (a, j) in lands:
                 return own_quads[:, lands[a, j]:lands[a, j] + n * T].bitcast(F32)
             return region(a, j * T, n * T).bitcast(F32)
@@ -98,7 +103,6 @@ def tile_moe_shr_lin_relu2_kernel(tc, xT, w_words, w_scales, b, gate, offs, pos1
         def load_row(dst, a, j):
             nc.sync.dma_start(out=dst, in_=xv[a][:, j, :])
 
-        gate_t = region(3, 0, 2 * T).bitcast(F32)
         order = (0, 1, X, 2, 3)
 
         def late_loads():
@@ -128,7 +132,7 @@ def tile_moe_shr_lin_relu2_kernel(tc, xT, w_words, w_scales, b, gate, offs, pos1
             s = raw(a, 2 * u, 2).rearrange("p (j t) -> p t j", j=2)
             rnd(d[:, lo:hi, :], s[:, lo:hi, :])
 
-        picks_in = {0: 4, 1: 0, 2: 1, 3: 2, X: 5}
+        picks_in = {0: 3, 1: 0, 2: 1, 3: 2, X: 4}
 
         def picks(a, u, lo, n):
             if (a, lo) == (X, 0):
@@ -148,7 +152,7 @@ def tile_moe_shr_lin_relu2_kernel(tc, xT, w_words, w_scales, b, gate, offs, pos1
                 v = picks(X, j // 2, lo, hi - lo).bitcast(BF16).rearrange("p (s j) -> p s j", j=2)
                 nc.scalar.activation(v[:, :, j % 2], window[:].indirect(offs_t[:, lo // 16:hi // 16]), COPY)
 
-        quads_in = {2: region(5, 0, RAW), 3: region(1, 0, RAW), X: region(4, 0, RAW)}
+        quads_in = {2: region(4, 0, RAW), 3: region(1, 0, RAW), X: region(3, 0, RAW)}
 
         def quads(a, lo, n):
             if (a, lo) == (3, 0):
@@ -179,6 +183,7 @@ def tile_moe_shr_lin_relu2_kernel(tc, xT, w_words, w_scales, b, gate, offs, pos1
         load_row(rows[3][:, :T], X, 3)
         load_plane(2, 0, 0, T)
         nc.sync.dma_start(out=raw(3, 0, 4).rearrange("p (j t) -> p j t", j=4), in_=xv[3])
+        load_row(extra[:], 3, 1)
 
         head_gather(0)
         head_gather(1)
@@ -202,11 +207,16 @@ def tile_moe_shr_lin_relu2_kernel(tc, xT, w_words, w_scales, b, gate, offs, pos1
         own_weave(1, 1, 0, T)
         pool_round(pairs(3, 0, 2 * T).bitcast(BF16).rearrange("p (u t j) -> p u t j", u=2, j=2), raw(3, 0, 4).rearrange("p (u j t) -> p u t j", u=2, j=2))
         gather(3, 1, 0, WINDOW)
-        gather(3, 0, 0, WINDOW)
-        late_loads()
+        gather(3, 0, SHARE, WINDOW)
         scalar_gather(3)
         quads_in[1] = tile("quads1", RAW, U32, "row3")[:]
         weave(1, 0, S)
+        shared_slots = picks(3, 0, 0, SHARE).bitcast(BF16).rearrange("p (s j) -> p s j", j=2)
+        for j, window in enumerate((x3, extra)):
+            nc.scalar.activation(shared_slots[:, :, j], window[:].indirect(offs_t[:, :SHARE // 16]), COPY)
+        ends = tile("ends", RAW, F32, "x3")
+        gate_t = ends[:, :2 * T]
+        late_loads()
         scalar_gather(0)
         weave(X, BANK, S - BANK)
         weave(X, 0, BANK)
@@ -233,7 +243,7 @@ def tile_moe_shr_lin_relu2_kernel(tc, xT, w_words, w_scales, b, gate, offs, pos1
                     at = a * width + lo - first
                     routed(codes[:, at:at + n], cscale[:, a * S + lo:a * S + lo + n], a, lo, n)
         y = tile("y", S, F32, "row1")
-        ys = tile("ys", T, F32, "ys")
+        ys = tile("ys", T, F32, "extra")
         for g, (lo, n) in enumerate(GROUPS):
             r = y[:, lo:lo + n] if n == BANK else ys[:, lo - 2 * BANK:lo - 2 * BANK + n]
             for c0 in range(0, n, C):
@@ -260,7 +270,7 @@ def tile_moe_shr_lin_relu2_kernel(tc, xT, w_words, w_scales, b, gate, offs, pos1
             mm(ps_sa[:], E, a, scodes, sscale, i * T, BANK, i == 0, i == PASSES - 1)
             mm(ps_sb[:], E, a, scodes, sscale, i * T + BANK, T - BANK, i == 0, i == PASSES - 1)
 
-        g1, g2 = region(3, 2 * T, T).bitcast(F32), region(3, 3 * T, T).bitcast(F32)
+        g1, g2 = ends[:, 2 * T:3 * T], ends[:, 3 * T:]
         halves = (slice(0, H), slice(H, T))
         nc.scalar.activation(g2, y[:].indirect(pos2_t[:]), COPY)
         for c in halves:

@@ -14,12 +14,13 @@ GROUPS = ((0, BANK), (BANK, BANK), (2 * BANK, 2 * C), (LAST, C), (LAST + C, C))
 FLOPS = 2 * K * N * (S + T)
 
 WINDOW = 2048
-PAD = 257
+PAD = T + 1
 RAW = 4 * T
-HEAD = 448
+HEAD = 480
 SPLIT = 416
-HEAD_TAIL = 705
-SHARE = 256
+HEAD_TAIL = 641
+EARLY = 576
+SHARE = 288
 
 F32 = mybir.dt.float32
 BF16 = mybir.dt.bfloat16
@@ -57,7 +58,7 @@ def tile_moe_shr_lin_relu2_kernel(tc, xT, w_words, w_scales, b, gate, offs, pos1
         x3 = tile("x3", RAW, F32, "x3")
         extra = tile("extra", T, F32, "extra")
         own_quads = tile("own_quads", PASSES * 2 * T, U32, "own_quads")
-        first_picks = tile("first_picks", 2 * BANK, U32, "first")
+        first_picks = tile("first_picks", 2 * T, U32, "first")
         cscale = tile("cscale", PASSES * S, U8, "cscale")
         sscale = tile("sscale", PASSES * T, U8, "sscale")
 
@@ -79,7 +80,7 @@ def tile_moe_shr_lin_relu2_kernel(tc, xT, w_words, w_scales, b, gate, offs, pos1
         def region(i, lo, n):
             return arena[:, i * RAW + lo:i * RAW + lo + n]
 
-        lands = {(1, 2): 7 * T, (2, 0): 4 * T}
+        lands = {(1, 2): 6 * T + 2 * EARLY, (2, 0): 4 * T}
 
         def raw(a, j, n):
             if a == 3:
@@ -136,7 +137,7 @@ def tile_moe_shr_lin_relu2_kernel(tc, xT, w_words, w_scales, b, gate, offs, pos1
 
         def picks(a, u, lo, n):
             if (a, lo) == (X, 0):
-                return first_picks[:, u * BANK:u * BANK + n]
+                return first_picks[:, u * T:u * T + n]
             return region(picks_in[a], u * S + lo, n)
 
         def gather(a, u, lo, window):
@@ -147,10 +148,10 @@ def tile_moe_shr_lin_relu2_kernel(tc, xT, w_words, w_scales, b, gate, offs, pos1
             nc.vector.tensor_copy(v[:, :, j], raw(0, 2 + j, 1).indirect(offs_t[:, :HEAD // 16]))
 
         def scalar_gather(j):
-            window, cuts = (rows[j], ((0, BANK), (BANK, 2 * BANK), (2 * BANK, S))) if j else (x_last, ((BANK, S), (0, BANK)))
-            for lo, hi in cuts:
-                v = picks(X, j // 2, lo, hi - lo).bitcast(BF16).rearrange("p (s j) -> p s j", j=2)
-                nc.scalar.activation(v[:, :, j % 2], window[:].indirect(offs_t[:, lo // 16:hi // 16]), COPY)
+            window = rows[j] if j else x_last
+            for lo in (T, 0):
+                v = picks(X, j // 2, lo, T).bitcast(BF16).rearrange("p (s j) -> p s j", j=2)
+                nc.scalar.activation(v[:, :, j % 2], window[:].indirect(offs_t[:, lo // 16:(lo + T) // 16]), COPY)
 
         quads_in = {2: region(4, 0, RAW), 3: region(1, 0, RAW), X: region(3, 0, RAW)}
 
@@ -197,10 +198,10 @@ def tile_moe_shr_lin_relu2_kernel(tc, xT, w_words, w_scales, b, gate, offs, pos1
         scalar_gather(2)
         quads_in[0] = tile("quads0", RAW, U32, "row2")[:]
         weave(0, 0, S)
-        own_weave(0, 1, 0, H)
+        own_weave(0, 1, 0, EARLY)
         round_pairs(1, 1, 0, T, pool_round)
         gather(1, 1, 0, WINDOW)
-        own_weave(0, 1, H, T)
+        own_weave(0, 1, EARLY, T)
         for a, u in ((1, 0), (2, 1), (2, 0)):
             round_pairs(a, u, 0, T, pool_round)
             gather(a, u, 0, WINDOW)
@@ -218,8 +219,8 @@ def tile_moe_shr_lin_relu2_kernel(tc, xT, w_words, w_scales, b, gate, offs, pos1
         gate_t = ends[:, :2 * T]
         late_loads()
         scalar_gather(0)
-        weave(X, BANK, S - BANK)
-        weave(X, 0, BANK)
+        weave(X, T, T)
+        weave(X, 0, T)
         quads_in["first"] = tile("first_quads", 2 * BANK, U32, "first")[:]
         weave(2, 0, S)
         own_weave(3, 2, 0, T)

@@ -20,7 +20,7 @@ HEAD = 480
 SPLIT = 416
 HEAD_TAIL = 641
 EARLY = 576
-SHARE = 288
+SHARE = 384
 
 F32 = mybir.dt.float32
 BF16 = mybir.dt.bfloat16
@@ -113,7 +113,7 @@ def tile_moe_shr_lin_relu2_kernel(tc, xT, w_words, w_scales, b, gate, offs, pos1
             nc.sync.dma_start(out=scale_rows[0:16].rearrange("p (a n) -> p a n", n=N // 4), in_=w_scales.bitcast(I32).rearrange("e a q n -> q (e a) n"))
             wv = w_words.bitcast(I32).rearrange("e a p n -> p (e a) n")
             wd = wt[:].rearrange("p a n -> p (a n)").bitcast(I32).rearrange("p (a n) -> p a n", n=N // 2)
-            first = 2 * BANK // C * PASSES
+            first = LAST // C * PASSES
             for a in order:
                 nc.sync.dma_start(out=wd[:, a:first:PASSES], in_=wv[:, a:first:PASSES])
                 if a == order[0]:
@@ -237,12 +237,15 @@ def tile_moe_shr_lin_relu2_kernel(tc, xT, w_words, w_scales, b, gate, offs, pos1
                 mm(ps[g][:, c0:c0 + C], s0 // C, a, codes, scales, s0 - lo, C,
                    a == order[0] and c0 == 0, a == order[-1] and c0 + C == GROUPS[g][1])
 
-        for first, width, sets, tag in ((0, 2 * BANK, (GROUPS[:2],), "x_last"), (2 * BANK, BANK, (GROUPS[2:3], GROUPS[3:]), "first")):
-            codes = tile("codes_" + tag, PASSES * width, U32, tag)
-            for groups in sets:
-                for a, lo, n in [(a, groups[0][0], width // len(sets)) for a in order[:-1]] + [(order[-1], lo, n) for lo, n in groups]:
-                    at = a * width + lo - first
-                    routed(codes[:, at:at + n], cscale[:, a * S + lo:a * S + lo + n], a, lo, n)
+        wide, third = (0, 2 * BANK), GROUPS[2]
+        sooner = [(a,) + wide for a in order[:3]] + [(a,) + third for a in order[:3]] + [(order[3],) + wide] + [(order[4],) + g for g in GROUPS[:2]]
+        later = [(a,) + third for a in order[3:]] + [(a, LAST, 2 * C) for a in order[:4]] + [(order[4],) + g for g in GROUPS[3:]]
+        for steps, tag in ((sooner, "x_last"), (later, "first")):
+            codes = tile("codes_" + tag, sum(n for a, lo, n in steps), U32, tag)
+            at = 0
+            for a, lo, n in steps:
+                routed(codes[:, at:at + n], cscale[:, a * S + lo:a * S + lo + n], a, lo, n)
+                at = at + n
         y = tile("y", S, F32, "row1")
         ys = tile("ys", T, F32, "extra")
         for g, (lo, n) in enumerate(GROUPS):

@@ -238,8 +238,8 @@ def tile_moe_shr_lin_relu2_kernel(tc, xT, w_words, w_scales, b, gate, offs, pos1
                    a == order[0] and c0 == 0, a == order[-1] and c0 + C == GROUPS[g][1])
 
         wide, third = (0, 2 * BANK), GROUPS[2]
-        sooner = [(a,) + wide for a in order[:3]] + [(a,) + third for a in order[:3]] + [(order[3],) + wide] + [(order[4],) + g for g in GROUPS[:2]]
-        later = [(a,) + third for a in order[3:]] + [(a, LAST, 2 * C) for a in order[:4]] + [(order[4],) + g for g in GROUPS[3:]]
+        sooner = [(a,) + wide for a in order[:3]] + [(a,) + third for a in order[:2]] + [(order[3],) + wide] + [(order[4],) + g for g in GROUPS[:2]]
+        later = [(a,) + third for a in order[2:]] + [(a, LAST, 2 * C) for a in order[:4]] + [(order[4],) + g for g in GROUPS[3:]]
         for steps, tag in ((sooner, "x_last"), (later, "first")):
             codes = tile("codes_" + tag, sum(n for a, lo, n in steps), U32, tag)
             at = 0

from contextlib import ExitStack

import concourse.mybir as mybir

K, T, E, C, N = 2560, 768, 12, 128, 128
S = E * C
P = 128
PASSES = K // 512
X = PASSES - 1
BANK = 512
H = T // 2
LAST = S - 2 * C
GROUPS = ((0, BANK), (BANK, BANK), (2 * BANK, 2 * C), (LAST, C), (LAST + C, C))
FLOPS = 2 * K * N * (S + T)

WINDOW = 2048
PAD = T + 1
RAW = 4 * T
HEAD = 480
SPLIT = 416
HEAD_TAIL = 641
EARLY = 576
SHARE = 384

F32 = mybir.dt.float32
BF16 = mybir.dt.bfloat16
U32 = mybir.dt.uint32
I32 = mybir.dt.int32
U16 = mybir.dt.uint16
U8 = mybir.dt.uint8
FP8 = mybir.dt.float8_e4m3fn_x4
FP4 = mybir.dt.float4_e2m1fn_x4
ADD, MULT = mybir.AluOpType.add, mybir.AluOpType.mult
COPY = mybir.ActivationFunctionType.Copy
RELU = mybir.ActivationFunctionType.Relu
SQUARE = mybir.ActivationFunctionType.Square


def tile_moe_shr_lin_relu2_kernel(tc, xT, w_words, w_scales, b, gate, offs, pos1, pos2, out):
    nc = tc.nc
    with ExitStack() as ctx:
        keep = ctx.enter_context(tc.tile_pool(name="keep", bufs=1))
        psum = ctx.enter_context(tc.psum_pool(name="psum", bufs=1))

        def tile(name, width, dtype, tag):
            return keep.tile([P, width], dtype, name=name, tag=tag, align_bytes=256)

        offs_t = keep.tile([P, S // 16], U16, name="offs_t")
        pos1_t = keep.tile([P, T // 16], U16, name="pos1_t")
        pos2_t = keep.tile([P, T // 16], U16, name="pos2_t")
        bias = keep.tile([P, E + 1], F32, name="bias")
        wt = keep.tile([P, (E + 1) * PASSES, 2 * N], U8, name="wt", align_bytes=256)
        wsc = keep.tile([P, (E + 1) * PASSES, N], U8, name="wsc", align_bytes=256)
        arena = tile("arena", 5 * RAW, U32, "arena")
        early = tile("early", 8 * T + HEAD_TAIL, U32, "early")
        rows = {j: tile("row%d" % j, T + PAD, F32, "row%d" % j) for j in (1, 2, 3)}
        x_last = tile("x_last", RAW, F32, "x_last")
        x3 = tile("x3", RAW, F32, "x3")
        extra = tile("extra", T, F32, "extra")
        own_quads = tile("own_quads", PASSES * 2 * T, U32, "own_quads")
        first_picks = tile("first_picks", 2 * T, U32, "first")
        cscale = tile("cscale", PASSES * S, U8, "cscale")
        sscale = tile("sscale", PASSES * T, U8, "sscale")

        ps_sa = psum.tile([P, BANK], F32, name="ps_sa")
        ps_sb = psum.tile([P, T - BANK], F32, name="ps_sb")
        ps = [psum.tile([P, n], F32, name="ps%d" % i) for i, (lo, n) in enumerate(GROUPS)]

        def pad(j):
            return rows[j][:, T:].bitcast(U32)

        nc.gpsimd.memset(pad(2), 0)
        nc.scalar.copy(out=pad(1), in_=pad(2))
        nc.gpsimd.memset(wsc[:].rearrange("p a n -> p (a n)").bitcast(I32), 0)
        nc.vector.memset(early[:, 8 * T:], 0)
        nc.vector.memset(pad(3), 0)

        xv = xT.rearrange("(a p j) t -> a p j t", a=PASSES, j=4)

        def region(i, lo, n):
            return arena[:, i * RAW + lo:i * RAW + lo + n]

        lands = {(1, 2): 6 * T + 2 * EARLY, (2, 0): 4 * T}

        def raw(a, j, n):
            if a == 3:
                return x3[:, j * T:(j + n) * T]
            if (a, j) in lands:
                return own_quads[:, lands[a, j]:lands[a, j] + n * T].bitcast(F32)
            return region(a, j * T, n * T).bitcast(F32)

        def own_weave(first, n, lo, hi):
            s = 2 * T * (3 - first)
            nc.gpsimd.tensor_copy(out=own_quads[:, s:s + 2 * T * n].rearrange("p (a t u) -> p a t u", a=n, u=2)[:, :, lo:hi, :],
                                  in_=early[:, s:s + 2 * T * n].rearrange("p (a u t) -> p a t u", a=n, u=2)[:, :, lo:hi, :])

        def pairs(a, u, n):
            s = 2 * T * (3 - a) + u * T
            return early[:, s:s + n]

        def load_plane(a, u, lo, hi):
            nc.sync.dma_start(out=raw(a, 2 * u, 2).rearrange("p (j t) -> p j t", j=2)[:, :, lo:hi], in_=xv[a][:, 2 * u:2 * u + 2, lo:hi])

        def load_row(dst, a, j):
            nc.sync.dma_start(out=dst, in_=xv[a][:, j, :])

        order = (0, 1, X, 2, 3)

        def late_loads():
            nc.sync.dma_start(out=x_last[:].rearrange("p (j t) -> p j t", j=4), in_=xv[X])
            nc.sync.dma_start(out=bias[:], in_=b)
            scale_rows = wsc[:].rearrange("p a n -> p (a n)").bitcast(I32)
            nc.sync.dma_start(out=scale_rows[0:16].rearrange("p (a n) -> p a n", n=N // 4), in_=w_scales.bitcast(I32).rearrange("e a q n -> q (e a) n"))
            wv = w_words.bitcast(I32).rearrange("e a p n -> p (e a) n")
            wd = wt[:].rearrange("p a n -> p (a n)").bitcast(I32).rearrange("p (a n) -> p a n", n=N // 2)
            first = LAST // C * PASSES
            for a in order:
                nc.sync.dma_start(out=wd[:, a:first:PASSES], in_=wv[:, a:first:PASSES])
                if a == order[0]:
                    for q in range(1, 4):
                        nc.sync.dma_start(out=scale_rows[32 * q:32 * q + 4], in_=scale_rows[4 * q:4 * q + 4])
            nc.sync.dma_start(out=wd[:, first:E * PASSES], in_=wv[:, first:E * PASSES])
            nc.sync.dma_start(pos2_t[:], pos2)
            nc.sync.dma_start(pos1_t[:], pos1)
            nc.sync.dma_start(out=gate_t.rearrange("p (g t) -> p g t", g=2), in_=gate.rearrange("g p t -> p g t"))
            nc.sync.dma_start(out=wd[:, E * PASSES:], in_=wv[:, E * PASSES:])

        def pool_round(dst, src):
            nc.gpsimd.tensor_scalar(out=dst, in0=src, scalar1=1.0, scalar2=0.0, op0=MULT, op1=ADD)

        def round_pairs(a, u, lo, hi, rnd):
            d = pairs(a, u, T).bitcast(BF16).rearrange("p (t j) -> p t j", j=2)
            s = raw(a, 2 * u, 2).rearrange("p (j t) -> p t j", j=2)
            rnd(d[:, lo:hi, :], s[:, lo:hi, :])

        picks_in = {0: 3, 1: 0, 2: 1, 3: 2, X: 4}

        def picks(a, u, lo, n):
            if (a, lo) == (X, 0):
                return first_picks[:, u * T:u * T + n]
            return region(picks_in[a], u * S + lo, n)

        def gather(a, u, lo, window):
            nc.vector.tensor_copy(picks(a, u, lo, S - lo), pairs(a, u, window).indirect(offs_t[:, lo // 16:]))

        def head_gather(j):
            v = picks(0, 1, 0, HEAD).bitcast(BF16).rearrange("p (s j) -> p s j", j=2)
            nc.vector.tensor_copy(v[:, :, j], raw(0, 2 + j, 1).indirect(offs_t[:, :HEAD // 16]))

        def scalar_gather(j):
            window = rows[j] if j else x_last
            for lo in (T, 0):
                v = picks(X, j // 2, lo, T).bitcast(BF16).rearrange("p (s j) -> p s j", j=2)
                nc.scalar.activation(v[:, :, j % 2], window[:].indirect(offs_t[:, lo // 16:(lo + T) // 16]), COPY)

        quads_in = {2: region(4, 0, RAW), 3: region(1, 0, RAW), X: region(3, 0, RAW)}

        def quads(a, lo, n):
            if (a, lo) == (3, 0):
                return quads_in["first"]
            return quads_in[a][:, 2 * lo:2 * (lo + n)]

        def weave(a, lo, n):
            if (a, lo) == (X, 0):
                src = first_picks[:].rearrange("p (u s) -> p s u", u=2)
            else:
                src = region(picks_in[a], 0, RAW).rearrange("p (u s) -> p s u", u=2)[:, lo:lo + n, :]
            nc.scalar.copy(out=quads(a, lo, n).rearrange("p (s u) -> p s u", u=2), in_=src)

        def mm(dst, e, a, cd, cs, lo, n, start, stop):
            nc.tensor.matmul_mx(out=dst, lhsT=wt[:, e * PASSES + a, :].bitcast(FP4), lhsT_scale=wsc[:, e * PASSES + a, :],
                                rhs=cd[:, lo:lo + n].bitcast(FP8), rhs_scale=cs[:, lo:lo + n], start=start, stop=stop)

        load_row(raw(0, 2, 1), 0, 2)
        nc.sync.dma_start(offs_t[:], offs)
        load_row(raw(0, 3, 1), 0, 3)
        load_row(rows[1][:, :T], X, 1)
        load_plane(0, 0, 0, H)
        load_plane(0, 0, H, T)
        load_row(rows[2][:, :T], X, 2)
        load_plane(1, 1, 0, T)
        load_plane(1, 0, 0, T)
        load_plane(2, 1, 0, T)
        load_row(rows[3][:, :T], X, 3)
        load_plane(2, 0, 0, T)
        nc.sync.dma_start(out=raw(3, 0, 4).rearrange("p (j t) -> p j t", j=4), in_=xv[3])
        load_row(extra[:], 3, 1)

        head_gather(0)
        head_gather(1)
        round_pairs(0, 1, 0, SPLIT, nc.scalar.copy)
        round_pairs(0, 1, SPLIT, T, pool_round)
        gather(0, 1, HEAD, T + HEAD_TAIL)
        scalar_gather(1)
        round_pairs(0, 0, 0, H, pool_round)
        round_pairs(0, 0, H, T, pool_round)
        gather(0, 0, 0, WINDOW)
        scalar_gather(2)
        quads_in[0] = tile("quads0", RAW, U32, "row2")[:]
        weave(0, 0, S)
        own_weave(0, 1, 0, EARLY)
        round_pairs(1, 1, 0, T, pool_round)
        gather(1, 1, 0, WINDOW)
        own_weave(0, 1, EARLY, T)
        for a, u in ((1, 0), (2, 1), (2, 0)):
            round_pairs(a, u, 0, T, pool_round)
            gather(a, u, 0, WINDOW)
        own_weave(1, 1, 0, T)
        pool_round(pairs(3, 0, 2 * T).bitcast(BF16).rearrange("p (u t j) -> p u t j", u=2, j=2), raw(3, 0, 4).rearrange("p (u j t) -> p u t j", u=2, j=2))
        gather(3, 1, 0, WINDOW)
        gather(3, 0, SHARE, WINDOW)
        scalar_gather(3)
        quads_in[1] = tile("quads1", RAW, U32, "row3")[:]
        weave(1, 0, S)
        shared_slots = picks(3, 0, 0, SHARE).bitcast(BF16).rearrange("p (s j) -> p s j", j=2)
        for j, window in enumerate((x3, extra)):
            nc.scalar.activation(shared_slots[:, :, j], window[:].indirect(offs_t[:, :SHARE // 16]), COPY)
        ends = tile("ends", RAW, F32, "x3")
        gate_t = ends[:, :2 * T]
        late_loads()
        scalar_gather(0)
        weave(X, T, T)
        weave(X, 0, T)
        quads_in["first"] = tile("first_quads", 2 * BANK, U32, "first")[:]
        weave(2, 0, S)
        own_weave(3, 2, 0, T)
        pool_round(own_quads[:, 8 * T:].bitcast(BF16).rearrange("p (t j) -> p t j", j=4), x_last[:].rearrange("p (j t) -> p t j", j=4))
        for lo, n in GROUPS[:3]:
            weave(3, lo, n)
        weave(3, LAST, S - LAST)

        def routed(codes, scales, a, lo, n):
            nc.vector.quantize_mx(out=codes.bitcast(FP8), scales=scales, in_=quads(a, lo, n).bitcast(BF16))
            for s0 in range(lo, lo + n, C):
                g = max(i for i in range(len(GROUPS)) if GROUPS[i][0] <= s0)
                c0 = s0 - GROUPS[g][0]
                mm(ps[g][:, c0:c0 + C], s0 // C, a, codes, scales, s0 - lo, C,
                   a == order[0] and c0 == 0, a == order[-1] and c0 + C == GROUPS[g][1])

        wide, third = (0, 2 * BANK), GROUPS[2]
        sooner = [(a,) + wide for a in order[:3]] + [(a,) + third for a in order[:2]] + [(order[3],) + wide] + [(order[4],) + g for g in GROUPS[:2]]
        later = [(a,) + third for a in order[2:]] + [(a, LAST, 2 * C) for a in order[:4]] + [(order[4],) + g for g in GROUPS[3:]]
        for steps, tag in ((sooner, "x_last"), (later, "first")):
            codes = tile("codes_" + tag, sum(n for a, lo, n in steps), U32, tag)
            at = 0
            for a, lo, n in steps:
                routed(codes[:, at:at + n], cscale[:, a * S + lo:a * S + lo + n], a, lo, n)
                at = at + n
        y = tile("y", S, F32, "row1")
        ys = tile("ys", T, F32, "extra")
        for g, (lo, n) in enumerate(GROUPS):
            r = y[:, lo:lo + n] if n == BANK else ys[:, lo - 2 * BANK:lo - 2 * BANK + n]
            for c0 in range(0, n, C):
                e = (lo + c0) // C
                nc.scalar.activation(out=r[:, c0:c0 + C], in_=ps[g][:, c0:c0 + C], func=RELU, bias=bias[:, e:e + 1])
            if n == BANK:
                for c0 in (0, n // 2):
                    nc.scalar.activation(out=r[:, c0:c0 + n // 2], in_=r[:, c0:c0 + n // 2], func=SQUARE)
        for lo, n in GROUPS[2:]:
            nc.scalar.activation(out=y[:, lo:lo + n], in_=ys[:, lo - 2 * BANK:lo - 2 * BANK + n], func=SQUARE)

        scodes = tile("scodes", PASSES * T, U32, "row3")
        shared_order = (3, 2, 1, 0, X)

        def shared_quantise(lo, n):
            nc.vector.quantize_mx(out=scodes[:, lo:lo + n].bitcast(FP8), scales=sscale[:, lo:lo + n], in_=own_quads[:, 2 * lo:2 * (lo + n)].bitcast(BF16))

        for i, a in enumerate(shared_order):
            if i < 3:
                shared_quantise(2 * BANK * i, 2 * BANK)
            if a == X:
                for lo, n in ((0, BANK), (BANK, T - BANK)):
                    shared_quantise(4 * T + lo, n)
            mm(ps_sa[:], E, a, scodes, sscale, i * T, BANK, i == 0, i == PASSES - 1)
            mm(ps_sb[:], E, a, scodes, sscale, i * T + BANK, T - BANK, i == 0, i == PASSES - 1)

        g1, g2 = ends[:, 2 * T:3 * T], ends[:, 3 * T:]
        halves = (slice(0, H), slice(H, T))
        nc.scalar.activation(g2, y[:].indirect(pos2_t[:]), COPY)
        for c in halves:
            nc.scalar.activation(g1[:, c], y[:].indirect(pos1_t[:, c.start // 16:c.stop // 16]), COPY)
        nc.scalar.activation(out=ys[:, :BANK], in_=ps_sa[:], func=RELU, bias=bias[:, E:E + 1])
        nc.scalar.activation(out=ys[:, BANK:], in_=ps_sb[:], func=RELU, bias=bias[:, E:E + 1])
        for c in halves:
            nc.scalar.activation(out=ys[:, c], in_=ys[:, c], func=SQUARE)

        nc.vector.tensor_tensor(g2, g2, gate_t[:, T:], MULT)
        for c in halves:
            nc.vector.tensor_tensor(g1[:, c], g1[:, c], gate_t[:, c], MULT)
        for c in halves:
            nc.vector.tensor_tensor(g1[:, c], g1[:, c], g2[:, c], ADD)
        for c in halves:
            nc.vector.tensor_tensor(g2[:, c], g1[:, c], ys[:, c], ADD)
            nc.sync.dma_start(out=out[:, c], in_=g2[:, c])
